import numpy as np, ml_dtypes
CORES = [8,136,40,168]
N = 4
BF = ml_dtypes.bfloat16
def gentries(a):
    return np.ascontiguousarray(a.reshape(8, 16, -1).transpose(0, 2, 1)).reshape(8, -1)
def gtable(e):
    e = np.asarray(e); return np.ascontiguousarray(e.reshape(8, -1, 16).transpose(0, 2, 1)).reshape(128, -1).astype(np.int32)
W, C, PB, R, INC, RO = 2048, 2, 192, 16, 96, 6
V = C * PB
TOP = 4080
def procs():
    return np.ascontiguousarray(np.broadcast_to(np.arange(V).reshape(C, 1, PB), (C, R, PB))).reshape(-1)
def rows():
    return np.ascontiguousarray(np.broadcast_to(np.arange(R).reshape(1, R, 1), (C, R, PB))).reshape(-1)
def owners(rng, E, share, rich):
    P = procs(); O = rng.integers(0, V, (N, 2, 8, W))
    for q in range(N):
        for g in range(8):
            e = E[q, g].reshape(-1); w = rng.random(V) < rich
            for s in range(2):
                p = rng.permutation(R * V); o = O[q, s, g].copy(); o[e[p]] = P[p]
                o = np.where(rng.random(W) < share[q, g], o, O[q, s, g])
                i = np.nonzero(w[P] & (P % 2 == s))[0]; o[e[i]] = P[i]
                O[q, s, g] = o
    return O
def parts(rng):
    M = rng.integers(0, 256, (N, 8, 16, W)); Z = rng.integers(0, 256, (N, 8, 16, V)); K = rng.integers(0, W, (N, 8, W)); E = rng.integers(0, W, (N, 8, C, R, PB))
    O = owners(rng, E, rng.choice(np.array([0.25, 0.5, 0.75, 0.95]), (N, 8)), 0.06); T = rng.integers(500, 1500, (N, 8, V))
    return M, K, O, E, Z, T
def least(M, O, E, Z):
    P = procs(); out = np.zeros((N, 8, V), np.int64)
    for q in range(N):
        for g in range(8):
            e = E[q, g].reshape(-1); y = M[q, g][:, e].reshape(16, C, R, PB)
            d = np.add.reduce(np.abs(y - Z[q, g].reshape(16, C, 1, PB)), axis=0)
            live = ((O[q, 0, g][e] == P) | (O[q, 1, g][e] == P)).reshape(C, R, PB)
            out[q, g] = np.min(np.where(live, d, TOP), axis=1).reshape(V)
    return out
def pack(M, K, O, E, Z, T):
    return {"msg": np.ascontiguousarray(M.reshape(N, 128, W)).astype(np.float32).astype(BF), "enc": K.astype(np.int32), "own": np.ascontiguousarray(O.reshape(N, 16, W)).astype(np.int32),
            "ends": np.stack([gtable(a.reshape(8, -1)) for a in E]), "st": np.ascontiguousarray(Z.reshape(N, 128, V)).astype(np.float32).astype(BF), "th": T.astype(np.int32)}
def setup_inputs(rng):
    return pack(*parts(rng))
def setup_inputs_corners(rng):
    M, K, O, E, Z, T = parts(rng); P = procs(); k = rows(); ee = np.arange(W); c = W // V
    x = rng.random(K.shape); K = np.where(x < 0.2, ee, np.where(x < 0.35, 0, np.where(x < 0.5, W - 1, np.where(x < 0.8, (ee + 1) % W, K))))
    for q in range(N):
        for g in range(8):
            w = (q + g) % 4
            if w == 0:
                x = rng.random(W); O[q, 0, g] = np.where(x < 0.1, 0, np.where(x < 0.2, V - 1, O[q, 0, g])); O[q, 1, g] = np.where(x > 0.85, O[q, 0, g], O[q, 1, g])
                continue
            O[q, :, g, :c * V] = np.tile(np.arange(V), c)
            mine = P + V * rng.integers(0, c, P.shape); other = (P + rng.integers(1, V, P.shape)) % V + V * rng.integers(0, c, P.shape)
            pos = rng.choice(np.array([0, R - 1, int(rng.integers(0, R))]), V)[P]; full = (rng.random(V) < 0.5)[P]
            hit = full if w == 1 else (k == pos if w == 2 else k != pos)
            E[q, g] = np.where(hit, mine, other).reshape(C, R, PB)
            if w == 1 and g >= 4:
                M[q, g] = 160 + ((M[q, g] * 3) >> 3); Z[q, g] = Z[q, g] >> 3
    low = least(M, O, E, Z); x = rng.integers(0, 5, T.shape)
    T = np.where(x == 0, low, np.where(x == 1, np.minimum(low + 1, TOP), np.where(x == 2, 0, np.where(x == 3, TOP, T))))
    for q in range(N):
        g = 4 + (1 - q) % 4; T[q, g] = low[q, g] + rng.integers(0, 2, V) - INC
    return pack(M, K, O, E, Z, T)
def setup_inputs_crowd(rng):
    M, K, O, E, Z, T = parts(rng); P = procs(); k = rows(); O = rng.integers(0, V, O.shape); a = np.arange(V); u = a - a % 2
    for q in range(N):
        for g in range(8):
            w = g % 4; e = E[q, g].reshape(-1).copy(); pos = rng.integers(0, R, V); hit = k == pos[P]; one = (0, W - 1, int(rng.integers(0, W)))[(q + g // 4) % 3]
            T[q, g] = TOP
            if w == 2:
                e[hit] = u[P[hit]]; O[q, 0, g, :V] = u; O[q, 1, g, :V] = u + 1; K[q, g] = rng.choice(np.array([0, W - 1, W // 2]), W)
            elif w == 3:
                m = rng.random(e.shape) < 0.5; e = np.where(m, rng.choice(np.array([V, V + 1, W - 1]), e.shape), e)
                e[hit] = P[hit]; O[q, 0, g] = (0, V - 1)[(q + g // 4) % 2]; O[q, 1, g, :V] = a; T[q, g] = TOP * rng.integers(0, 2, V)
            else:
                e[hit] = P[hit]; O[q, 0, g, :V] = a; K[q, g] = one
                if w == 1:
                    for b in range(C): T[q, g, b * PB + (0 if g == 1 else int(rng.integers(0, PB)))] = 0
            E[q, g] = e.reshape(C, R, PB)
    return pack(M, K, O, E, Z, T)
def setup_inputs_ends(rng):
    x = rng.random((N, 8, 1, W)); M = np.where(x < 0.4, 255, np.where(x < 0.8, 0, 255 * rng.integers(0, 2, (N, 8, 16, W))))
    x = rng.random((N, 8, 1, V)); Z = np.where(x < 0.35, 255, np.where(x < 0.7, 0, 255 * rng.integers(0, 2, (N, 8, 16, V))))
    E = rng.integers(0, W, (N, 8, C, R, PB)); E = np.where(rng.random(E.shape) < 0.68, (W - 1) * rng.integers(0, 2, E.shape), E)
    O = owners(rng, E, np.ones((N, 8)), 0.0); O = np.where(rng.random(O.shape) < 0.65, (V - 1) * rng.integers(0, 2, O.shape), O)
    K = rng.integers(0, W, (N, 8, W)); K = np.where(rng.random(K.shape) < 0.7, (W - 1) * rng.integers(0, 2, K.shape), K)
    T = TOP * rng.integers(0, 2, (N, 8, V))
    T[:, 7, :V - PB] = 0; T[:, 7, V - 1] = TOP
    M[:, 7, :, W - 1] = 255; M[:, 7, :, 0] = 0; Z[:, 7, :, V - 1] = 0
    O[:, 0, 7, W - 1] = 0; O[:, 1, 7, W - 1] = V - 1; O[:, 0, 7, 0] = V - 1; O[:, 1, 7, 0] = 0
    k = np.arange(R); both = np.where((k % 2 == 1) | (k == R - 2), W - 1, 0)
    for q in range(N): E[q, 7, C - 1, :, PB - 1] = both if (N - 1 - q) % 2 == 0 else W - 1
    T[:, 6] = 0; T[:, 6, 0] = TOP
    M[:, 6, :, W - 1] = 255; M[:, 6, :, 0] = 0; Z[:, 6, :, 0] = 0; Z[:, 6, :, 1] = 0
    O[:, 0, 6, W - 1] = V - 1; O[:, 1, 6, W - 1] = 0; E[:, 6, 0, :, 0] = W - 1
    O[:, 0, 6, 0] = 1; E[:, 6, 0, :, 1] = 0; E[:, 6, 0, R - 1, 1] = W - 1
    return pack(M, K, O, E, Z, T)
def setup_inputs_spread(rng):
    M, K, O, E, Z, T = parts(rng)
    M = np.minimum((np.exp2(8.5 * rng.random((N, 8, 1, W))) * rng.random(M.shape)).astype(np.int64), 255)
    Z = np.minimum((np.exp2(8.5 * rng.random((N, 8, 1, V))) * rng.random(Z.shape)).astype(np.int64), 255)
    K = np.minimum((W * rng.random(K.shape) ** 3).astype(np.int64), W - 1); E = np.minimum((W * rng.random(E.shape) ** 2).astype(np.int64), W - 1)
    O = owners(rng, E, rng.choice(np.array([0.5, 0.8, 1.0]), (N, 8)), 0.03)
    O = np.where(rng.random(O.shape) < 0.15, np.minimum((V * rng.random(O.shape) ** 3).astype(np.int64), V - 1), O)
    T = np.minimum(np.exp2(12 * rng.random(T.shape)).astype(np.int64) - 1, TOP)
    return pack(M, K, O, E, Z, T)
def setup_inputs_ties(rng):
    M, K, O, E, Z, T = parts(rng); base = rng.integers(0, 3, (N, 8, 16, W)); top = (np.arange(8) % 2).reshape(1, 8, 1, 1)
    for q in range(N):
        for g in range(8):
            M[q, g] = base[q, g][:, rng.integers(0, 24, W)]
            z = M[q, g][:, rng.integers(0, W, V)]; Z[q, g] = np.where(rng.random(V) < 0.5, z, rng.integers(0, 3, (16, V)))
    E[:, ::3, :, 1::2] = E[:, ::3, :, 0::2]
    O = owners(rng, E, rng.choice(np.array([0.6, 0.9]), (N, 8)), 0.05)
    M = np.where(top == 1, 255 - M, M); Z = np.where(top == 1, 255 - Z, Z); T = rng.integers(0, 24, T.shape)
    T = np.where(rng.random(T.shape) < 0.2, rng.integers(0, 2, T.shape), T)
    return pack(M, K, O, E, Z, T)
def check_inputs(d):
    bad = []
    for k, hi in (("msg", 255), ("enc", W - 1), ("own", V - 1), ("ends", W - 1), ("st", 255), ("th", TOP)):
        a = np.asarray(d[k]).astype(np.float64)
        if not (np.min(a) >= 0 and np.max(a) <= hi): bad.append("range of " + k)
        elif np.any(a != np.floor(a)): bad.append("whole numbers of " + k)
    return bad
def first(name, ok):
    qi = np.arange(N)[:, None, None]; gi = np.arange(8)[None, :, None]; lane = np.arange(PB)
    low = np.full((N, 8, W), PB, np.int64); np.minimum.at(low, (qi, gi, name), np.where(ok, lane, PB))
    return ok & (low[qi, gi, name] == lane)
def pick(a, k):
    return np.take_along_axis(a, k[:, :, None, :], 2)[:, :, 0]
def reference(msg, enc, own, ends, st, th):
    M = msg.astype(np.float32).astype(np.int64).reshape(N, 8, 16, W); K = enc.astype(np.int64); O = own.astype(np.int64).reshape(N, 2, 8, W)
    E = np.stack([gentries(a) for a in ends]).astype(np.int64).reshape(N, 8, C, R, PB)
    Z = st.astype(np.float32).astype(np.int64).reshape(N, 8, 16, V); T = th.astype(np.int64)
    qi = np.arange(N)[:, None, None]; gi = np.arange(8)[None, :, None]; lane = np.arange(PB); far = 2 ** 20
    for t in range(RO):
        b = t % C; lo = b * PB; v = lo + lane
        e = E[:, :, b].copy(); z = Z[..., lo:lo + PB].copy(); flat = e.reshape(N, 8, R * PB)
        y = np.take_along_axis(M, flat[:, :, None, :], 3).reshape(N, 8, 16, R, PB)
        d = np.add.reduce(np.abs(y - z[:, :, :, None, :]), axis=2)
        o0 = np.take_along_axis(O[:, 0], flat, 2).reshape(e.shape); o1 = np.take_along_axis(O[:, 1], flat, 2).reshape(e.shape)
        live = (o0 == v) | (o1 == v); stale = np.logical_not(live); has = np.any(stale, axis=2)
        dl = np.where(live, d, far); f = np.argmin(dl, axis=2); fire = np.min(dl, axis=2) < T[..., lo:lo + PB]
        m = np.argmax(np.where(live, d, -1), axis=2); s = np.argmin(np.where(stale, d, far), axis=2); j = np.where(has, np.argmax(stale, axis=2), f)
        ef = pick(e, f); em = pick(e, m); es = pick(e, s)
        yf = np.take_along_axis(M, ef[:, :, None, :], 3); ys = np.take_along_axis(M, es[:, :, None, :], 3)
        c = np.take_along_axis(K, ef, 2); hop = np.take_along_axis(O[:, 0], es, 2); hint = E[qi, gi, hop // PB, s, hop % PB]
        fb = fire[:, :, None, :]; hb = has[:, :, None, :]
        zn = np.where(fb, np.abs(z - yf), np.where(hb, (z + ys) >> 1, z))
        E[qi, gi, b, np.where(fire, j, s), lane] = np.where(fire, c, np.where(has, hint, es))
        Z[..., lo:lo + PB] = zn; T[..., lo:lo + PB] += np.where(fire, 0, INC)
        q, g, i = np.nonzero(first(c, fire)); O[q, t & 1, g, c[q, g, i]] = lo + i
        q, g, i = np.nonzero(first(ef, fire)); to = (q + 1 + t % (N - 1)) % N; a = ef[q, g, i]
        M[to, g, :, a] = zn[q, g, :, i]; K[to, g, a] = em[q, g, i]
    return {"ym": M.reshape(N, 128, W).astype(np.float32).astype(BF), "yk": K.astype(np.float32), "yo": O.reshape(N, 16, W).astype(np.float32),
            "ye": np.stack([gtable(a.reshape(8, -1)) for a in E]).astype(np.float32), "yz": Z.reshape(N, 128, V).astype(np.float32).astype(BF), "yt": T.astype(np.float32)}

@@ -1,0 +1,640 @@
+from concourse.mybir import dt, AluOpType as Op, ActivationFunctionType as AF
+
+N, STEPS = 4, 6
+BS = 3264
+EXT = 2 * BS
+B = float(2 ** 21)
+OFF = float(2 ** 22)
+BIG = float(2 ** 23)
+FAR = float(2 ** 21)
+MAGIC = 25165824.0
+GROW = 96.0 * 256
+DROP = 2304.0
+WIDE = 2240 + 24576 + 2304
+bf, f32, i32, u16 = "bfloat16", "float32", "int32", "uint16"
+
+SCRATCH = {}
+for _n, _w, _d in (
+        ("M", WIDE, bf), ("K", WIDE, bf), ("A", 2240, bf), ("AX", 6720, bf), ("X", BS, bf), ("ABX", BS, bf), ("Z0", 384, bf),
+        ("ZN", 1152, bf), ("ZI", 1152, bf), ("LS", 2304, bf), ("EM", 1152, bf), ("OO", 96, u16), ("OI", 96, u16), ("G", 384, u16),
+        ("EI", 384, i32), ("OW", 256, i32), ("OB", 256, bf), ("O0", 128, i32), ("EN", 128, i32), ("SR", 768, bf), ("S1", 256, i32), ("S3", 256, i32),
+        ("S2", 256, f32), ("TH", 384, i32), ("THF", 384, f32), ("TT", 32, f32), ("T0", 32, f32), ("XF", 192, f32), ("XG", 384, f32), ("XQ", 192, f32),
+        ("PI", 8, i32), ("CO", 40, f32), ("W", 512, f32), ("WI", 128, i32), ("WU", 192, u16), ("GE", 16, bf), ("CU", 64, u16), ("CL", 256, f32), ("CH", 80, bf),
+        ("LB", 144, bf), ("LD", 144, bf), ("L0", 144, bf), ("L1", 144, bf), ("LE", 144, bf), ("LN", 144, bf), ("LP", 144, bf), ("LH", 144, bf), ("LF", 144, f32),
+        ("BO", 144, bf), ("I1", 128, bf), ("IB", 128, bf), ("NB", 128, bf), ("ON", 128, bf), ("TR", 128, bf), ("BC", 128, bf),
+        ("C15", 192, bf), ("CAW", 192, f32), ("TWO", 192, bf), ("HALF", 192, bf), ("ONE", 192, bf), ("CF", 192, bf), ("CM", 192, bf), ("NV", 384, bf),
+        ("DS", 192, f32), ("VR", 384, bf), ("LW", 592, bf), ("LQ", 192, bf), ("SG", 192, bf), ("Q", 192, bf), ("SIG", 208, bf), ("DF", 192, f32),
+        ("DC", 192, f32), ("SC", 1344, f32), ("ZS", 1152, bf), ("OK", 128, bf), ("XS", 192, bf), ("U", 192, f32), ("CB", 192, f32), ("B0", 384, bf), ("GM", 192, bf), ("VAL", 192, bf),
+        ("EF", 192, f32), ("YE", 384, f32), ("YT", 384, f32), ("YO", 256, f32), ("YK", 128, f32), ("T1", 384, bf), ("T2", 208, bf), ("T3", 576, bf), ("T4", 8, f32), ("T5", 192, f32)):
+    SCRATCH[_n] = ("sbuf", [128, _w], _d)
+SCRATCH["ZR0"] = ("sbuf", [128, 12, 256], bf)
+SCRATCH["ZR1"] = ("sbuf", [128, 12, 256], bf)
+for _k in range(8):
+    SCRATCH["P%d" % _k] = ("psum", [128, 512], f32)
+SEMAPHORES = ["v", "a", "pe", "p", "sent"] + ["d%d" % _k for _k in range(40)] + ["r%d" % _k for _k in range(18)]
+CY, WAKE, FLIGHT = 0.83, 60.0, 2600.0
+URGENCY = ['@(Z9<xhkvJE(jMOFbh[xpO*ocTq]E`B]j5Sxx5d(tW(s.gPi`(u=bFQ9LxJXnK,O\\KN6(x/MTMe3xwS:>>nL\\t[7s(o(:WGnvo5c<(q2e;([=W3Cx`(x+(rl*+os;^x*_xK=8=I((\\fFQKiS(x)PH52<lTN:(+g(4/D-M,7U-(vT4jjet?xsSQR(C1X+kuponnGx4d^e-IxWV3d(XL(uvN<(xxg:N(f?Mu8a_>:)T5BY(,S.hFeH-txQ47iGH.2AHjU(X2G+-<;rk3@2>,ONp^B1+rK^Ya@IFg6v0(f7xbN+JV]H071g]j=']
+PLAN = {}
+FDF, FZS, FCB = True, True, False
+CHUNKS = ((0, 4), (4, 8), (8, 11), (11, 12))
+AUXV0, AUXV = (4, 5), ()
+
+
+def needs(ops):
+    seen, deps, after = {}, [], []
+    for n, o in enumerate(ops):
+        e, d, f = o["e"], set(), set(o["after"])
+        for w, accs in ((0, o["r"]), (1, o["w"])):
+            for (name, lo, hi, pk) in accs:
+                for (l2, h2, p2, w2, m) in seen.get(name, []):
+                    e2 = ops[m]["e"]
+                    if name[0] == "P" and name[1:].isdigit():
+                        if e2 == e == "pe":
+                            f.add(m)
+                        elif e2 != e or ((w or w2) and lo < h2 and l2 < hi):
+                            d.add(m)
+                    elif (w or w2) and lo < h2 and l2 < hi and (pk is None or p2 is None or pk == p2):
+                        d.add(m)
+        for w, accs in ((0, o["r"]), (1, o["w"])):
+            for (name, lo, hi, pk) in accs:
+                old = seen.get(name, [])
+                if w and pk is None:
+                    old = [x for x in old if not (lo <= x[0] and x[1] <= hi)]
+                seen[name] = old + [(lo, hi, pk, w, n)]
+        deps.append(d)
+        after.append(f)
+    return deps, after
+
+
+def place(ops, pred, prio):
+    start, busy, end = [0.0] * len(ops), {}, 0.0
+    for i in prio:
+        q, c, l = ops[i]
+        s = 0.0
+        for m, d in pred[i]:
+            if start[m] + d > s:
+                s = start[m] + d
+        line = busy.setdefault(q, [])
+        lo, hi = 0, len(line)
+        while lo < hi:
+            mid = (lo + hi) // 2
+            if line[mid][1] <= s:
+                lo = mid + 1
+            else:
+                hi = mid
+        while lo < len(line) and line[lo][0] < s + c:
+            s = max(s, line[lo][1])
+            lo += 1
+        line.insert(lo, (s, s + c))
+        start[i] = s
+        if s + c + l > end:
+            end = s + c + l
+    return start, end
+
+
+def chains(succ, short):
+    rest = [0.0] * len(short)
+    for i in range(len(short) - 1, -1, -1):
+        rest[i] = max([rest[j] for j in succ[i]] + [0.0]) + short[i][1] + short[i][2] + WAKE
+    return rest
+
+
+def ranked(pred, succ, rest, kind, urge):
+    key = [rest[i] + 100.0 * urge[kind[i]] for i in range(len(rest))]
+    for i in range(len(rest) - 1, -1, -1):
+        for j in succ[i]:
+            if key[j] >= key[i]:
+                key[i] = key[j] + 0.01
+    return sorted(range(len(rest)), key=lambda i: -key[i])
+
+
+def order(ops, deps, after):
+    pred, succ, short, kind, nk = graph(ops, deps, after)
+    urge = [ord(c) - 80 for c in URGENCY[0]] if len(URGENCY[0]) == nk else [0] * nk
+    start = place(short, pred, ranked(pred, succ, chains(succ, short), kind, urge))[0]
+    return sorted(range(len(ops)), key=lambda i: start[i])
+
+
+def graph(ops, deps, after):
+    n = len(ops)
+    pred, succ = [[] for _ in ops], [[] for _ in ops]
+    for i in range(n):
+        for m in deps[i] | after[i]:
+            pred[i].append((m, ops[m]["c"] + ops[m]["l"] + (WAKE if m in deps[i] else 0.0) + 0.001))
+            succ[m].append(i)
+    short = [(o["q"], o["c"], o["l"]) for o in ops]
+    kinds = sorted(set(o["kind"] for o in ops))
+    kind = [kinds.index(o["kind"]) for o in ops]
+    return pred, succ, short, kind, len(kinds)
+
+
+def schedule(g, T, ops):
+    queue = {"v": g.vector, "a": g.scalar, "pe": g.tensor, "p": g, "sp": g.sync}
+    deps, after = needs(ops)
+    if "seq" not in PLAN:
+        PLAN["seq"] = order(ops, deps, after)
+    seq = PLAN["seq"]
+    at = {m: n for n, m in enumerate(seq)}
+    known, clock, waits, marked = {e: {} for e in queue}, {}, {}, set()
+    for i in seq:
+        o = ops[i]
+        mine, ws = known[o["e"]], []
+        for m in sorted(deps[i], key=lambda m: -at[m]):
+            key = ops[m]["e"] if ops[m]["k"] == "c" else ("x", m)
+            if ops[m]["k"] == "s" or mine.get(key, -1) >= at[m]:
+                continue
+            ws.append(m)
+            marked.add(m)
+            for k2, v2 in clock[m].items():
+                if mine.get(k2, -1) < v2:
+                    mine[k2] = v2
+        waits[i] = ws
+        clock[i] = {} if o["k"] == "x" else dict(mine)
+        clock[i][o["e"] if o["k"] == "c" else ("x", i)] = at[i]
+    count, val, nd, sent = {e: 0 for e in queue}, {}, 0, 0
+    for i in seq:
+        o = ops[i]
+        e = o["e"]
+        for m in waits[i]:
+            queue[e].wait_ge(val[m][0], val[m][1])
+        if o["k"] == "c":
+            ins = o["f"]()
+            if i in marked:
+                count[e] += 1
+                val[i] = (T.sem[e], count[e])
+                ins.then_inc(T.sem[e], 1)
+        elif o["k"] == "d":
+            val[i] = (T.sem["d%d" % nd], 16)
+            nd += 1
+            o["f"]().then_inc(val[i][0], 16)
+        elif o["k"] == "x":
+            val[i] = o["f"]
+        else:
+            sent += o["f"]()
+    for i in seq:
+        if ops[i]["k"] in "dx" and i not in marked:
+            g.sync.wait_ge(val[i][0], val[i][1])
+    g.wait_ge(T.sem["sent"], sent)
+
+
+def rank_program(g, core, T, topo):
+    rank = T.rank_of(core)
+    if rank is None:
+        return
+    ops, sends, step = [], {}, [-1, {}]
+    V, S, PE = g.vector, g.scalar, g.tensor
+
+    def v(name, lo, hi, st=1):
+        return (T[name][:, lo:hi:st] if st > 1 else T[name][:, lo:hi], [(name, lo, hi, None)], [], (hi - lo + st - 1) // st, False)
+
+    def raw(ap, name, lo=0, hi=10 ** 6, pk=None, n=0):
+        return (ap, [(name, lo, hi, pk)], [], n, False)
+
+    def ind(win, off):
+        return (win[0].indirect(off[0]), win[1], off[1], 16 * off[3], True)
+
+    def op(e, f, outs, ins, c, k="c", lat=0.0, after=()):
+        r, w = [], []
+        for x in ins:
+            if isinstance(x, tuple):
+                r += x[1] + x[2]
+        for x in outs:
+            w += x[1]
+            r += x[2]
+        key = (step[0] < 0, e, k, w[0][0] if w else r[0][0])
+        step[1][key] = step[1].get(key, 0) + 1
+        ops.append({"kind": key + (step[1][key],), "e": e, "q": "x" if k == "x" else e, "f": f, "r": r, "w": w, "k": k, "c": c, "l": lat, "after": after})
+
+    def cost(o, x, f=1.0):
+        n = max(o[3], x[3])
+        if o[4]:
+            return 50 + 3.8 * CY * n
+        if x[4]:
+            return 50 + 1.56 * CY * n
+        if f == 1.0 and all(SCRATCH[y[1][0][0]][2] in (bf, u16) for y in (o, x)):
+            f = 0.5
+        return 30 + CY * max(64, f * n)
+
+    def a_(x):
+        return x[0] if isinstance(x, tuple) else x
+
+    def tt(o, x, y, f):
+        two = 1.01 if "psum" in (SCRATCH[x[1][0][0]][0], SCRATCH[y[1][0][0]][0]) else 2.0
+        op("v", lambda: V.tensor_tensor(o[0], x[0], y[0], f), [o], [x, y], cost(o, x, two))
+
+    def ts(o, x, s1, f1, s2=None, f2=None):
+        if f2 is None:
+            op("v", lambda: V.tensor_scalar(o[0], x[0], a_(s1), None, f1), [o], [x, s1], cost(o, x))
+        else:
+            op("v", lambda: V.tensor_scalar(o[0], x[0], a_(s1), a_(s2), f1, f2), [o], [x, s1, s2], cost(o, x))
+
+    def cp(o, x):
+        op("v", lambda: V.tensor_copy(o[0], x[0]), [o], [x], cost(o, x))
+
+    def ms(o, c):
+        op("v", lambda: V.memset(o[0], c), [o], [], cost(o, o))
+
+    def scan(o, d0, d1, f):
+        op("v", lambda: V.tensor_tensor_scan(o[0], d0[0], d1[0], 0.0, Op.add, f), [o], [d0, d1], cost(o, d0))
+
+    def act(o, x, f=AF.Copy, bias=0.0, scale=1.0):
+        if f == AF.Copy:
+            op("a", lambda: S.activation(o[0], x[0], f), [o], [x], cost(o, x, 1.01))
+        else:
+            op("a", lambda: S.activation(o[0], x[0], f, bias=a_(bias), scale=a_(scale)), [o], [x, bias, scale], cost(o, x, 1.01))
+
+    def lin(o, x, scale, bias=0.0):
+        act(o, x, AF.Identity, bias, scale)
+
+    def io(o, pattern, base, cm=0):
+        if SCRATCH[o[1][0][0]][2] == i32:
+            op("p", lambda: g.iota(o[0], pattern, base, cm), [o], [], 130 + 2 * CY * o[3])
+        else:
+            op("p", lambda: g.iota(o[0], pattern, base, cm, allow_small_or_imprecise_dtypes=True), [o], [], 130 + 2 * CY * o[3])
+
+    def sel(o, x, pattern, f, fill, cm=0):
+        op("p", lambda: g.affine_select(o[0], x[0], pattern, f, fill, 0, cm), [o], [x], 170 + 2 * CY * o[3])
+
+    def mm(items, start, stop):
+        def f():
+            for n, (o, l, r) in enumerate(items):
+                ins = PE.matmul(o[0], l[0], r[0], start and n == 0, stop and n == len(items) - 1)
+            return ins
+        c = sum(0.42 * max(64, r[3]) * (4 if SCRATCH[l[1][0][0]][2] == f32 else 1) for o, l, r in items)
+        op("pe", f, [x[0] for x in items], [x[1] for x in items] + [x[2] for x in items], c)
+
+    def diag(o, L, name, lo, hi):
+        return [(o, v(L, 15 - q, 143 - q), v(name, lo + q, hi, 16)) for q in range(16)]
+
+    def dma(e, o, x, kb=32):
+        q = {"sp": g.sync, "a": g.scalar}[e]
+        op(e, lambda: q.dma_start(o[0], x[0]), [o], [x], 50.0, "d", 2000.0 + 5 * kb)
+
+    def send(t, j, dst, src):
+        to = T.cores[(rank + 1 + t % (N - 1)) % N]
+        rid, pid = topo.addr(to, core)
+
+        def f():
+            g.remote_dma(dst[0], src[0], T.sem["r%d" % (3 * t + j)], T.sem["sent"], pid, rid, topo.mask(core, to))
+            return len(topo.engines(core, to))
+        sends[t, j] = len(ops)
+        op("p", f, [], [src], 500.0, "s")
+
+    def arrive(t, j, dst):
+        frm = T.cores[(rank - 1 - t % (N - 1)) % N]
+        op("sp", (T.sem["r%d" % (3 * t + j)], len(topo.engines(frm, core))), [dst], [], 0.0, "x", FLIGHT, (sends[t, j],))
+
+    def col(j):
+        return v("CO", j, j + 1)
+
+    def w(j, n=12):
+        return v("W", 16 * j, 16 * j + n)
+
+    def wi(j, n=1):
+        return v("WI", 12 * j, 12 * (j + n))
+
+    def wu(j, n=12):
+        return v("WU", 16 * j, 16 * j + n)
+
+    def cl(j, n=12):
+        return v("CL", 16 * j, 16 * j + n)
+
+    def ch(j):
+        return v("CH", 12 * j, 12 * j + 12)
+
+    def zr(b, lo, hi):
+        return raw(T["ZR%d" % b][:, :, lo:hi], "ZR%d" % b, n=12 * (hi - lo))
+
+    def rows(name, r):
+        return raw(T[name][r::16, 0:2048], name, 0, 2048, r)
+
+    def hbm(name):
+        return raw(T[name][:], name)
+
+    add, sub, mul, mx, mn = Op.add, Op.subtract, Op.mult, Op.max, Op.min
+    eq, ne, ge, lt, band = Op.is_equal, Op.not_equal, Op.is_ge, Op.is_lt, Op.bitwise_and
+    x12, x128, x144, x192 = v("XF", 0, 12), v("XF", 0, 128), v("XF", 0, 144), v("XF", 0, 192)
+    xg, xq = v("XG", 0, 192), v("XQ", 0, 192)
+    cN, cG15, cP, cG, cNE, cK0, cK1 = 0, 1, 2, 3, 5, 6, 7
+    cW01, cWE, cWH, cN1, cA15, cW0, cW1, cW2, cW3, cW4, cW5 = 8, 10, 12, 14, 15, 16, 17, 18, 19, 20, 21
+    c192, c128, c12, c24, cW35, cW416, cBO, cN14, cT, cXW, cNN, cVI, cK, cA30 = range(22, 36)
+    IL, VID, DUM, EXI, C2, CT, CA2 = range(7)
+    WA, HA, HN = 0, 2, 3
+
+    dma("sp", v("OW", 0, 256), hbm("own"), 128)
+    dma("a", v("O0", 0, 128), raw(T.own[0:8, :], "own"), 64)
+    dma("sp", v("EI", 0, 384), hbm("ends"), 192)
+    dma("a", v("Z0", 0, 384), hbm("st"), 96)
+    dma("sp", v("M", 0, 2048), hbm("msg"), 512)
+    dma("a", v("EN", 0, 128), hbm("enc"), 64)
+    io(v("TH", 0, 384), [[0, 384]], 0)
+    dma("sp", raw(T.TH[0::16, :], "TH"), hbm("th"))
+    io(v("PI", 0, 1), [[0, 1]], 0, 1)
+    io(col(cP), [[0, 1]], 0, 1)
+    io(x192, [[1, 192]], 0)
+    io(v("XG", 0, 384), [[16, 24], [0, 16]], 0)
+    io(xq, [[0, 12], [1, 16]], 0)
+    io(v("SR", 128, 256), [[0, 8], [1, 16]], 0)
+    io(v("K", 0, 2048), [[0, 2048]], 0)
+    io(v("C15", 0, 192), [[16, 12], [0, 16]], 15)
+    io(v("CAW", 0, 192), [[16, 12], [0, 16]], 15 + int(OFF))
+    io(v("X", 3072, BS), [[0, 192]], 0)
+    io(v("LW", 0, 592), [[0, 592]], 4000)
+    io(v("SIG", 0, 1), [[0, 1]], 0)
+    io(cl(CT), [[2, 12]], int(BIG) - 128)
+    io(v("CH", 48, 72), [[0, 2], [1, 12]], -64)
+    io(cl(C2), [[32, 12]], 30 + int(BIG))
+    io(v("CH", 0, 24), [[-384, 2], [-16, 12]], 576)
+    io(ch(HA), [[-256, 12]], 0)
+    io(v("ONE", 0, 192), [[0, 192]], 1)
+    one = v("ONE", 0, 192)
+    sel(v("I1", 0, 128), v("ONE", 0, 128), [[-1, 128]], eq, 0.0, 1)
+    sel(v("CM", 0, 192), one, [[0, 12], [1, 16]], ne, -BIG)
+    lin(v("CF", 0, 192), v("CM", 0, 192), -1.0)
+    lin(v("TWO", 0, 192), one, 2.0)
+    lin(v("HALF", 0, 192), one, -0.5)
+    ms(v("A", 0, 2240), 0.0)
+    ts(v("PI", 1, 2), v("PI", 0, 1), 15, band)
+    ts(v("PI", 2, 3), v("PI", 0, 1), 0x70, band)
+    ts(v("PI", 3, 4), v("PI", 0, 1), 14, band)
+    cp(col(cN), v("PI", 1, 2))
+    cp(col(cG), v("PI", 2, 3))
+    cp(col(cN14), v("PI", 3, 4))
+    lin(col(c128), col(cN), 128.0)
+    lin(col(c12), col(cN), 12.0)
+    lin(col(cG15), col(cG), 1.0, 15.0)
+    lin(col(c192), col(cN), -1.0, 192.0)
+    lin(col(cNN), col(cN), -1.0)
+    lin(col(cVI), col(cN), 2.0, 192.0)
+    ts(v("CO", 8, 14), v("XF", 0, 6), col(cN14), eq)
+    ts(v("CO", 16, 22), v("XF", 0, 6), col(cN), eq)
+    ts(col(cA15), col(cN), 15.0, ne, FAR, mul)
+    lin(col(cNE), col(cWE), -1.0)
+    lin(col(c24), col(cW2), 2048.0)
+    lin(col(cW35), col(cW3), 1.0, col(cW5))
+    lin(col(cW416), col(cW4), 16.0)
+    lin(col(cXW), col(cW416), 1.0, col(cW2))
+    lin(col(cK1), col(cW1), -1.0, 1.0)
+    lin(col(cK), col(cW0), -1.0, 1.0)
+    lin(col(cK0), col(cWH), -1.0, col(cK))
+    lin(col(cT), col(cG), 0.5, 7.0)
+    lin(col(cBO), col(cN), 64.0, col(cT))
+    ts(v("LB", 0, 144), x144, col(cG15), eq)
+    for name, c in (("L0", col(cW0)), ("L1", col(cW1)), ("LE", col(cWE)), ("LN", col(cNE)), ("LP", col(cW01)), ("LH", col(cWH)), ("LD", 128.0)):
+        lin(v(name, 0, 144), v("LB", 0, 144), c)
+    lin(v("LF", 0, 144), v("L0", 0, 144), 256.0)
+    ts(v("BO", 0, 144), x144, col(cBO), eq, col(cW01), mul)
+    ib, nb, i1 = v("IB", 0, 128), v("NB", 0, 128), v("I1", 0, 128)
+    lin(ib, i1, B)
+    lin(nb, i1, -B)
+    ts(v("ON", 0, 128), v("XG", 0, 128), col(cG), eq)
+    lin(v("BC", 0, 128), v("ON", 0, 128), col(cWE))
+    lin(v("OK", 0, 128), v("ON", 0, 128), 4096.0)
+    sel(v("TR", 0, 128), v("OK", 0, 128), [[1, 128]], Op.is_gt, 0.0, -1)
+    lin(v("NV", 0, 384), v("XG", 0, 384), -1.0, col(c192))
+    lin(cl(IL), x12, 16.0, col(cN))
+    lin(cl(VID), x12, 16.0, col(cVI))
+    lin(cl(DUM), cl(IL), 1.0, 2048.0)
+    lin(cl(EXI), cl(IL), 1.0, float(EXT))
+    lin(ch(HN), x12, 0.0, col(cNN))
+    cp(v("CU", 24, 36), x12)
+    ts(v("CU", 0, 12), x12, col(c12), add)
+    ts(v("CU", 12, 24), x12, col(c12), add, 192.0, add)
+    ts(w(30), cl(IL), -5.5, add, 1.0 / 12, mul)
+    cp(wi(9), w(30))
+    lin(w(31), cl(IL), 16.0)
+    ts(w(30), wi(9), -191.0, mul)
+    tt(w(30), w(30), w(31), add)
+    cp(v("CU", 36, 48), w(30))
+    lin(v("T4", 0, 8), v("XF", 0, 8), 96.0)
+    io(v("T2", 0, 1), [[0, 1]], 0)
+    ts(v("T2", 1, 193), xq, col(cN), eq)
+    mm([(v("P6", 0, 192), ib, v("T2", 1, 193)), (v("P6", 0, 192), nb, v("T2", 0, 192))], True, True)
+    act(v("T5", 0, 192), v("P6", 0, 192))
+    sel(v("DS", 0, 192), v("T5", 0, 192), [[0, 12], [1, 16]], ne, 4 * FAR)
+    lin(col(cA30), col(cA15), 2.0)
+    io(v("ABX", 3072, BS), [[0, 192]], 0)
+    lin(v("VR", 192, 384), x192, col(cW1))
+    lin(col(cN1), col(cW0), -192.0)
+    lin(v("T3", 0, 192), x192, col(cW0), col(cN1))
+    lin(v("T3", 192, 384), xg, col(cW416))
+    lin(v("T3", 384, 576), xq, col(cW5))
+    mm([(v("P4", 0, 192), i1, v("T3", 192 * j, 192 * j + 192)) for j in range(3)], True, True)
+    act(v("VR", 0, 192), v("P4", 0, 192))
+    lin(v("T1", 0, 192), xg, col(cXW), col(c24))
+    lin(v("T1", 192, 384), xq, col(cW35))
+    mm([(v("P5", 0, 192), i1, v("T1", 192 * j, 192 * j + 192)) for j in range(2)], True, True)
+    for o in (v("AX", 3072, BS), v("AX", BS + 3072, 2 * BS), v("K", 2048, 2240)):
+        act(o, v("P5", 0, 192))
+    lin(v("SR", 0, 128), v("XG", 0, 128), 1.0, col(c128))
+    dma("sp", rows("A", 2), v("SR", 0, 128))
+    dma("sp", rows("A", 3), v("SR", 128, 256))
+    ts(v("OB", 0, 256), v("OW", 0, 256), -192.0, add)
+    dma("sp", rows("A", 0), raw(T.OB[0:64, :], "OB"))
+    dma("sp", rows("A", 1), raw(T.OB[64:128, :], "OB"))
+    ts(v("S1", 0, 128), v("O0", 0, 128), 0x1F0, band)
+    ts(v("S1", 128, 256), v("O0", 0, 128), 15, band)
+    ts(v("S2", 0, 128), v("O0", 0, 128), 192.0, ge, float(BS - 3072), mul)
+    ts(v("S2", 128, 256), v("S1", 0, 128), 16.0, mul)
+    cp(v("SR", 384, 512), v("S1", 128, 256))
+    tt(v("SR", 256, 384), v("S2", 0, 128), v("S2", 128, 256), add)
+    dma("sp", rows("A", 5), v("SR", 384, 512))
+    dma("sp", rows("A", 4), v("SR", 256, 384))
+    ts(v("S3", 0, 128), v("EN", 0, 128), 0x7F0, band)
+    ts(v("S3", 128, 256), v("EN", 0, 128), 15, band)
+    cp(v("SR", 512, 768), v("S3", 0, 256))
+    dma("sp", rows("K", 2), v("SR", 512, 640))
+    dma("sp", rows("K", 3), v("SR", 640, 768))
+    cp(v("G", 0, 192), ind(v("EI", 0, 384), v("CU", 0, 12)))
+    cp(v("G", 192, 384), ind(v("EI", 0, 384), v("CU", 12, 24)))
+    cp(v("THF", 0, 384), v("TH", 0, 384))
+    mm(diag(v("P7", 0, 24), "LF", "THF", 0, 384), True, True)
+    tt(v("TT", 0, 12), v("P7", 0, 12), cl(CT), add)
+    tt(v("TT", 12, 24), v("P7", 12, 24), cl(CT), add)
+    act(v("T0", 0, 24), v("TT", 0, 24))
+    cp(zr(0, 0, 16), v("Z0", 0, 192))
+    for s in (16, 32, 64, 128):
+        cp(zr(0, s, 2 * s), zr(0, 0, s))
+
+    def spread(b, z):
+        sel(zr(b, 0, 16), z, [[0, 192]], ge, 0.0)
+        for s in (16, 32, 64, 128):
+            sel(zr(b, s, 2 * s), zr(b, 0, s), [[0, 12 * s]], ge, 0.0)
+    spread(1, v("Z0", 192, 384))
+
+    THR, BASE, TD, OFFS, HINT, FE, CLI, DUP, PM, NFA = range(10)
+    U15, THS, J3, F3, S3, CLA = 10, 12, 14, 17, 20, 23
+
+    def w3(s, j):
+        return v("W", 16 * s + 12 * j, 16 * s + 12 * j + 12)
+    iM, iS, iJ, iF, cM, cS, cJ, cF = range(8)
+    JF, WX, EFU, CO_, VU, PU, JM = range(7)
+    CU_ = 8
+
+    def take(t, j, table, src):
+        arrive(t, j, src)
+        cp(ind(v(table, 0, WIDE), v("OI", 16 * t, 16 * t + 12)), src)
+
+    for t in range(STEPS):
+        b = t % 2
+        step[0], step[1] = t, {}
+        blk = v("AX", BS * b, BS * b + BS)
+        z = v("Z0", 192 * b, 192 * b + 192) if t < 2 else v("ZN", 192 * (t - 2), 192 * (t - 1))
+        zn = v("ZN", 192 * t, 192 * t + 192)
+        for c in range(3):
+            for e in (2 * c, 2 * c + 1):
+                (cp if e in (AUXV if t else AUXV0) else act)(v("AX", BS * b + 512 * e, BS * b + 512 * e + 512),
+                                                             ind(v("A", 0, 2240), v("G", 192 * b + 32 * e, 192 * b + 32 * e + 32)))
+            for P, L in (("P1", "L0"), ("P2", "L1")):
+                first = [(v(P, 0, 192), i1, v("NV", 192 * b, 192 * b + 192))] if c == 0 else []
+                mm(first + diag(v(P, 64 * c, 64 * c + 64), L, "AX", BS * b + 1024 * c, BS * b + 1024 * c + 1024), c == 0, c == 2)
+        if t == 1:
+            relist(0)
+        act(v("SG", 0, 192), v("P1", 0, 192), AF.Sign)
+        tt(v("Q", 0, 192), v("SG", 0, 192), v("P2", 0, 192), mul)
+        ts(v("SIG", 1, 193), v("Q", 0, 192), 0.0, ne)
+        s0, s1 = v("SIG", 0, 192), v("SIG", 1, 193)
+        for o, p, q, c in ((v("P3", 0, 192), ib, nb, "CF"), (v("P3", 192, 384), nb, ib, "CF"), (v("P5", 0, 192), nb, ib, "CM")):
+            mm([(o, i1, v(c, 0, 192)), (o, p, s0), (o, q, s1)], True, True)
+        ths = v("P4", 32, 56)
+        mm([(ths, ib, v("TWO", 0, 24)), (ths, i1, v("CH", 48, 72))] + [(v("P4", 32 + 12 * j, 44 + 12 * j), ib, v("SIG", 16, 193, 16)) for j in range(2)], True, True)
+        if FDF:
+            act(v("DF", 0, 192), v("P3", 0, 192))
+        tt(w(THR), v("TT", 12 * b, 12 * b + 12), v("P4", 32, 44), sub)
+        act(w(THS, 24), ths)
+        scan(v("SC", 192, 384), v("P3", 192, 384), v("CAW", 0, 192), mn)
+        if t:
+            arrive(t - 1, 1, v("OI", 16 * t - 16, 16 * t - 4))
+            take(t - 1, 0, "M", v("ZI", 192 * t - 192, 192 * t))
+            take(t - 1, 2, "K", v("EM", 192 * t - 192, 192 * t))
+        for a in range(12):
+            tt(v("X", 256 * a, 256 * a + 256), ind(v("M", 0, 2048), v("G", 192 * b + 16 * a, 192 * b + 16 * a + 16)),
+               raw(T["ZR%d" % b][:, a], "ZR%d" % b), sub)
+        for lo, hi in CHUNKS:
+            act(v("ABX", 256 * lo, 256 * hi), v("X", 256 * lo, 256 * hi), AF.Abs, scale=2.0)
+            first = [(v("P0", 0, 192), i1, v("C15", 0, 192)), (v("P0", 0, 192), ib, v("TWO", 0, 192))] if lo == 0 else []
+            mm(first + diag(v("P0", 16 * lo, 16 * hi), "LD", "ABX", 256 * lo, 256 * hi), lo == 0, hi == 12)
+        if FDF:
+            scan(v("SC", 384, 576), v("DF", 0, 192), v("P0", 0, 192), mn)
+        act(v("DC", 0, 192), v("P0", 0, 192))
+        if not FDF:
+            scan(v("SC", 384, 576), v("P3", 0, 192), v("DC", 0, 192), mn)
+        tt(wi(iF), v("SC", 399, 576, 16), w(THR), mn)
+        ts(wi(cF), wi(iF), 255, band)
+        ts(wu(JF), wi(cF), 16.0, mul, col(cN), add)
+        ts(w3(F3, 1), wi(cF), 192.0, ge, GROW, mul)
+        nf = w3(F3, 1)
+        tt(v("TT", 12 * b, 12 * b + 12), v("TT", 12 * b, 12 * b + 12), nf, add)
+        act(v("LW", 192, 384), ind(blk, wu(JF)))
+        zs = v("ZS", 192 * t, 192 * t + 192)
+        if FZS:
+            lin(zs, ind(v("ABX", 0, BS), wu(JF)), 0.5)
+            send(t, 0, v("ZI", 192 * t, 192 * t + 192), zs)
+        mm([(v("P2", 0, 192), v("BC", 0, 128), v("LW", 192, 384))], True, True)
+        mm([(v("P4", 0, 12), i1, ch(WA + b))] + diag(v("P4", 0, 12), "LP", "LW", 192, 384), True, True)
+        mm(diag(v("P1", 0, 12), "LN", "LW", 192, 384), True, False)
+        scan(v("SC", 960, 1152), v("DS", 0, 192), v("P2", 0, 192), mn)
+        ts(wu(WX), v("P4", 0, 12), col(cNN), add)
+        tt(v("GE", 0, 12), v("P4", 0, 12), cl(VID), ge)
+        act(v("LQ", 0, 192), ind(v("LW", 0, 592), wu(WX)))
+        ts(wu(EFU), v("SC", 975, 1152, 16), col(cA15), add)
+        lin(w(NFA), nf, 1.0, col(cA15))
+        tt(w(BASE), v("SC", 975, 1152, 16), w(NFA), add)
+        mm([(v("P1", 0, 12), ib, v("GE", 0, 12))], False, False)
+        mm(diag(v("P1", 0, 12), "LE", "LQ", 0, 192), False, True)
+        ts(w(TD), v("P1", 0, 12), 0.0, eq, DROP, mul)
+        tt(w(OFFS), w(TD), w(BASE), add)
+        cp(v("OO", 16 * t, 16 * t + 12), w(OFFS))
+        send(t, 1, v("OI", 16 * t, 16 * t + 12), v("OO", 16 * t, 16 * t + 12))
+        scan(v("SC", 0, 192), v("P3", 192, 384), v("DC", 0, 192), mn)
+        scan(v("SC", 576, 768), v("P5", 0, 192), v("DC", 0, 192), mx)
+        tt(wi(iS, 2), v("SC", 15, 384, 16), w(THS, 24), mn)
+        tt(wi(iM), cl(C2), v("SC", 591, 768, 16), sub)
+        ts(wi(cM, 3), wi(iM, 3), 255, band)
+        ts(wu(JM, 24), wi(cM, 2), 16.0, mul, col(cN), add)
+        ts(w(J3, 36), wi(cS, 3), 16.0, mul, col(cN), add)
+        act(w3(F3, 0), w3(J3, 2), AF.Relu, 3072.0 * 8192, -8192.0)
+        act(w3(F3, 2), w3(J3, 1), AF.Relu, 3072.0 * 8192, -8192.0)
+        act(v("XS", 0, 192), ind(v("X", 0, BS), v("WU", 16 * JM + 12, 16 * JM + 24)))
+        u = v("P7", 192, 384)
+        mm([(u, i1, v("HALF", 0, 192)), (u, i1, z), (u, i1, z), (u, i1, v("XS", 0, 192))], True, True)
+        lin(v("U", 0, 192), u, 1.0, MAGIC)
+        lin(v("ABX", 3072, BS), v("U", 0, 192), 1.0, -MAGIC)
+        lin(zn, ind(v("ABX", 0, BS), wu(JF)), 0.5)
+        if not FZS:
+            send(t, 0, v("ZI", 192 * t, 192 * t + 192), zn)
+        act(v("LS", 384 * t, 384 * t + 384), ind(blk, wu(JM, 24)))
+        send(t, 2, v("EM", 192 * t, 192 * t + 192), v("LS", 384 * t, 384 * t + 192))
+        if t < STEPS - 2:
+            spread(b, zn)
+        ext = v("AX", EXT, EXT + 192)
+        act(ext, ind(v("K", 0, 2240), wu(EFU)))
+        mm([(v("P6", 0, 192), v("BC", 0, 128), ext)], True, True)
+        if not FCB:
+            mm([(v("P0", 192, 384), v("BC", 0, 128), ext)], True, True)
+            act(v("CB", 0, 192), v("P0", 192, 384))
+        scan(v("SC", 1152, 1344), v("DS", 0, 192), v("P6", 0, 192), mn)
+        craw = v("SC", 1167, 1344, 16)
+        ts(w(CLI), craw, col(cA15), add)
+        ts(wu(CU_), craw, col(cA15), add)
+        lin(w(CLA), craw, 1.0, col(cA30))
+        lin(v("GM", 0, 192), ind(v("A", 0, 2240), wu(CU_)), col(cK0 + b))
+        if FCB:
+            act(v("CB", 0, 192), ind(w(CLI), v("CU", 24, 36)))
+            tt(v("B0", 0, 192), v("CB", 0, 192), v("P6", 0, 192), eq)
+            tt(v("B0", 192, 368), v("CB", 0, 176), v("P6", 16, 192), eq)
+        else:
+            tt(v("B0", 0, 192), ind(w(CLI), v("CU", 24, 36)), v("CB", 0, 192), eq)
+            tt(v("B0", 192, 368), ind(w(CLI), v("CU", 24, 35)), v("CB", 16, 192), eq)
+        mm([(v("P6", 192, 384), v("TR", 0, 128), v("B0", 0, 192)), (v("P6", 208, 384), v("OK", 0, 128), v("B0", 192, 368))], True, True)
+        scan(v("SC", 768, 960), v("DS", 0, 192), v("P6", 192, 384), mn)
+        tt(w(DUP), v("SC", 783, 960, 16), w(CLA), add)
+        tt(w(DUP), w(DUP), cl(DUM), mn)
+        cp(wu(CO_), w(DUP))
+        for c in range(5, -1, -1):
+            tt(ind(v("A", 0, 2240), v("WU", 16 * CO_ + 2 * c, 16 * CO_ + 2 * c + 2)), v("GM", 32 * c, 32 * c + 32),
+               v("VR", 192 * b + 32 * c, 192 * b + 32 * c + 32), add)
+        h = v("P5", 192, 204)
+        mm([(h, i1, ch(HA)), (h, i1, ch(HN))] + diag(h, "LH", "LS", 384 * t + 192, 384 * t + 384), True, True)
+        tt(w(HINT), h, w3(J3, 0), add)
+        tt(w(FE), cl(EXI), nf, sub)
+        tt(w(HINT), w(HINT), w(FE), mx)
+        cp(wu(VU), w(HINT))
+        tt(w(S3, 36), w(J3, 36), w(F3, 36), add)
+        tt(w(PM), w3(S3, 0), w3(S3, 1), mn)
+        tt(w(PM), w(PM), w3(S3, 2), mn)
+        cp(wu(PU), w(PM))
+
+        def relist(t):
+            b = t % 2
+            act(v("VAL", 0, 192), ind(v("AX", 0, EXT + 192), wu(VU)))
+            cp(ind(v("AX", BS * b, BS * b + BS), wu(PU)), v("VAL", 0, 192))
+            items = diag(v("P7", 0, 192), "LE", "AX", BS * b, BS * b + 3072)
+            for c in range(4):
+                mm(items[4 * c:4 * c + 4], c == 0, c == 3)
+            if t < STEPS - 2:
+                cp(v("G", 192 * b, 192 * b + 192), v("P7", 0, 192))
+            else:
+                act(v("EF", 0, 192), v("P7", 0, 192))
+                act(v("YE", 192 * b, 192 * b + 192), ind(v("EF", 0, 192), v("CU", 36, 48)))
+                dma("sp", raw(T.ye[:, 192 * b:192 * b + 192], "ye", b, b + 1), v("YE", 192 * b, 192 * b + 192), 96)
+        if t:
+            relist(t)
+        if t >= STEPS - 2:
+            dma("sp", raw(T.yz[:, 192 * b:192 * b + 192], "yz", b, b + 1), zn, 48)
+    mm([(v("P1", 0, 256), v("BO", 7 - c, 135 - c), v("A", 256 * c, 256 * c + 256)) for c in range(8)], True, True)
+    lin(v("YO", 0, 256), v("P1", 0, 256), 1.0, 192.0)
+    dma("a", hbm("yo"), v("YO", 0, 256), 128)
+    arrive(STEPS - 1, 1, v("OI", 80, 92))
+    take(STEPS - 1, 0, "M", v("ZI", 960, 1152))
+    dma("sp", hbm("ym"), v("M", 0, 2048), 512)
+    take(STEPS - 1, 2, "K", v("EM", 960, 1152))
+    mm([(v("P2", 0, 128), v("LE", 15 - c, 143 - c), v("K", 128 * c, 128 * c + 128)) for c in range(16)], True, True)
+    act(v("YK", 0, 128), v("P2", 0, 128))
+    dma("a", hbm("yk"), v("YK", 0, 128), 64)
+    tt(w(24, 24), v("TT", 0, 24), v("T0", 0, 24), sub)
+    ts(w(26, 24), w(24, 24), 1.0 / GROW, mul, 0.25, add)
+    cp(wu(10, 24), w(26, 24))
+    tt(v("YT", 0, 384), ind(v("T4", 0, 8), wu(10, 24)), v("THF", 0, 384), add)
+    dma("sp", hbm("yt"), raw(T.YT[0::16, :], "YT"))
+    schedule(g, T, ops)

@@ -1,43 +1,47 @@
 from concourse.mybir import dt, AluOpType as Op, ActivationFunctionType as AF
 
 N, STEPS = 4, 6
-BS = 3264
+BS = 3456
 EXT = 2 * BS
 B = float(2 ** 21)
-OFF = float(2 ** 22)
-BIG = float(2 ** 23)
+BIG = float(2 ** 24)
 FAR = float(2 ** 21)
-MAGIC = 25165824.0
+ROUND = 12582912.0
 GROW = 96.0 * 256
 DROP = 2304.0
-WIDE = 2240 + 24576 + 2304
+LIFT = 256.0
+WIDE = 4608
+AW = 2816
 bf, f32, i32, u16 = "bfloat16", "float32", "int32", "uint16"
 
 SCRATCH = {}
 for _n, _w, _d in (
-        ("M", WIDE, bf), ("K", WIDE, bf), ("A", 2240, bf), ("AX", 6720, bf), ("X", BS, bf), ("ABX", BS, bf), ("Z0", 384, bf),
-        ("ZN", 1152, bf), ("ZI", 1152, bf), ("LS", 2304, bf), ("EM", 1152, bf), ("OO", 96, u16), ("OI", 96, u16), ("G", 384, u16),
-        ("EI", 384, i32), ("OW", 256, i32), ("OB", 256, bf), ("O0", 128, i32), ("EN", 128, i32), ("SR", 768, bf), ("S1", 256, i32), ("S3", 256, i32),
-        ("S2", 256, f32), ("TH", 384, i32), ("THF", 384, f32), ("TT", 32, f32), ("T0", 32, f32), ("XF", 192, f32), ("XG", 384, f32), ("XQ", 192, f32),
-        ("PI", 8, i32), ("CO", 40, f32), ("W", 512, f32), ("WI", 128, i32), ("WU", 192, u16), ("GE", 16, bf), ("CU", 64, u16), ("CL", 256, f32), ("CH", 80, bf),
-        ("LB", 144, bf), ("LD", 144, bf), ("L0", 144, bf), ("L1", 144, bf), ("LE", 144, bf), ("LN", 144, bf), ("LP", 144, bf), ("LH", 144, bf), ("LF", 144, f32),
-        ("BO", 144, bf), ("I1", 128, bf), ("IB", 128, bf), ("NB", 128, bf), ("ON", 128, bf), ("TR", 128, bf), ("BC", 128, bf),
-        ("C15", 192, bf), ("CAW", 192, f32), ("TWO", 192, bf), ("HALF", 192, bf), ("ONE", 192, bf), ("CF", 192, bf), ("CM", 192, bf), ("NV", 384, bf),
-        ("DS", 192, f32), ("VR", 384, bf), ("LW", 592, bf), ("LQ", 192, bf), ("SG", 192, bf), ("Q", 192, bf), ("SIG", 208, bf), ("DF", 192, f32),
-        ("DC", 192, f32), ("SC", 1344, f32), ("ZS", 1152, bf), ("OK", 128, bf), ("XS", 192, bf), ("U", 192, f32), ("CB", 192, f32), ("B0", 384, bf), ("GM", 192, bf), ("VAL", 192, bf),
-        ("EF", 192, f32), ("YE", 384, f32), ("YT", 384, f32), ("YO", 256, f32), ("YK", 128, f32), ("T1", 384, bf), ("T2", 208, bf), ("T3", 576, bf), ("T4", 8, f32), ("T5", 192, f32)):
+        ("M", WIDE, bf), ("K", WIDE, f32), ("KB", WIDE, bf), ("A", AW, bf), ("AX", EXT + 192, bf), ("X", BS, bf), ("ABX", 3072, bf),
+        ("ZE", 1344, bf), ("ZI", 1344, bf), ("EO", 960, f32), ("EM", 960, f32), ("OO", 96, u16), ("OI", 96, u16), ("G", 384, u16),
+        ("EI", 384, i32), ("OW", 256, i32), ("OB", 256, bf), ("OH", 512, bf), ("EN", 128, i32), ("SR", 256, bf), ("SK", 256, f32),
+        ("TH", 384, i32), ("THF", 384, f32), ("TT", 32, f32), ("XF", 192, bf), ("XG", 192, bf), ("XQ", 288, bf),
+        ("PI", 8, i32), ("CO", 48, f32), ("W", 96 * STEPS, f32), ("WI", 112 * STEPS, i32), ("WU", 144 * STEPS, u16), ("WB", 64 * STEPS, bf),
+        ("CU", 80, u16), ("CL", 128, f32), ("CH", 96, bf),
+        ("LB", 144, bf), ("LD", 144, bf), ("LR", 144, bf), ("LX", 144, bf), ("L0", 144, bf), ("L1", 144, bf), ("LE", 144, bf), ("LP", 144, bf),
+        ("LH", 144, bf), ("LT", 144, bf), ("LF", 144, f32), ("BO", 144, bf), ("I1", 128, bf), ("I2", 128, bf), ("IB", 128, bf), ("ID", 128, bf), ("ND", 128, bf),
+        ("IG", 128, bf), ("IO", 128, bf), ("IW", 128, bf), ("NW", 128, bf), ("IF", 128, f32), ("NF", 128, f32), ("ON", 128, bf), ("BC", 128, bf),
+        ("CAW", 192, f32), ("ONE", 288, bf), ("RS", 192, bf), ("RN", 192, bf), ("CM", 192, bf), ("NV", 384, bf), ("NM", 192, bf),
+        ("MK", 288, bf), ("DD", 288, bf), ("VR", 384, bf), ("LW", 592, bf), ("LQ", 192, bf), ("LS", 192, bf), ("SG", 192, bf), ("Q", 192, bf), ("SIG", 208, bf),
+        ("DT", 384, f32), ("SC", 1152, f32), ("XS", 192, bf), ("U", 192, f32), ("CB", 288, f32), ("B0", 288, bf), ("SB", 288, bf), ("GM", 192, bf), ("VAL", 192, bf),
+        ("EF", 192, f32), ("YE", 384, f32), ("YT", 384, f32), ("YO", 256, f32), ("YK", 128, f32), ("T1", 384, bf), ("T2", 384, bf), ("T3", 384, bf)):
     SCRATCH[_n] = ("sbuf", [128, _w], _d)
-SCRATCH["ZR0"] = ("sbuf", [128, 12, 256], bf)
-SCRATCH["ZR1"] = ("sbuf", [128, 12, 256], bf)
+SCRATCH["ZR0"] = ("sbuf", [128, 6, 512], bf)
+SCRATCH["ZR1"] = ("sbuf", [128, 6, 512], bf)
+SCRATCH["Z"] = ("sbuf", [128, 48, 32], bf)
 for _k in range(8):
     SCRATCH["P%d" % _k] = ("psum", [128, 512], f32)
 SEMAPHORES = ["v", "a", "pe", "p", "sent"] + ["d%d" % _k for _k in range(40)] + ["r%d" % _k for _k in range(18)]
-CY, WAKE, FLIGHT = 0.83, 60.0, 2600.0
-URGENCY = ['@(Z9<xhkvJE(jMOFbh[xpO*ocTq]E`B]j5Sxx5d(tW(s.gPi`(u=bFQ9LxJXnK,O\\KN6(x/MTMe3xwS:>>nL\\t[7s(o(:WGnvo5c<(q2e;([=W3Cx`(x+(rl*+os;^x*_xK=8=I((\\fFQKiS(x)PH52<lTN:(+g(4/D-M,7U-(vT4jjet?xsSQR(C1X+kuponnGx4d^e-IxWV3d(XL(uvN<(xxg:N(f?Mu8a_>:)T5BY(,S.hFeH-txQ47iGH.2AHjU(X2G+-<;rk3@2>,ONp^B1+rK^Ya@IFg6v0(f7xbN+JV]H071g]j=']
+CY, WAKE, FLIGHT = 0.83, 150.0, 2100.0
+GATH, SCAT = 1.56, 3.8
+OPT = {"pick_e": True, "pick_c": True, "mch": ((0, 4, "a"), (4, 8, "a"), (8, 12, "v")), "ach": ((0, 4, "a"), (4, 8, "a"), (8, 12, "a")),
+       "mch0": ((0, 4, "a"), (4, 8, "v"), (8, 12, "v")),
+       "ach0": ((0, 4, "a"), (4, 8, "a"), (8, 12, "a")), "val": 0, "tries": 12000, "heat": 200, "seed": 2}
 PLAN = {}
-FDF, FZS, FCB = True, True, False
-CHUNKS = ((0, 4), (4, 8), (8, 11), (11, 12))
-AUXV0, AUXV = (4, 5), ()
 
 
 def needs(ops):
@@ -50,7 +54,8 @@ def needs(ops):
                     e2 = ops[m]["e"]
                     if name[0] == "P" and name[1:].isdigit():
                         if e2 == e == "pe":
-                            f.add(m)
+                            if not (o["mid"] and ops[m]["mid"]):
+                                f.add(m)
                         elif e2 != e or ((w or w2) and lo < h2 and l2 < hi):
                             d.add(m)
                     elif (w or w2) and lo < h2 and l2 < hi and (pk is None or p2 is None or pk == p2):
@@ -58,7 +63,7 @@ def needs(ops):
         for w, accs in ((0, o["r"]), (1, o["w"])):
             for (name, lo, hi, pk) in accs:
                 old = seen.get(name, [])
-                if w and pk is None:
+                if w and pk is None and not o["mid"]:
                     old = [x for x in old if not (lo <= x[0] and x[1] <= hi)]
                 seen[name] = old + [(lo, hi, pk, w, n)]
         deps.append(d)
@@ -67,73 +72,111 @@ def needs(ops):
 
 
 def place(ops, pred, prio):
-    start, busy, end = [0.0] * len(ops), {}, 0.0
+    start, end = [0.0] * len(ops), 0.0
+    busy = {q: ([], []) for q in ("v", "a", "pe", "p", "sp", "x")}
     for i in prio:
         q, c, l = ops[i]
         s = 0.0
         for m, d in pred[i]:
-            if start[m] + d > s:
-                s = start[m] + d
-        line = busy.setdefault(q, [])
-        lo, hi = 0, len(line)
-        while lo < hi:
-            mid = (lo + hi) // 2
-            if line[mid][1] <= s:
-                lo = mid + 1
-            else:
-                hi = mid
-        while lo < len(line) and line[lo][0] < s + c:
-            s = max(s, line[lo][1])
-            lo += 1
-        line.insert(lo, (s, s + c))
+            d += start[m]
+            if d > s:
+                s = d
+        if c:
+            on, off = busy[q]
+            lo = hi = len(on)
+            if hi and off[-1] > s:
+                lo = 0
+                while lo < hi:
+                    mid = (lo + hi) >> 1
+                    if off[mid] <= s:
+                        lo = mid + 1
+                    else:
+                        hi = mid
+                hi = len(on)
+                while lo < hi and on[lo] < s + c:
+                    s = off[lo]
+                    lo += 1
+            on.insert(lo, s)
+            off.insert(lo, s + c)
         start[i] = s
         if s + c + l > end:
             end = s + c + l
     return start, end
 
 
-def chains(succ, short):
-    rest = [0.0] * len(short)
-    for i in range(len(short) - 1, -1, -1):
-        rest[i] = max([rest[j] for j in succ[i]] + [0.0]) + short[i][1] + short[i][2] + WAKE
-    return rest
-
-
-def ranked(pred, succ, rest, kind, urge):
-    key = [rest[i] + 100.0 * urge[kind[i]] for i in range(len(rest))]
-    for i in range(len(rest) - 1, -1, -1):
+def ranked(succ, due, kind, shift):
+    key = [due[i] + shift[kind[i]] for i in range(len(due))]
+    for i in range(len(due) - 1, -1, -1):
+        k = key[i]
         for j in succ[i]:
-            if key[j] >= key[i]:
-                key[i] = key[j] + 0.01
-    return sorted(range(len(rest)), key=lambda i: -key[i])
+            if key[j] <= k:
+                k = key[j] - 0.01
+        key[i] = k
+    return sorted(range(len(due)), key=lambda i: key[i])
+
+
+def blocked(ops, pred, start):
+    ends = {(ops[i][0], round(start[i] + ops[i][1])): i for i in range(len(ops)) if ops[i][1]}
+    i, pairs = max(range(len(ops)), key=lambda i: start[i] + ops[i][1] + ops[i][2]), []
+    while start[i] > 1.0:
+        m, ready = max([(m, start[m] + d) for m, d in pred[i]] + [(None, 0.0)], key=lambda x: x[1])
+        if ready < start[i] - 0.5:
+            m = ends.get((ops[i][0], round(start[i])))
+            if m is None or m == i:
+                break
+            pairs.append((m, i))
+        i = m
+    return pairs
 
 
 def order(ops, deps, after):
-    pred, succ, short, kind, nk = graph(ops, deps, after)
-    urge = [ord(c) - 80 for c in URGENCY[0]] if len(URGENCY[0]) == nk else [0] * nk
-    start = place(short, pred, ranked(pred, succ, chains(succ, short), kind, urge))[0]
-    return sorted(range(len(ops)), key=lambda i: start[i])
-
-
-def graph(ops, deps, after):
     n = len(ops)
-    pred, succ = [[] for _ in ops], [[] for _ in ops]
+    pred, succ, behind = [[] for _ in ops], [[] for _ in ops], []
     for i in range(n):
-        for m in deps[i] | after[i]:
-            pred[i].append((m, ops[m]["c"] + ops[m]["l"] + (WAKE if m in deps[i] else 0.0) + 0.001))
-            succ[m].append(i)
+        near = deps[i] | after[i]
+        far = 0
+        for m in near:
+            far |= behind[m]
+        behind.append(far | sum(1 << m for m in near))
+        for m in near:
+            if not far >> m & 1 or ops[m]["l"]:
+                pred[i].append((m, ops[m]["c"] + ops[m]["l"] + (WAKE if m in deps[i] else 0.0) + 0.001))
+                succ[m].append(i)
     short = [(o["q"], o["c"], o["l"]) for o in ops]
     kinds = sorted(set(o["kind"] for o in ops))
     kind = [kinds.index(o["kind"]) for o in ops]
-    return pred, succ, short, kind, len(kinds)
+    due = [o["due"] for o in ops]
+    shift, seed = [0.0] * len(kinds), OPT["seed"]
+    start, end = place(short, pred, ranked(succ, due, kind, shift))
+    best, pairs = (end, start), blocked(short, pred, start)
+    for r in range(OPT["tries"]):
+        trial = list(shift)
+        seed = (seed * 1103515245 + 12345) % 2 ** 31
+        if r % 2 and pairs:
+            x, y = pairs[(seed >> 8) % len(pairs)]
+            gap = max(due[y] + shift[kind[y]] - due[x] - shift[kind[x]], 0.0) + 20.0 + (seed >> 4) % 200
+            if seed >> 20 & 1:
+                trial[kind[x]] += gap
+            else:
+                trial[kind[y]] -= gap
+        else:
+            trial[(seed >> 8) % len(kinds)] += ((seed >> 3) % 31 - 15) * (20.0, 60.0, 200.0)[(seed >> 20) % 3]
+        s2, e2 = place(short, pred, ranked(succ, due, kind, trial))
+        if e2 <= end + OPT["heat"] * (1 - r / OPT["tries"]):
+            shift, start, end = trial, s2, e2
+            pairs = blocked(short, pred, start)
+            if end < best[0]:
+                best = (end, start)
+    PLAN["end"] = best[0]
+    return sorted(range(n), key=lambda i: best[1][i])
 
 
 def schedule(g, T, ops):
     queue = {"v": g.vector, "a": g.scalar, "pe": g.tensor, "p": g, "sp": g.sync}
-    deps, after = needs(ops)
     if "seq" not in PLAN:
-        PLAN["seq"] = order(ops, deps, after)
-    seq = PLAN["seq"]
+        PLAN["deps"], after = needs(ops)
+        PLAN["seq"] = order(ops, PLAN["deps"], after)
+    seq, deps = PLAN["seq"], PLAN["deps"]
     at = {m: n for n, m in enumerate(seq)}
     known, clock, waits, marked = {e: {} for e in queue}, {}, {}, set()
     for i in seq:
@@ -181,8 +224,11 @@ def rank_program(g, core, T, topo):
     rank = T.rank_of(core)
     if rank is None:
         return
-    ops, sends, step = [], {}, [-1, {}]
+    ops, sends, step, now = [], {}, [-1, {}], [0.0]
     V, S, PE = g.vector, g.scalar, g.tensor
+
+    def at(t, x):
+        now[0] = 12000.0 + 12500.0 * t + 1000.0 * x
 
     def v(name, lo, hi, st=1):
         return (T[name][:, lo:hi:st] if st > 1 else T[name][:, lo:hi], [(name, lo, hi, None)], [], (hi - lo + st - 1) // st, False)
@@ -193,7 +239,7 @@ def rank_program(g, core, T, topo):
     def ind(win, off):
         return (win[0].indirect(off[0]), win[1], off[1], 16 * off[3], True)
 
-    def op(e, f, outs, ins, c, k="c", lat=0.0, after=()):
+    def op(e, f, outs, ins, c, k="c", lat=0.0, after=(), mid=False):
         r, w = [], []
         for x in ins:
             if isinstance(x, tuple):
@@ -201,16 +247,17 @@ def rank_program(g, core, T, topo):
         for x in outs:
             w += x[1]
             r += x[2]
-        key = (step[0] < 0, e, k, w[0][0] if w else r[0][0])
+        key = (step[0] if step[0] in (-1, 0, STEPS - 1) else 1, e, k, w[0][0] if w else r[0][0])
         step[1][key] = step[1].get(key, 0) + 1
-        ops.append({"kind": key + (step[1][key],), "e": e, "q": "x" if k == "x" else e, "f": f, "r": r, "w": w, "k": k, "c": c, "l": lat, "after": after})
+        now[0] += 10.0
+        ops.append({"mid": mid, "due": now[0], "kind": key + (step[1][key],), "e": e, "q": "x" if k == "x" else e, "f": f, "r": r, "w": w, "k": k, "c": c, "l": lat, "after": after})
 
     def cost(o, x, f=1.0):
         n = max(o[3], x[3])
         if o[4]:
-            return 50 + 3.8 * CY * n
+            return 50 + SCAT * CY * n
         if x[4]:
-            return 50 + 1.56 * CY * n
+            return 55 + GATH * CY * n
         if f == 1.0 and all(SCRATCH[y[1][0][0]][2] in (bf, u16) for y in (o, x)):
             f = 0.5
         return 30 + CY * max(64, f * n)
@@ -234,12 +281,13 @@ def rank_program(g, core, T, topo):
     def ms(o, c):
         op("v", lambda: V.memset(o[0], c), [o], [], cost(o, o))
 
-    def scan(o, d0, d1, f):
-        op("v", lambda: V.tensor_tensor_scan(o[0], d0[0], d1[0], 0.0, Op.add, f), [o], [d0, d1], cost(o, d0))
+    def scan(o, d0, d1, f, f0=Op.add):
+        fast = all(SCRATCH[y[1][0][0]][2] == bf for y in (o, d0, d1))
+        op("v", lambda: V.tensor_tensor_scan(o[0], d0[0], d1[0], 0.0, f0, f), [o], [d0, d1], cost(o, d0, 1.0 if fast else 1.01))
 
-    def act(o, x, f=AF.Copy, bias=0.0, scale=1.0):
-        if f == AF.Copy:
-            op("a", lambda: S.activation(o[0], x[0], f), [o], [x], cost(o, x, 1.01))
+    def act(o, x, f=AF.Copy, bias=0.0, scale=1.0, first=0.0):
+        if f in (AF.Copy, AF.Silu):
+            op("a", lambda: S.activation(o[0], x[0], f), [o], [x], cost(o, x, 1.01) + first)
         else:
             op("a", lambda: S.activation(o[0], x[0], f, bias=a_(bias), scale=a_(scale)), [o], [x, bias, scale], cost(o, x, 1.01))
 
@@ -252,16 +300,16 @@ def rank_program(g, core, T, topo):
         else:
             op("p", lambda: g.iota(o[0], pattern, base, cm, allow_small_or_imprecise_dtypes=True), [o], [], 130 + 2 * CY * o[3])
 
-    def sel(o, x, pattern, f, fill, cm=0):
-        op("p", lambda: g.affine_select(o[0], x[0], pattern, f, fill, 0, cm), [o], [x], 170 + 2 * CY * o[3])
+    def sel(o, x, pattern, f, fill, cm=0, base=0):
+        op("p", lambda: g.affine_select(o[0], x[0], pattern, f, fill, base, cm), [o], [x], 170 + 2 * CY * o[3])
 
-    def mm(items, start, stop):
+    def mm(items, start=True, stop=True):
         def f():
             for n, (o, l, r) in enumerate(items):
                 ins = PE.matmul(o[0], l[0], r[0], start and n == 0, stop and n == len(items) - 1)
             return ins
-        c = sum(0.42 * max(64, r[3]) * (4 if SCRATCH[l[1][0][0]][2] == f32 else 1) for o, l, r in items)
-        op("pe", f, [x[0] for x in items], [x[1] for x in items] + [x[2] for x in items], c)
+        c = sum(0.42 * max(min(64, l[3]), r[3]) * (4 if SCRATCH[l[1][0][0]][2] == f32 else 1) for o, l, r in items)
+        op("pe", f, [x[0] for x in items], [x[1] for x in items] + [x[2] for x in items], c, mid=not (start or stop))
 
     def diag(o, L, name, lo, hi):
         return [(o, v(L, 15 - q, 143 - q), v(name, lo + q, hi, 16)) for q in range(16)]
@@ -277,33 +325,40 @@ def rank_program(g, core, T, topo):
         def f():
             g.remote_dma(dst[0], src[0], T.sem["r%d" % (3 * t + j)], T.sem["sent"], pid, rid, topo.mask(core, to))
             return len(topo.engines(core, to))
+        first = not sends
         sends[t, j] = len(ops)
-        op("p", f, [], [src], 500.0, "s")
+        op("p", f, [], [src], 2500.0 if first else 500.0, "s")
 
     def arrive(t, j, dst):
         frm = T.cores[(rank - 1 - t % (N - 1)) % N]
-        op("sp", (T.sem["r%d" % (3 * t + j)], len(topo.engines(frm, core))), [dst], [], 0.0, "x", FLIGHT, (sends[t, j],))
+        op("sp", (T.sem["r%d" % (3 * t + j)], len(topo.engines(frm, core))), [dst], [], 0.0, "x", FLIGHT + (0, -100, 600)[j] + 500 * (j != 1), (sends[t, j],))
 
     def col(j):
         return v("CO", j, j + 1)
 
-    def w(j, n=12):
-        return v("W", 16 * j, 16 * j + n)
-
-    def wi(j, n=1):
-        return v("WI", 12 * j, 12 * (j + n))
-
-    def wu(j, n=12):
-        return v("WU", 16 * j, 16 * j + n)
-
     def cl(j, n=12):
         return v("CL", 16 * j, 16 * j + n)
 
-    def ch(j):
-        return v("CH", 12 * j, 12 * j + 12)
+    def ch(j, n=12):
+        return v("CH", 12 * j, 12 * j + n)
 
     def zr(b, lo, hi):
-        return raw(T["ZR%d" % b][:, :, lo:hi], "ZR%d" % b, n=12 * (hi - lo))
+        return raw(T["ZR%d" % b][:, :, lo:hi], "ZR%d" % b, lo, hi, n=6 * (hi - lo))
+
+    def zs(n, lo=0, hi=32):
+        return raw(T.Z[:, 6 * n:6 * n + 6, lo:hi], "Z", n, n + 1, n=6 * (hi - lo))
+
+    def spread(n, copy):
+        for o in (0, 256):
+            copy(zr(n % 2, o, o + 16), zs(n, o // 16, o // 16 + 16))
+            for s in (16, 32, 64, 128):
+                if n == 1 and s == 128:
+                    dma("sp", zr(n % 2, o + s, o + 2 * s), zr(n % 2, o, o + s), 480)
+                else:
+                    copy(zr(n % 2, o + s, o + 2 * s), zr(n % 2, o, o + s))
+
+    def pool_copy(o, x):
+        sel(o, x, [[0, o[3]]], ge, 0.0)
 
     def rows(name, r):
         return raw(T[name][r::16, 0:2048], name, 0, 2048, r)
@@ -311,330 +366,372 @@ def rank_program(g, core, T, topo):
     def hbm(name):
         return raw(T[name][:], name)
 
-    add, sub, mul, mx, mn = Op.add, Op.subtract, Op.mult, Op.max, Op.min
-    eq, ne, ge, lt, band = Op.is_equal, Op.not_equal, Op.is_ge, Op.is_lt, Op.bitwise_and
-    x12, x128, x144, x192 = v("XF", 0, 12), v("XF", 0, 128), v("XF", 0, 144), v("XF", 0, 192)
-    xg, xq = v("XG", 0, 192), v("XQ", 0, 192)
-    cN, cG15, cP, cG, cNE, cK0, cK1 = 0, 1, 2, 3, 5, 6, 7
-    cW01, cWE, cWH, cN1, cA15, cW0, cW1, cW2, cW3, cW4, cW5 = 8, 10, 12, 14, 15, 16, 17, 18, 19, 20, 21
-    c192, c128, c12, c24, cW35, cW416, cBO, cN14, cT, cXW, cNN, cVI, cK, cA30 = range(22, 36)
-    IL, VID, DUM, EXI, C2, CT, CA2 = range(7)
-    WA, HA, HN = 0, 2, 3
+    def full(name, n=128):
+        return v(name, 0, n)
 
+    add, sub, mul, mx, mn = Op.add, Op.subtract, Op.mult, Op.max, Op.min
+    eq, ne, ge, band = Op.is_equal, Op.not_equal, Op.is_ge, Op.bitwise_and
+    x12, x144, x192 = v("XF", 0, 12), v("XF", 0, 144), v("XF", 0, 192)
+    xg, xq, one = v("XG", 0, 192), v("XQ", 0, 192), v("ONE", 0, 192)
+    i1, ib, i2b, n2b, ig, iw, nw = full("I1"), full("IB"), full("ID"), full("ND"), full("IG"), full("IW"), full("NW")
+    (cN, cG, cN14, cNN, c12, cK0, cK1, cW01, _x, cWE, _y, cWH, _z, cW0, cW1, cW2, cW3, cW4, cW5, cW6, cP, cX) = range(22)
+    spare = [cX]
+
+    def scaled(j, scale, bias=0.0):
+        spare[0] += 1
+        lin(col(spare[0]), col(j), scale, bias)
+        return col(spare[0])
+    IL, VID, C2, CT = range(4)
+    WA, HA, CC, CN = 0, 2, 3, 5
+
+    at(0, -12.0)
     dma("sp", v("OW", 0, 256), hbm("own"), 128)
-    dma("a", v("O0", 0, 128), raw(T.own[0:8, :], "own"), 64)
+    dma("a", raw(T.Z[:, 0:12], "Z", 0, 2), hbm("st"), 96)
     dma("sp", v("EI", 0, 384), hbm("ends"), 192)
-    dma("a", v("Z0", 0, 384), hbm("st"), 96)
-    dma("sp", v("M", 0, 2048), hbm("msg"), 512)
-    dma("a", v("EN", 0, 128), hbm("enc"), 64)
-    io(v("TH", 0, 384), [[0, 384]], 0)
-    dma("sp", raw(T.TH[0::16, :], "TH"), hbm("th"))
+    dma("a", v("M", 0, 2048), hbm("msg"), 512)
+    dma("sp", v("EN", 0, 128), hbm("enc"), 64)
+    dma("a", raw(T.TH[0:8, :], "TH"), hbm("th"))
+    ms(v("A", 0, 2240), 0.0)
     io(v("PI", 0, 1), [[0, 1]], 0, 1)
     io(col(cP), [[0, 1]], 0, 1)
     io(x192, [[1, 192]], 0)
-    io(v("XG", 0, 384), [[16, 24], [0, 16]], 0)
-    io(xq, [[0, 12], [1, 16]], 0)
-    io(v("SR", 128, 256), [[0, 8], [1, 16]], 0)
-    io(v("K", 0, 2048), [[0, 2048]], 0)
-    io(v("C15", 0, 192), [[16, 12], [0, 16]], 15)
-    io(v("CAW", 0, 192), [[16, 12], [0, 16]], 15 + int(OFF))
-    io(v("X", 3072, BS), [[0, 192]], 0)
-    io(v("LW", 0, 592), [[0, 592]], 4000)
-    io(v("SIG", 0, 1), [[0, 1]], 0)
-    io(cl(CT), [[2, 12]], int(BIG) - 128)
-    io(v("CH", 48, 72), [[0, 2], [1, 12]], -64)
-    io(cl(C2), [[32, 12]], 30 + int(BIG))
-    io(v("CH", 0, 24), [[-384, 2], [-16, 12]], 576)
-    io(ch(HA), [[-256, 12]], 0)
-    io(v("ONE", 0, 192), [[0, 192]], 1)
-    one = v("ONE", 0, 192)
-    sel(v("I1", 0, 128), v("ONE", 0, 128), [[-1, 128]], eq, 0.0, 1)
-    sel(v("CM", 0, 192), one, [[0, 12], [1, 16]], ne, -BIG)
-    lin(v("CF", 0, 192), v("CM", 0, 192), -1.0)
-    lin(v("TWO", 0, 192), one, 2.0)
-    lin(v("HALF", 0, 192), one, -0.5)
-    ms(v("A", 0, 2240), 0.0)
     ts(v("PI", 1, 2), v("PI", 0, 1), 15, band)
-    ts(v("PI", 2, 3), v("PI", 0, 1), 0x70, band)
-    ts(v("PI", 3, 4), v("PI", 0, 1), 14, band)
     cp(col(cN), v("PI", 1, 2))
-    cp(col(cG), v("PI", 2, 3))
-    cp(col(cN14), v("PI", 3, 4))
-    lin(col(c128), col(cN), 128.0)
-    lin(col(c12), col(cN), 12.0)
-    lin(col(cG15), col(cG), 1.0, 15.0)
-    lin(col(c192), col(cN), -1.0, 192.0)
-    lin(col(cNN), col(cN), -1.0)
-    lin(col(cVI), col(cN), 2.0, 192.0)
-    ts(v("CO", 8, 14), v("XF", 0, 6), col(cN14), eq)
-    ts(v("CO", 16, 22), v("XF", 0, 6), col(cN), eq)
-    ts(col(cA15), col(cN), 15.0, ne, FAR, mul)
-    lin(col(cNE), col(cWE), -1.0)
-    lin(col(c24), col(cW2), 2048.0)
-    lin(col(cW35), col(cW3), 1.0, col(cW5))
-    lin(col(cW416), col(cW4), 16.0)
-    lin(col(cXW), col(cW416), 1.0, col(cW2))
-    lin(col(cK1), col(cW1), -1.0, 1.0)
-    lin(col(cK), col(cW0), -1.0, 1.0)
-    lin(col(cK0), col(cWH), -1.0, col(cK))
-    lin(col(cT), col(cG), 0.5, 7.0)
-    lin(col(cBO), col(cN), 64.0, col(cT))
-    ts(v("LB", 0, 144), x144, col(cG15), eq)
-    for name, c in (("L0", col(cW0)), ("L1", col(cW1)), ("LE", col(cWE)), ("LN", col(cNE)), ("LP", col(cW01)), ("LH", col(cWH)), ("LD", 128.0)):
-        lin(v(name, 0, 144), v("LB", 0, 144), c)
-    lin(v("LF", 0, 144), v("L0", 0, 144), 256.0)
-    ts(v("BO", 0, 144), x144, col(cBO), eq, col(cW01), mul)
-    ib, nb, i1 = v("IB", 0, 128), v("NB", 0, 128), v("I1", 0, 128)
-    lin(ib, i1, B)
-    lin(nb, i1, -B)
-    ts(v("ON", 0, 128), v("XG", 0, 128), col(cG), eq)
-    lin(v("BC", 0, 128), v("ON", 0, 128), col(cWE))
-    lin(v("OK", 0, 128), v("ON", 0, 128), 4096.0)
-    sel(v("TR", 0, 128), v("OK", 0, 128), [[1, 128]], Op.is_gt, 0.0, -1)
-    lin(v("NV", 0, 384), v("XG", 0, 384), -1.0, col(c192))
-    lin(cl(IL), x12, 16.0, col(cN))
-    lin(cl(VID), x12, 16.0, col(cVI))
-    lin(cl(DUM), cl(IL), 1.0, 2048.0)
-    lin(cl(EXI), cl(IL), 1.0, float(EXT))
-    lin(ch(HN), x12, 0.0, col(cNN))
-    cp(v("CU", 24, 36), x12)
-    ts(v("CU", 0, 12), x12, col(c12), add)
-    ts(v("CU", 12, 24), x12, col(c12), add, 192.0, add)
-    ts(w(30), cl(IL), -5.5, add, 1.0 / 12, mul)
-    cp(wi(9), w(30))
-    lin(w(31), cl(IL), 16.0)
-    ts(w(30), wi(9), -191.0, mul)
-    tt(w(30), w(30), w(31), add)
-    cp(v("CU", 36, 48), w(30))
-    lin(v("T4", 0, 8), v("XF", 0, 8), 96.0)
-    io(v("T2", 0, 1), [[0, 1]], 0)
-    ts(v("T2", 1, 193), xq, col(cN), eq)
-    mm([(v("P6", 0, 192), ib, v("T2", 1, 193)), (v("P6", 0, 192), nb, v("T2", 0, 192))], True, True)
-    act(v("T5", 0, 192), v("P6", 0, 192))
-    sel(v("DS", 0, 192), v("T5", 0, 192), [[0, 12], [1, 16]], ne, 4 * FAR)
-    lin(col(cA30), col(cA15), 2.0)
-    io(v("ABX", 3072, BS), [[0, 192]], 0)
-    lin(v("VR", 192, 384), x192, col(cW1))
-    lin(col(cN1), col(cW0), -192.0)
-    lin(v("T3", 0, 192), x192, col(cW0), col(cN1))
-    lin(v("T3", 192, 384), xg, col(cW416))
-    lin(v("T3", 384, 576), xq, col(cW5))
-    mm([(v("P4", 0, 192), i1, v("T3", 192 * j, 192 * j + 192)) for j in range(3)], True, True)
-    act(v("VR", 0, 192), v("P4", 0, 192))
-    lin(v("T1", 0, 192), xg, col(cXW), col(c24))
-    lin(v("T1", 192, 384), xq, col(cW35))
-    mm([(v("P5", 0, 192), i1, v("T1", 192 * j, 192 * j + 192)) for j in range(2)], True, True)
-    for o in (v("AX", 3072, BS), v("AX", BS + 3072, 2 * BS), v("K", 2048, 2240)):
-        act(o, v("P5", 0, 192))
-    lin(v("SR", 0, 128), v("XG", 0, 128), 1.0, col(c128))
+    lin(v("SR", 128, 256), v("XF", 0, 128), 1.0, 128.0)
+    lin(v("SR", 0, 128), v("XF", 0, 128), 0.0, scaled(cN, 128.0, 128.0))
     dma("sp", rows("A", 2), v("SR", 0, 128))
     dma("sp", rows("A", 3), v("SR", 128, 256))
     ts(v("OB", 0, 256), v("OW", 0, 256), -192.0, add)
     dma("sp", rows("A", 0), raw(T.OB[0:64, :], "OB"))
     dma("sp", rows("A", 1), raw(T.OB[64:128, :], "OB"))
-    ts(v("S1", 0, 128), v("O0", 0, 128), 0x1F0, band)
-    ts(v("S1", 128, 256), v("O0", 0, 128), 15, band)
-    ts(v("S2", 0, 128), v("O0", 0, 128), 192.0, ge, float(BS - 3072), mul)
-    ts(v("S2", 128, 256), v("S1", 0, 128), 16.0, mul)
-    cp(v("SR", 384, 512), v("S1", 128, 256))
-    tt(v("SR", 256, 384), v("S2", 0, 128), v("S2", 128, 256), add)
-    dma("sp", rows("A", 5), v("SR", 384, 512))
-    dma("sp", rows("A", 4), v("SR", 256, 384))
-    ts(v("S3", 0, 128), v("EN", 0, 128), 0x7F0, band)
-    ts(v("S3", 128, 256), v("EN", 0, 128), 15, band)
-    cp(v("SR", 512, 768), v("S3", 0, 256))
-    dma("sp", rows("K", 2), v("SR", 512, 640))
-    dma("sp", rows("K", 3), v("SR", 640, 768))
+    lin(v("OH", 0, 256), v("OB", 0, 256), 1.0, 3256.5)
+    dma("a", rows("A", 4), raw(T.OH[0:64, 0:256], "OH", 0, 256))
+    ts(v("OH", 256, 512), v("OB", 0, 256), 0.0, ge)
+    dma("sp", rows("A", 5), raw(T.OH[0:64, 256:512], "OH", 256, 512))
+    lin(col(c12), col(cN), 12.0)
+    ts(v("CU", 0, 12), x12, col(c12), add)
     cp(v("G", 0, 192), ind(v("EI", 0, 384), v("CU", 0, 12)))
-    cp(v("G", 192, 384), ind(v("EI", 0, 384), v("CU", 12, 24)))
-    cp(v("THF", 0, 384), v("TH", 0, 384))
-    mm(diag(v("P7", 0, 24), "LF", "THF", 0, 384), True, True)
+    spread(0, cp)
+    at(STEPS, 0.0)
+    io(xg, [[16, 12], [0, 16]], 0)
+    io(v("XQ", 0, 288), [[0, 18], [1, 16]], 0)
+    lin(v("ONE", 0, 288), v("XQ", 0, 288), 0.0, 1.0)
+    ts(i1, v("XF", 0, 128), col(cP), eq)
+    lin(col(cNN), col(cN), -1.0)
+    lin(col(cG), col(cP), 1.0, col(cNN))
+    ts(v("PI", 3, 4), v("PI", 0, 1), 14, band)
+    cp(col(cN14), v("PI", 3, 4))
+    ts(v("CO", cW01, cW01 + 6), v("XF", 0, 6), col(cN14), eq)
+    ts(v("CO", cW0, cW0 + 7), v("XF", 0, 7), col(cN), eq)
+    ts(v("LB", 0, 144), x144, -15.0, add, col(cG), eq)
+    for name, c in (("L0", col(cW0)), ("L1", col(cW1)), ("LD", 256.0), ("LR", 512.0), ("LX", -256.0), ("LE", col(cWE)), ("LP", col(cW01))):
+        lin(v(name, 0, 144), v("LB", 0, 144), c)
+    for name, c in (("ID", 2 * B), ("IB", B), ("ND", -2 * B), ("IF", 1.0), ("NF", -1.0)):
+        lin(full(name), i1, c)
+    for name, c in (("IG", GROW / 2), ("IW", 0.75 * B), ("NW", -0.75 * B), ("I2", 2.0), ("IO", DROP / 2)):
+        ts(full(name), i1, c, mul)
+    lin(v("NV", 0, 192), xg, -1.0, scaled(cN, -1.0, 192.0))
+    lin(v("NV", 192, 384), xg, -1.0, col(cNN))
+    io(v("X", 3264, BS), [[0, 192]], 0)
+    sel(v("RN", 0, 192), v("X", 3264, BS), [[0, 12], [1, 16]], ne, -BIG)
+    lin(v("RS", 0, 192), v("RN", 0, 192), -1.0)
+    lin(v("CM", 0, 192), v("RN", 0, 192), 1.0, 2.0)
+    io(cl(CT), [[1, 12]], 2 ** 22 - 64)
+    thf = raw(T.THF[0:8, :], "THF", n=384)
+    cp(thf, raw(T.TH[0:8, :], "TH", n=384))
+    ts(v("LF", 0, 144), x144, scaled(cP, 16.0, 15.0), eq, 256.0, mul)
+    mm([(v("P7", 0, 24), raw(T.LF[0:8, 15 - q:143 - q], "LF", n=128), raw(T.THF[0:8, q::16], "THF", n=24)) for q in range(16)])
     tt(v("TT", 0, 12), v("P7", 0, 12), cl(CT), add)
     tt(v("TT", 12, 24), v("P7", 12, 24), cl(CT), add)
-    act(v("T0", 0, 24), v("TT", 0, 24))
-    cp(zr(0, 0, 16), v("Z0", 0, 192))
-    for s in (16, 32, 64, 128):
-        cp(zr(0, s, 2 * s), zr(0, 0, s))
-
-    def spread(b, z):
-        sel(zr(b, 0, 16), z, [[0, 192]], ge, 0.0)
-        for s in (16, 32, 64, 128):
-            sel(zr(b, s, 2 * s), zr(b, 0, s), [[0, 12 * s]], ge, 0.0)
-    spread(1, v("Z0", 192, 384))
-
-    THR, BASE, TD, OFFS, HINT, FE, CLI, DUP, PM, NFA = range(10)
-    U15, THS, J3, F3, S3, CLA = 10, 12, 14, 17, 20, 23
-
-    def w3(s, j):
-        return v("W", 16 * s + 12 * j, 16 * s + 12 * j + 12)
-    iM, iS, iJ, iF, cM, cS, cJ, cF = range(8)
-    JF, WX, EFU, CO_, VU, PU, JM = range(7)
-    CU_ = 8
+    ts(v("T1", 0, 192), xg, 2176.0, add, col(cW2), mul)
+    ts(v("T1", 192, 384), xq, 128.0, add, col(cW3), mul)
+    mm([(v("P5", 0, 192), i1, v("T1", 192 * j, 192 * j + 192)) for j in range(2)])
+    lin(v("T2", 0, 192), xg, scaled(cW6, 16.0), scaled(cW5, 129.0))
+    lin(v("T2", 192, 384), xq, col(cW0))
+    mm([(v("P5", 192, 384), i1, v("T2", 192 * j, 192 * j + 192)) for j in range(2)])
+    act(v("AX", 3072, BS), v("P5", 0, 384))
+    dma("sp", v("AX", BS + 3072, 2 * BS), v("AX", 3072, BS), 96)
+    act(v("K", 2048, 2240), v("P5", 0, 192))
+    at(0, -3.0)
+    io(v("K", 0, 2048), [[0, 2048]], 0)
+    ts(v("SK", 0, 128), v("EN", 0, 128), 16 * ROUND + 128, add, -16 * ROUND, add)
+    tt(v("SK", 128, 256), v("EN", 0, 128), v("SK", 0, 128), sub)
+    lin(v("SK", 128, 256), v("SK", 128, 256), 1.0, LIFT)
+    dma("sp", rows("K", 2), v("SK", 0, 128))
+    dma("sp", rows("K", 3), v("SK", 128, 256))
+    at(STEPS, 0.0)
+    io(v("LW", 0, 192), [[0, 192]], 4000)
+    io(v("LW", 384, 592), [[0, 208]], 4000)
+    io(v("CH", 0, 24), [[-384, 2], [-16, 12]], 576)
+    io(cl(C2), [[32, 12]], 15 * 2 ** 20 + 30)
+    io(ch(HA), [[-16, 12]], 0)
+    io(ch(CN), [[1, 12]], 204)
+    io(ch(CC, 24), [[2, 2], [0, 12]], 1)
+    io(cl(4, 18), [[2, 6], [0, 3]], 1)
+    io(v("CL", 64, 82, 3), [[2, 6]], 0)
+    ts(full("ON"), v("XG", 0, 128), col(cG), eq)
+    lin(full("BC"), full("ON"), col(cWE))
+    lin(cl(VID), x12, 16.0, scaled(cN, 2.0, 192.0))
+    if OPT["pick_c"]:
+        ts(v("CU", 24, 42), cl(4, 18), 16.0, mul, 15.0, add)
+    else:
+        cp(v("CU", 24, 42), cl(4, 18))
+    ts(v("NM", 0, 192), xq, col(cN), ne, -FAR, mul)
+    ts(v("MK", 0, 288), v("XQ", 0, 288), col(cN), ge, 4096.0, mul)
+    sel(v("MK", 0, 288), v("MK", 0, 288), [[0, 6], [1, 3], [0, 16]], ne, 0.0, base=-1)
+    io(v("DD", 0, 288), [[0, 288]], 1)
+    c16 = scaled(cN, 16.0)
+    for j in range(2):
+        lin(v("DD", 16 * j, 288, 48), v("ONE", 0, 6), 0.0)
+        lin(v("DD", 15 + 32 * j, 288, 48), v("ONE", 0, 6), 2304.0 + 256 * j + LIFT, c16)
+    ts(v("LH", 0, 144), v("LB", 0, 144), scaled(cW5, 384.0, scaled(cW4, 15.0, scaled(cW0, 1.0, col(cW6)))), mul, 1.0 / 16, mul)
+    lin(col(cK1), col(cW1), -1.0, 1.0)
+    lin(col(cK0), col(cWH), -1.0, scaled(cW0, -1.0, 1.0))
+    lin(v("VR", 192, 384), x192, col(cW1))
+    ts(v("T3", 0, 192), x192, -192.0, add, col(cW0), mul)
+    ts(v("T3", 192, 384), xg, 3072.0, add, col(cW4), mul)
+    mm([(v("P4", 0, 192), i1, v("T3", 192 * j, 192 * j + 192)) for j in range(2)])
+    act(v("VR", 0, 192), v("P4", 0, 192))
+    ts(v("CU", 12, 24), x12, col(c12), add, 192.0, add)
+    cp(v("G", 192, 384), ind(v("EI", 0, 384), v("CU", 12, 24)))
+    at(0, 0.5)
+    spread(1, pool_copy)
+    at(STEPS, 0.0)
+    lin(cl(IL), x12, 16.0, col(cN))
+    ts(cl(6), cl(IL), -5.5, add, 1.0 / 12, mul)
+    cp(v("EI", 0, 12), cl(6))
+    lin(cl(7), cl(IL), 16.0)
+    ts(cl(6), v("EI", 0, 12), -191.0, mul)
+    tt(cl(6), cl(6), cl(7), add)
+    cp(v("CU", 48, 60), cl(6))
 
     def take(t, j, table, src):
         arrive(t, j, src)
-        cp(ind(v(table, 0, WIDE), v("OI", 16 * t, 16 * t + 12)), src)
+        to = ind(v(table, 0, WIDE), v("OI", 16 * t, 16 * t + 12))
+        if table == "K":
+            act(to, src, AF.Silu, first=1300.0 * (t == 0))
+        else:
+            cp(to, src)
 
+    def pick(P, src, out):
+        mm([(P, i1, v("NM", 0, 192))], True, False)
+        mm([(P, full("BC"), src)], False, True)
+        scan(v("SC", out, out + 192), v("RN", 0, 192), P, mx)
+        return v("SC", out + 15, out + 192, 16)
+
+    def relist(t):
+        b = t % 2
+        at(t, 4.55)
+        act(v("VAL", 0, 192), ind(v("AX", 0, EXT + 192), v("WU", 144 * t + 112, 144 * t + 124)))
+        at(t, 5.3)
+        cp(ind(v("AX", BS * b, BS * b + BS), v("WU", 144 * t + 128, 144 * t + 140)), v("VAL", 0, 192))
+        items = diag(v("P7", 0, 192), "LE", "AX", BS * b, BS * b + 3072)
+        at(t, 12.6)
+        for c in range(4):
+            mm(items[4 * c:4 * c + 4], c == 0, c == 3)
+        if t < STEPS - 2:
+            ts(v("G", 192 * b, 192 * b + 192), v("P7", 0, 192), -LIFT, add)
+        else:
+            lin(v("EF", 0, 192), v("P7", 0, 192), 1.0, -LIFT)
+            act(v("YE", 192 * b, 192 * b + 192), ind(v("EF", 0, 192), v("CU", 48, 60)))
+            dma("sp", raw(T.ye[:, 192 * b:192 * b + 192], "ye", b, b + 1), v("YE", 192 * b, 192 * b + 192), 96)
+
+    idle = []
     for t in range(STEPS):
         b = t % 2
         step[0], step[1] = t, {}
+
+        def w(j, n=12):
+            return v("W", 96 * t + 16 * j, 96 * t + 16 * j + n)
+
+        def wi(j, n=1):
+            return v("WI", 112 * t + 12 * j, 112 * t + 12 * (j + n))
+
+        def wu(j, n=12):
+            return v("WU", 144 * t + j, 144 * t + j + n)
+
+        def wb(j):
+            return v("WB", 64 * t + 16 * j, 64 * t + 16 * j + 12)
+        kF, cF, kM, kS, kJ, cM, cS, cJ, cU = range(9)
+        JF, JM, JS, WX, EFU, CU_, CO_, VU, PU = 0, 16, 28, 48, 64, 80, 96, 112, 128
+        sN, cFb, GE, TD = range(4)
         blk = v("AX", BS * b, BS * b + BS)
-        z = v("Z0", 192 * b, 192 * b + 192) if t < 2 else v("ZN", 192 * (t - 2), 192 * (t - 1))
-        zn = v("ZN", 192 * t, 192 * t + 192)
-        for c in range(3):
-            for e in (2 * c, 2 * c + 1):
-                (cp if e in (AUXV if t else AUXV0) else act)(v("AX", BS * b + 512 * e, BS * b + 512 * e + 512),
-                                                             ind(v("A", 0, 2240), v("G", 192 * b + 32 * e, 192 * b + 32 * e + 32)))
+        z, zn = zs(t), zs(t + 2)
+        pieces = OPT["ach"] if t else OPT["ach0"]
+        late = len(pieces) if t == 1 else OPT["val"]
+        for n, (lo, hi, e) in enumerate(pieces):
+            if t and n == late:
+                relist(t - 1)
+            at(t, -7.1 + 0.35 * lo)
+            (cp if e == "v" else act)(v("AX", BS * b + 256 * lo, BS * b + 256 * hi), ind(v("A", 0, 2240), v("G", 192 * b + 16 * lo, 192 * b + 16 * hi)))
             for P, L in (("P1", "L0"), ("P2", "L1")):
-                first = [(v(P, 0, 192), i1, v("NV", 192 * b, 192 * b + 192))] if c == 0 else []
-                mm(first + diag(v(P, 64 * c, 64 * c + 64), L, "AX", BS * b + 1024 * c, BS * b + 1024 * c + 1024), c == 0, c == 2)
-        if t == 1:
-            relist(0)
+                first = [(v(P, 0, 192), i1, v("NV", 192 * b, 192 * b + 192))] if lo == 0 else []
+                mm(first + diag(v(P, 16 * lo, 16 * hi), L, "AX", BS * b + 256 * lo, BS * b + 256 * hi), lo == 0, hi == 12)
+        if t and late == len(pieces):
+            relist(t - 1)
+        at(t, -2.1)
         act(v("SG", 0, 192), v("P1", 0, 192), AF.Sign)
+        at(t, -0.7)
         tt(v("Q", 0, 192), v("SG", 0, 192), v("P2", 0, 192), mul)
-        ts(v("SIG", 1, 193), v("Q", 0, 192), 0.0, ne)
-        s0, s1 = v("SIG", 0, 192), v("SIG", 1, 193)
-        for o, p, q, c in ((v("P3", 0, 192), ib, nb, "CF"), (v("P3", 192, 384), nb, ib, "CF"), (v("P5", 0, 192), nb, ib, "CM")):
-            mm([(o, i1, v(c, 0, 192)), (o, p, s0), (o, q, s1)], True, True)
-        ths = v("P4", 32, 56)
-        mm([(ths, ib, v("TWO", 0, 24)), (ths, i1, v("CH", 48, 72))] + [(v("P4", 32 + 12 * j, 44 + 12 * j), ib, v("SIG", 16, 193, 16)) for j in range(2)], True, True)
-        if FDF:
-            act(v("DF", 0, 192), v("P3", 0, 192))
-        tt(w(THR), v("TT", 12 * b, 12 * b + 12), v("P4", 32, 44), sub)
-        act(w(THS, 24), ths)
-        scan(v("SC", 192, 384), v("P3", 192, 384), v("CAW", 0, 192), mn)
+        s1 = v("SIG", 0, 192)
+        ts(s1, v("Q", 0, 192), 0.0, ne)
+        at(t, -0.1)
+        thr = v("P4", 0, 12)
+        mm([(thr, full("IF"), v("TT", 12 * b, 12 * b + 12))] + [(thr, ig, x) for s in idle[b::2] for x in (s, v("ONE", 0, 12))])
+        at(t, -8.0)
+        pool_copy(v("X", 3072, 3264), z)
         if t:
+            at(t, -6.2)
             arrive(t - 1, 1, v("OI", 16 * t - 16, 16 * t - 4))
             take(t - 1, 0, "M", v("ZI", 192 * t - 192, 192 * t))
+            at(t, -0.9)
             take(t - 1, 2, "K", v("EM", 192 * t - 192, 192 * t))
-        for a in range(12):
-            tt(v("X", 256 * a, 256 * a + 256), ind(v("M", 0, 2048), v("G", 192 * b + 16 * a, 192 * b + 16 * a + 16)),
-               raw(T["ZR%d" % b][:, a], "ZR%d" % b), sub)
-        for lo, hi in CHUNKS:
-            act(v("ABX", 256 * lo, 256 * hi), v("X", 256 * lo, 256 * hi), AF.Abs, scale=2.0)
-            first = [(v("P0", 0, 192), i1, v("C15", 0, 192)), (v("P0", 0, 192), ib, v("TWO", 0, 192))] if lo == 0 else []
-            mm(first + diag(v("P0", 16 * lo, 16 * hi), "LD", "ABX", 256 * lo, 256 * hi), lo == 0, hi == 12)
-        if FDF:
-            scan(v("SC", 384, 576), v("DF", 0, 192), v("P0", 0, 192), mn)
-        act(v("DC", 0, 192), v("P0", 0, 192))
-        if not FDF:
-            scan(v("SC", 384, 576), v("P3", 0, 192), v("DC", 0, 192), mn)
-        tt(wi(iF), v("SC", 399, 576, 16), w(THR), mn)
-        ts(wi(cF), wi(iF), 255, band)
+        key = v("P0", 0, 192)
+        mm([(key, i1, x192), (key, i2b, one)], True, False)
+        for lo, hi, e in OPT["mch" if t else "mch0"]:
+            x, ab, o = v("X", 256 * lo, 256 * hi), v("ABX", 256 * lo, 256 * hi), v("P0", 16 * lo, 16 * hi)
+            at(t, -5.5 + 0.35 * lo)
+            for c in range(lo // 2, hi // 2):
+                tt(v("X", 512 * c, 512 * c + 512), ind(v("M", 0, 2048), v("G", 192 * b + 32 * c, 192 * b + 32 * c + 32)), raw(T["ZR%d" % b][:, c], "ZR%d" % b, 0, 512, n=512), sub)
+            at(t, -2.9 + 0.22 * lo)
+            if e == "a":
+                act(ab, x, AF.Abs)
+                mm(diag(o, "LD", "ABX", 256 * lo, 256 * hi), False, False)
+            else:
+                mm(diag(o, "LX", "X", 256 * lo, 256 * hi), False, False)
+                ts(ab, x, 0.0, mx)
+                mm(diag(o, "LR", "ABX", 256 * lo, 256 * hi), False, False)
+        at(t, -0.2)
+        mm([(key, ib, s1)], False, True)
+        at(t, 0.0)
+        scan(v("SC", 0, 192), v("RS", 0, 192), key, mn)
+        at(t, 0.7)
+        act(v("DT", 0, 192), key)
+        key = v("P7", 192, 384)
+        mm([(key, n2b, s1), (key, full("IF"), v("DT", 0, 192))])
+        row = v("P3", 192, 384)
+        mm([(row, i1, x192), (row, i2b, one), (row, i2b, one)], True, False)
+        mm([(row, n2b, s1)], False, True)
+        scan(v("SC", 576, 768), v("RS", 0, 192), row, mn)
+        at(t, 0.1)
+        tt(wi(kF), v("SC", 15, 192, 16), thr, mn)
+        ts(wi(cF), wi(kF), 255, band)
         ts(wu(JF), wi(cF), 16.0, mul, col(cN), add)
-        ts(w3(F3, 1), wi(cF), 192.0, ge, GROW, mul)
-        nf = w3(F3, 1)
-        tt(v("TT", 12 * b, 12 * b + 12), v("TT", 12 * b, 12 * b + 12), nf, add)
         act(v("LW", 192, 384), ind(blk, wu(JF)))
-        zs = v("ZS", 192 * t, 192 * t + 192)
-        if FZS:
-            lin(zs, ind(v("ABX", 0, BS), wu(JF)), 0.5)
-            send(t, 0, v("ZI", 192 * t, 192 * t + 192), zs)
-        mm([(v("P2", 0, 192), v("BC", 0, 128), v("LW", 192, 384))], True, True)
-        mm([(v("P4", 0, 12), i1, ch(WA + b))] + diag(v("P4", 0, 12), "LP", "LW", 192, 384), True, True)
-        mm(diag(v("P1", 0, 12), "LN", "LW", 192, 384), True, False)
-        scan(v("SC", 960, 1152), v("DS", 0, 192), v("P2", 0, 192), mn)
-        ts(wu(WX), v("P4", 0, 12), col(cNN), add)
-        tt(v("GE", 0, 12), v("P4", 0, 12), cl(VID), ge)
-        act(v("LQ", 0, 192), ind(v("LW", 0, 592), wu(WX)))
-        ts(wu(EFU), v("SC", 975, 1152, 16), col(cA15), add)
-        lin(w(NFA), nf, 1.0, col(cA15))
-        tt(w(BASE), v("SC", 975, 1152, 16), w(NFA), add)
-        mm([(v("P1", 0, 12), ib, v("GE", 0, 12))], False, False)
-        mm(diag(v("P1", 0, 12), "LE", "LQ", 0, 192), False, True)
-        ts(w(TD), v("P1", 0, 12), 0.0, eq, DROP, mul)
-        tt(w(OFFS), w(TD), w(BASE), add)
-        cp(v("OO", 16 * t, 16 * t + 12), w(OFFS))
-        send(t, 1, v("OI", 16 * t, 16 * t + 12), v("OO", 16 * t, 16 * t + 12))
-        scan(v("SC", 0, 192), v("P3", 192, 384), v("DC", 0, 192), mn)
-        scan(v("SC", 576, 768), v("P5", 0, 192), v("DC", 0, 192), mx)
-        tt(wi(iS, 2), v("SC", 15, 384, 16), w(THS, 24), mn)
-        tt(wi(iM), cl(C2), v("SC", 591, 768, 16), sub)
-        ts(wi(cM, 3), wi(iM, 3), 255, band)
-        ts(wu(JM, 24), wi(cM, 2), 16.0, mul, col(cN), add)
-        ts(w(J3, 36), wi(cS, 3), 16.0, mul, col(cN), add)
-        act(w3(F3, 0), w3(J3, 2), AF.Relu, 3072.0 * 8192, -8192.0)
-        act(w3(F3, 2), w3(J3, 1), AF.Relu, 3072.0 * 8192, -8192.0)
-        act(v("XS", 0, 192), ind(v("X", 0, BS), v("WU", 16 * JM + 12, 16 * JM + 24)))
-        u = v("P7", 192, 384)
-        mm([(u, i1, v("HALF", 0, 192)), (u, i1, z), (u, i1, z), (u, i1, v("XS", 0, 192))], True, True)
-        lin(v("U", 0, 192), u, 1.0, MAGIC)
-        lin(v("ABX", 3072, BS), v("U", 0, 192), 1.0, -MAGIC)
-        lin(zn, ind(v("ABX", 0, BS), wu(JF)), 0.5)
-        if not FZS:
-            send(t, 0, v("ZI", 192 * t, 192 * t + 192), zn)
-        act(v("LS", 384 * t, 384 * t + 384), ind(blk, wu(JM, 24)))
-        send(t, 2, v("EM", 192 * t, 192 * t + 192), v("LS", 384 * t, 384 * t + 192))
-        if t < STEPS - 2:
-            spread(b, zn)
+        at(t, 1.7)
+        cp(wb(cFb), wi(cF))
+        act(wb(sN), wb(cFb), AF.Sign, -191.5)
+        idle.append(wb(sN))
+        zf = v("ZE", 192 * t, 192 * t + 192)
+        at(t, 2.35)
+        act(zf, ind(v("X", 0, BS), wu(JF)), AF.Abs)
+        send(t, 0, v("ZI", 192 * t, 192 * t + 192), zf)
+        at(t, 1.0)
+        par, test, oo = v("P5", 0, 12), v("P2", 0, 12), v("P5", 16, 28)
+        if OPT["pick_e"]:
+            el = pick(v("P1", 0, 192), v("LW", 192, 384), 768)
+            ts(wu(EFU), el, -LIFT, add)
+        else:
+            mm(diag(v("P1", 0, 12), "LE", "LW", 192, 384))
+            ts(wu(EFU), v("P1", 0, 12), -LIFT, add)
+            el = w(0)
+            act(el, v("P1", 0, 12))
         ext = v("AX", EXT, EXT + 192)
         act(ext, ind(v("K", 0, 2240), wu(EFU)))
-        mm([(v("P6", 0, 192), v("BC", 0, 128), ext)], True, True)
-        if not FCB:
-            mm([(v("P0", 192, 384), v("BC", 0, 128), ext)], True, True)
-            act(v("CB", 0, 192), v("P0", 192, 384))
-        scan(v("SC", 1152, 1344), v("DS", 0, 192), v("P6", 0, 192), mn)
-        craw = v("SC", 1167, 1344, 16)
-        ts(w(CLI), craw, col(cA15), add)
-        ts(wu(CU_), craw, col(cA15), add)
-        lin(w(CLA), craw, 1.0, col(cA30))
+        at(t, 1.2)
+        mm([(par, i1, ch(WA + b))] + diag(par, "LP", "LW", 192, 384))
+        at(t, 1.8)
+        ts(wu(WX), par, col(cNN), add)
+        tt(wb(GE), par, cl(VID), ge)
+        act(v("LQ", 0, 192), ind(v("LW", 0, 592), wu(WX)))
+        at(t, 2.5)
+        mm([(test, full("NF"), el), (test, ib, wb(GE))], True, False)
+        mm(diag(test, "LE", "LQ", 0, 192), False, True)
+        mm([(oo, full("IF"), el), (oo, full("IO"), wb(sN))], True, False)
+        at(t, 3.2)
+        ts(wb(TD), test, 0.0, eq, DROP, mul)
+        mm([(oo, i1, wb(TD))], False, True)
+        ts(v("OO", 16 * t, 16 * t + 12), oo, DROP / 2 - LIFT, add)
+        send(t, 1, v("OI", 16 * t, 16 * t + 12), v("OO", 16 * t, 16 * t + 12))
+        at(t, 2.0)
+        if OPT["pick_c"]:
+            cl_ = pick(v("P3", 0, 192), ext, 960)
+            win = v("SC", 960, 1152)
+        mm([(v("P6", 0, 288), i1, v("MK", 0, 288))], True, False)
+        mm([(v("P6", 48 * c + lo, 48 * c + lo + n), full("BC"), v("AX", EXT + 32 * c, EXT + 32 * c + n)) for c in range(6) for lo, n in ((0, 16), (16, 32))], False, True)
+        act(v("CB", 0, 288), v("P6", 0, 288))
+        if not OPT["pick_c"]:
+            mm(diag(v("P3", 0, 12), "LE", "AX", EXT, EXT + 192))
+            cl_ = win = w(1)
+            act(cl_, v("P3", 0, 12))
+        at(t, 2.8)
+        tt(v("B0", 0, 288), ind(win, v("CU", 24, 42)), v("CB", 0, 288), eq)
+        ts(wu(CU_), cl_, -LIFT, add)
         lin(v("GM", 0, 192), ind(v("A", 0, 2240), wu(CU_)), col(cK0 + b))
-        if FCB:
-            act(v("CB", 0, 192), ind(w(CLI), v("CU", 24, 36)))
-            tt(v("B0", 0, 192), v("CB", 0, 192), v("P6", 0, 192), eq)
-            tt(v("B0", 192, 368), v("CB", 0, 176), v("P6", 16, 192), eq)
-        else:
-            tt(v("B0", 0, 192), ind(w(CLI), v("CU", 24, 36)), v("CB", 0, 192), eq)
-            tt(v("B0", 192, 368), ind(w(CLI), v("CU", 24, 35)), v("CB", 16, 192), eq)
-        mm([(v("P6", 192, 384), v("TR", 0, 128), v("B0", 0, 192)), (v("P6", 208, 384), v("OK", 0, 128), v("B0", 192, 368))], True, True)
-        scan(v("SC", 768, 960), v("DS", 0, 192), v("P6", 192, 384), mn)
-        tt(w(DUP), v("SC", 783, 960, 16), w(CLA), add)
-        tt(w(DUP), w(DUP), cl(DUM), mn)
-        cp(wu(CO_), w(DUP))
+        at(t, 3.3)
+        scan(v("SB", 0, 288), v("DD", 0, 288), v("B0", 0, 288), mx, mul)
+        for j in range(2):
+            mine = v("SC", 975 + 16 * j, 1152, 32) if OPT["pick_c"] else v("W", 96 * t + 16 + j, 96 * t + 28, 2)
+            tt(raw(T.W[:, 96 * t + 32 + j:96 * t + 44:2], "W", 96 * t + 32, 96 * t + 44, j, 6), v("SB", 15 + 32 * j, 288, 48), mine, mx)
+        ts(wu(CO_), w(2), -LIFT, add)
         for c in range(5, -1, -1):
-            tt(ind(v("A", 0, 2240), v("WU", 16 * CO_ + 2 * c, 16 * CO_ + 2 * c + 2)), v("GM", 32 * c, 32 * c + 32),
-               v("VR", 192 * b + 32 * c, 192 * b + 32 * c + 32), add)
-        h = v("P5", 192, 204)
-        mm([(h, i1, ch(HA)), (h, i1, ch(HN))] + diag(h, "LH", "LS", 384 * t + 192, 384 * t + 384), True, True)
-        tt(w(HINT), h, w3(J3, 0), add)
-        tt(w(FE), cl(EXI), nf, sub)
-        tt(w(HINT), w(HINT), w(FE), mx)
-        cp(wu(VU), w(HINT))
-        tt(w(S3, 36), w(J3, 36), w(F3, 36), add)
-        tt(w(PM), w3(S3, 0), w3(S3, 1), mn)
-        tt(w(PM), w(PM), w3(S3, 2), mn)
-        cp(wu(PU), w(PM))
-
-        def relist(t):
-            b = t % 2
-            act(v("VAL", 0, 192), ind(v("AX", 0, EXT + 192), wu(VU)))
-            cp(ind(v("AX", BS * b, BS * b + BS), wu(PU)), v("VAL", 0, 192))
-            items = diag(v("P7", 0, 192), "LE", "AX", BS * b, BS * b + 3072)
-            for c in range(4):
-                mm(items[4 * c:4 * c + 4], c == 0, c == 3)
-            if t < STEPS - 2:
-                cp(v("G", 192 * b, 192 * b + 192), v("P7", 0, 192))
-            else:
-                act(v("EF", 0, 192), v("P7", 0, 192))
-                act(v("YE", 192 * b, 192 * b + 192), ind(v("EF", 0, 192), v("CU", 36, 48)))
-                dma("sp", raw(T.ye[:, 192 * b:192 * b + 192], "ye", b, b + 1), v("YE", 192 * b, 192 * b + 192), 96)
-        if t:
-            relist(t)
-        if t >= STEPS - 2:
+            at(t, 5.1 - 0.22 * c)
+            tt(ind(v("A", 0, AW), wu(CO_ + 2 * c, 2)), v("GM", 32 * c, 32 * c + 32), v("VR", 192 * b + 32 * c, 192 * b + 32 * c + 32), add)
+        at(t, 3.4)
+        scan(v("SC", 384, 576), v("RS", 0, 192), key, mn)
+        scan(v("SC", 192, 384), v("CM", 0, 192), key, mx)
+        tt(wi(kM), cl(C2), v("SC", 207, 384, 16), sub)
+        ths, thj = v("P4", 16, 28), v("P4", 28, 40)
+        mm([(v("P4", 16, 40), iw, ch(CC, 24)), (ths, i1, ch(CN)), (thj, i1, wb(cFb)), (ths, iw, wb(sN)), (thj, nw, wb(sN))])
+        tt(wi(kS, 2), v("SC", 399, 768, 16), v("P4", 16, 40), mn)
+        ts(wi(cM, 3), wi(kM, 3), 255, band)
+        ts(wu(JM, 24), wi(cM, 2), 16.0, mul, col(cN), add)
+        act(v("LS", 0, 192), ind(blk, wu(JS)))
+        h = v("P4", 48, 60)
+        mm([(h, i1, ch(HA))] + diag(h, "LH", "LS", 0, 192))
+        at(t, 4.15)
+        tt(w(3), h, wi(cS), add)
+        ts(wu(VU), w(3), 16.0, mul, -45888.0, add)
+        at(t, 5.2)
+        tt(wi(cU), wi(cS), wi(cJ), mn)
+        ts(wu(PU), wi(cU), 16.0, mul, col(cN), add)
+        at(t, 4.7)
+        eo, em = (v("EO", 192 * t, 192 * t + 192), v("EM", 192 * t, 192 * t + 192)) if t < STEPS - 1 else (v("ZE", 1152, 1344), v("ZI", 1152, 1344))
+        act(eo, ind(blk, wu(JM)))
+        send(t, 2, em, eo)
+        at(t, 4.6)
+        act(v("XS", 0, 192), ind(v("X", 0, BS), wu(JS)))
+        u = v("P6", 320, 512)
+        mm([(u, full("I2"), zf), (u, i1, v("XS", 0, 192))])
+        at(t, 4.8)
+        lin(v("U", 0, 192), u, 0.5 - 2.0 ** -11, ROUND)
+        lin(zn, v("U", 0, 192), 1.0, -ROUND)
+        at(t, 6.0)
+        if t < STEPS - 2:
+            spread(t + 2, pool_copy)
+        else:
             dma("sp", raw(T.yz[:, 192 * b:192 * b + 192], "yz", b, b + 1), zn, 48)
-    mm([(v("P1", 0, 256), v("BO", 7 - c, 135 - c), v("A", 256 * c, 256 * c + 256)) for c in range(8)], True, True)
+    relist(STEPS - 1)
+    t = STEPS - 1
+    at(t, 4.0)
+    arrive(t, 1, v("OI", 16 * t, 16 * t + 12))
+    take(t, 0, "M", v("ZI", 192 * t, 192 * t + 192))
+    dma("sp", hbm("ym"), v("M", 0, 2048), 512)
+    at(t, 6.0)
+    for c in range(2):
+        act(v("KB", 1024 * c, 1024 * c + 1024), v("K", 1024 * c, 1024 * c + 1024))
+    take(t, 2, "KB", v("ZI", 1152, 1344))
+    mm([(v("P2", 0, 128), v("LE", 15 - c, 143 - c), v("KB", 128 * c, 128 * c + 128)) for c in range(16)])
+    lin(v("YK", 0, 128), v("P2", 0, 128), 1.0, -LIFT)
+    dma("a", hbm("yk"), v("YK", 0, 128), 64)
+    ts(v("BO", 0, 144), x144, scaled(cN, 64.0, scaled(cG, 0.5, 7.0)), eq, col(cW01), mul)
+    mm([(v("P1", 0, 256), v("BO", 7 - c, 135 - c), v("A", 256 * c, 256 * c + 256)) for c in range(8)])
     lin(v("YO", 0, 256), v("P1", 0, 256), 1.0, 192.0)
     dma("a", hbm("yo"), v("YO", 0, 256), 128)
-    arrive(STEPS - 1, 1, v("OI", 80, 92))
-    take(STEPS - 1, 0, "M", v("ZI", 960, 1152))
-    dma("sp", hbm("ym"), v("M", 0, 2048), 512)
-    take(STEPS - 1, 2, "K", v("EM", 960, 1152))
-    mm([(v("P2", 0, 128), v("LE", 15 - c, 143 - c), v("K", 128 * c, 128 * c + 128)) for c in range(16)], True, True)
-    act(v("YK", 0, 128), v("P2", 0, 128))
-    dma("a", hbm("yk"), v("YK", 0, 128), 64)
-    tt(w(24, 24), v("TT", 0, 24), v("T0", 0, 24), sub)
-    ts(w(26, 24), w(24, 24), 1.0 / GROW, mul, 0.25, add)
-    cp(wu(10, 24), w(26, 24))
-    tt(v("YT", 0, 384), ind(v("T4", 0, 8), wu(10, 24)), v("THF", 0, 384), add)
-    dma("sp", hbm("yt"), raw(T.YT[0::16, :], "YT"))
+    ts(v("LT", 0, 144), x144, col(cP), eq, 48.0, mul)
+    yt = raw(T.P3[0:8, 0:384], "P3", 0, 384, n=384)
+    mm([(yt, raw(T.IF[0:8, 0:8], "IF", n=8), thf)] +
+       [(raw(T.P3[0:8, 192 * (t % 2) + q:192 * (t % 2) + 192:16], "P3", 0, 384, n=12), v("LT", q, 128, 16), idle[t]) for t in range(STEPS) for q in range(16)])
+    lin(raw(T.YT[0:8, :], "YT", n=384), yt, 1.0, 144.0)
+    dma("sp", hbm("yt"), raw(T.YT[0:8, :], "YT"))
     schedule(g, T, ops)

@@ -10,23 +10,25 @@ ROUND = 12582912.0
 GROW = 96.0 * 256
 DROP = 2304.0
 LIFT = 256.0
+RISE = 73728.0
+PAD = 256
 WIDE = 4608
 AW = 2816
 bf, f32, i32, u16 = "bfloat16", "float32", "int32", "uint16"
 
 SCRATCH = {}
 for _n, _w, _d in (
-        ("M", WIDE, bf), ("K", WIDE, f32), ("KB", WIDE, bf), ("A", AW, bf), ("AX", EXT + 192, bf), ("X", BS, bf), ("ABX", 3072, bf),
+        ("M", PAD + WIDE, bf), ("K", PAD + WIDE, f32), ("KB", PAD + WIDE, bf), ("A", PAD + AW, bf), ("AX", EXT + 192, bf), ("X", BS, bf), ("ABX", 3072, bf),
         ("ZE", 1344, bf), ("ZI", 1344, bf), ("EO", 960, f32), ("EM", 960, f32), ("OO", 96, u16), ("OI", 96, u16), ("G", 384, u16),
         ("EI", 384, i32), ("OW", 256, i32), ("OB", 256, bf), ("OH", 512, bf), ("EN", 128, i32), ("SR", 256, bf), ("SK", 256, f32),
         ("TH", 384, i32), ("THF", 384, f32), ("TT", 32, f32), ("XF", 192, bf), ("XG", 192, bf), ("XQ", 288, bf),
         ("PI", 8, i32), ("CO", 48, f32), ("W", 96 * STEPS, f32), ("WI", 112 * STEPS, i32), ("WU", 144 * STEPS, u16), ("WB", 64 * STEPS, bf),
-        ("CU", 80, u16), ("CL", 128, f32), ("CH", 96, bf),
+        ("CU", 80, u16), ("CL", 128, f32), ("CH", 112, bf),
         ("LB", 144, bf), ("LD", 144, bf), ("LR", 144, bf), ("LX", 144, bf), ("L0", 144, bf), ("L1", 144, bf), ("LE", 144, bf), ("LP", 144, bf),
         ("LH", 144, bf), ("LT", 144, bf), ("LF", 144, f32), ("BO", 144, bf), ("I1", 128, bf), ("I2", 128, bf), ("IB", 128, bf), ("ID", 128, bf), ("ND", 128, bf),
         ("IG", 128, bf), ("IO", 128, bf), ("IW", 128, bf), ("NW", 128, bf), ("IF", 128, f32), ("NF", 128, f32), ("ON", 128, bf), ("BC", 128, bf),
-        ("CAW", 192, f32), ("ONE", 288, bf), ("RS", 192, bf), ("RN", 192, bf), ("CM", 192, bf), ("NV", 384, bf), ("NM", 192, bf),
-        ("MK", 288, bf), ("DD", 288, bf), ("VR", 384, bf), ("LW", 592, bf), ("LQ", 192, bf), ("LS", 192, bf), ("SG", 192, bf), ("Q", 192, bf), ("SIG", 208, bf),
+        ("SI", 192, i32), ("DF", 192, f32), ("XA", 192, bf), ("IC", 128, bf), ("NC", 128, bf), ("LN", 144, bf), ("ONE", 288, bf), ("RS", 192, bf), ("RN", 192, bf), ("CM", 192, bf), ("NV", 384, bf), ("NM", 192, bf),
+        ("MK", 288, bf), ("DD", 288, bf), ("VR", 384, bf), ("LW", 784, bf), ("LQ", 192, bf), ("LS", 192, bf), ("SG", 192, bf), ("Q", 192, bf), ("SIG", 208, bf),
         ("DT", 384, f32), ("SC", 1152, f32), ("XS", 192, bf), ("U", 192, f32), ("CB", 288, f32), ("B0", 288, bf), ("SB", 288, bf), ("GM", 192, bf), ("VAL", 192, bf),
         ("EF", 192, f32), ("YE", 384, f32), ("YT", 384, f32), ("YO", 256, f32), ("YK", 128, f32), ("T1", 384, bf), ("T2", 384, bf), ("T3", 384, bf)):
     SCRATCH[_n] = ("sbuf", [128, _w], _d)
@@ -36,11 +38,16 @@ SCRATCH["Z"] = ("sbuf", [128, 48, 32], bf)
 for _k in range(8):
     SCRATCH["P%d" % _k] = ("psum", [128, 512], f32)
 SEMAPHORES = ["v", "a", "pe", "p", "sent"] + ["d%d" % _k for _k in range(40)] + ["r%d" % _k for _k in range(18)]
-CY, WAKE, FLIGHT = 0.83, 150.0, 2100.0
+CY, WAKE, FLIGHT = 0.83, 170.0, 2600.0
 GATH, SCAT = 1.56, 3.8
 OPT = {"pick_e": True, "pick_c": True, "mch": ((0, 4, "a"), (4, 8, "a"), (8, 12, "v")), "ach": ((0, 4, "a"), (4, 8, "a"), (8, 12, "a")),
-       "mch0": ((0, 4, "a"), (4, 8, "v"), (8, 12, "v")),
-       "ach0": ((0, 4, "a"), (4, 8, "a"), (8, 12, "a")), "val": 0, "tries": 12000, "heat": 200, "seed": 2}
+       "mch0": ((0, 4, "v"), (4, 8, "a"), (8, 12, "v")),
+       "ach0": ((0, 4, "a"), (4, 8, "a"), (8, 12, "a")), "val": 0, "iscan": True, "ne": 2, "tries": 18000, "more": 7000, "heat": 400, "seed": 13, "tied": 0.0, "mix": 0.7, "wary": 0.0}
+DUE = {"owners": -6.5, "sign": -2.0, "stale": -0.9, "thresholds": -3.0, "idle states": -8.0, "take states": -6.8, "take names": -0.9,
+       "distances": -5.9, "sizes": -2.6, "key": -0.2, "nearest": 0.0, "stale key": 2.6, "first stale": 2.5, "fired": 2.6, "name": 1.3,
+       "partner": 1.45, "same name": 2.2, "claimed": 2.1, "compare": 3.7, "winners": 4.3, "claim": 7.0, "other rows": 7.05, "hint": 7.08,
+       "row": 7.1, "farthest": 7.3, "halve": 7.2, "state": 7.25, "spread": 7.5, "value": 7.1, "list": 13.3, "relist": 17.0}
+SLOW = (1.4, 2.0 / GATH, 5.5 / SCAT)
 PLAN = {}
 
 
@@ -104,6 +111,23 @@ def place(ops, pred, prio):
     return start, end
 
 
+def replay(ops, pred, start):
+    begin, free, end = [0.0] * len(ops), {}, 0.0
+    for i in sorted(range(len(ops)), key=lambda i: start[i]):
+        q, c, l = ops[i]
+        s = free.get(q, 0.0) if c else 0.0
+        for m, d in pred[i]:
+            d += begin[m]
+            if d > s:
+                s = d
+        begin[i] = s
+        if c:
+            free[q] = s + c
+        if s + c + l > end:
+            end = s + c + l
+    return begin, end
+
+
 def ranked(succ, due, kind, shift):
     key = [due[i] + shift[kind[i]] for i in range(len(due))]
     for i in range(len(due) - 1, -1, -1):
@@ -112,7 +136,7 @@ def ranked(succ, due, kind, shift):
             if key[j] <= k:
                 k = key[j] - 0.01
         key[i] = k
-    return sorted(range(len(due)), key=lambda i: key[i])
+    return sorted(range(len(due)), key=lambda i: key[i]), key
 
 
 def blocked(ops, pred, start):
@@ -145,29 +169,60 @@ def order(ops, deps, after):
     short = [(o["q"], o["c"], o["l"]) for o in ops]
     kinds = sorted(set(o["kind"] for o in ops))
     kind = [kinds.index(o["kind"]) for o in ops]
+    alike = [[m for m, y in enumerate(kinds) if y[1:] == x[1:] and (x[0] < 0) == (y[0] < 0)] for x in kinds]
+    steady = [m for m, x in enumerate(kinds) if x[0] == 1]
     due = [o["due"] for o in ops]
     shift, seed = [0.0] * len(kinds), OPT["seed"]
-    start, end = place(short, pred, ranked(succ, due, kind, shift))
-    best, pairs = (end, start), blocked(short, pred, start)
-    for r in range(OPT["tries"]):
+    prio, key = ranked(succ, due, kind, shift)
+    slow = [(o["q"], o["slow"], o["l"]) for o in ops]
+    pred2 = [[(m, d + ops[m]["slow"] - ops[m]["c"]) for m, d in pred[i]] for i in range(n)]
+    start, end = place(short, pred, prio)
+    best, pairs, mix = (end, start, shift, key), blocked(short, pred, start), 0.0
+    for r in range(OPT["tries"] + OPT["more"]):
+        heat = OPT["heat"] * (1 - r / OPT["tries"])
+        if r >= OPT["tries"]:
+            heat = 150.0 * (1 - (r - OPT["tries"]) / OPT["more"])
+        if r == OPT["tries"]:
+            mix = OPT["mix"]
+            fast, start, shift, key = best
+            end = fast * (1 - mix) + mix * replay(slow, pred2, start)[1] / 1.5
+            best = (end, start, shift, key)
         trial = list(shift)
         seed = (seed * 1103515245 + 12345) % 2 ** 31
-        if r % 2 and pairs:
+        moves = {}
+        if r % 3 and pairs:
             x, y = pairs[(seed >> 8) % len(pairs)]
-            gap = max(due[y] + shift[kind[y]] - due[x] - shift[kind[x]], 0.0) + 20.0 + (seed >> 4) % 200
+            more = 20.0 + (seed >> 4) % 200
             if seed >> 20 & 1:
-                trial[kind[x]] += gap
+                todo = [x]
+                while todo:
+                    m = todo.pop()
+                    if kind[m] not in moves and due[m] + shift[kind[m]] < key[y] + more:
+                        moves[kind[m]] = key[y] + more - due[m] - shift[kind[m]]
+                        todo += succ[m]
             else:
-                trial[kind[y]] -= gap
+                moves[kind[y]] = min(key[x] - more - due[y] - shift[kind[y]], 0.0)
         else:
-            trial[(seed >> 8) % len(kinds)] += ((seed >> 3) % 31 - 15) * (20.0, 60.0, 200.0)[(seed >> 20) % 3]
-        s2, e2 = place(short, pred, ranked(succ, due, kind, trial))
-        if e2 <= end + OPT["heat"] * (1 - r / OPT["tries"]):
-            shift, start, end = trial, s2, e2
-            pairs = blocked(short, pred, start)
+            x = steady[(seed >> 8) % len(steady)] if seed >> 24 & 1 else (seed >> 8) % len(kinds)
+            moves[x] = ((seed >> 3) % 31 - 15) * (20.0, 60.0, 200.0)[(seed >> 20) % 3]
+        for x, by in moves.items():
+            for m in alike[x] if r < OPT["tries"] * OPT["tied"] else [x]:
+                trial[m] += by
+        prio, k2 = ranked(succ, due, kind, trial)
+        s2, e2 = place(short, pred, prio)
+        e1 = e2
+        if mix:
+            if e1 > fast + 1200.0:
+                continue
+            s3, e3 = replay(slow, pred2, s2)
+            e2 = e1 * (1 - mix) + mix * e3 / 1.5
+        if e2 <= end + heat:
+            shift, start, end, key, fast = trial, s2, e2, k2, e1
+            pairs = blocked(short, pred, start) + (blocked(slow, pred2, s3) if mix else [])
             if end < best[0]:
-                best = (end, start)
+                best = (end, start, shift, key)
     PLAN["end"] = best[0]
+    PLAN["dbg"] = (ops, pred, best[1], short)
     return sorted(range(n), key=lambda i: best[1][i])
 
 
@@ -227,10 +282,12 @@ def rank_program(g, core, T, topo):
     ops, sends, step, now = [], {}, [-1, {}], [0.0]
     V, S, PE = g.vector, g.scalar, g.tensor
 
-    def at(t, x):
-        now[0] = 12000.0 + 12500.0 * t + 1000.0 * x
+    def at(t, x, by=0.0):
+        now[0] = 13000.0 + 14000.0 * t + 1000.0 * (DUE[x] + by if x in DUE else x)
 
     def v(name, lo, hi, st=1):
+        if name in ("A", "M", "K", "KB"):
+            lo, hi = lo + PAD, hi + PAD
         return (T[name][:, lo:hi:st] if st > 1 else T[name][:, lo:hi], [(name, lo, hi, None)], [], (hi - lo + st - 1) // st, False)
 
     def raw(ap, name, lo=0, hi=10 ** 6, pk=None, n=0):
@@ -250,7 +307,11 @@ def rank_program(g, core, T, topo):
         key = (step[0] if step[0] in (-1, 0, STEPS - 1) else 1, e, k, w[0][0] if w else r[0][0])
         step[1][key] = step[1].get(key, 0) + 1
         now[0] += 10.0
-        ops.append({"mid": mid, "due": now[0], "kind": key + (step[1][key],), "e": e, "q": "x" if k == "x" else e, "f": f, "r": r, "w": w, "k": k, "c": c, "l": lat, "after": after})
+        rate = SLOW[2] if outs and outs[0][4] else SLOW[1] if any(isinstance(x, tuple) and x[4] for x in ins) else 1.0
+        slow = SLOW[0] * (55 + (c - 55) * rate) if k == "c" else c
+        if step[0] < 0:
+            c = c + OPT["wary"] * (slow - c)
+        ops.append({"slow": slow, "mid": mid, "due": now[0], "kind": key + (step[1][key],), "e": e, "q": "x" if k == "x" else e, "f": f, "r": r, "w": w, "k": k, "c": c, "l": lat, "after": after})
 
     def cost(o, x, f=1.0):
         n = max(o[3], x[3])
@@ -303,10 +364,10 @@ def rank_program(g, core, T, topo):
     def sel(o, x, pattern, f, fill, cm=0, base=0):
         op("p", lambda: g.affine_select(o[0], x[0], pattern, f, fill, base, cm), [o], [x], 170 + 2 * CY * o[3])
 
-    def mm(items, start=True, stop=True):
+    def mm(items, start=True, stop=True, each=False):
         def f():
             for n, (o, l, r) in enumerate(items):
-                ins = PE.matmul(o[0], l[0], r[0], start and n == 0, stop and n == len(items) - 1)
+                ins = PE.matmul(o[0], l[0], r[0], each or (start and n == 0), each or (stop and n == len(items) - 1))
             return ins
         c = sum(0.42 * max(min(64, l[3]), r[3]) * (4 if SCRATCH[l[1][0][0]][2] == f32 else 1) for o, l, r in items)
         op("pe", f, [x[0] for x in items], [x[1] for x in items] + [x[2] for x in items], c, mid=not (start or stop))
@@ -361,7 +422,7 @@ def rank_program(g, core, T, topo):
         sel(o, x, [[0, o[3]]], ge, 0.0)
 
     def rows(name, r):
-        return raw(T[name][r::16, 0:2048], name, 0, 2048, r)
+        return raw(T[name][r::16, PAD:PAD + 2048], name, PAD, PAD + 2048, r)
 
     def hbm(name):
         return raw(T[name][:], name)
@@ -382,9 +443,9 @@ def rank_program(g, core, T, topo):
         lin(col(spare[0]), col(j), scale, bias)
         return col(spare[0])
     IL, VID, C2, CT = range(4)
-    WA, HA, CC, CN = 0, 2, 3, 5
+    WA, HA, CC, CN, CI, HN, HC = 0, 2, 3, 5, 6, 7, 8
 
-    at(0, -12.0)
+    at(0, -13.0)
     dma("sp", v("OW", 0, 256), hbm("own"), 128)
     dma("a", raw(T.Z[:, 0:12], "Z", 0, 2), hbm("st"), 96)
     dma("sp", v("EI", 0, 384), hbm("ends"), 192)
@@ -414,8 +475,8 @@ def rank_program(g, core, T, topo):
     spread(0, cp)
     at(STEPS, 0.0)
     io(xg, [[16, 12], [0, 16]], 0)
-    io(v("XQ", 0, 288), [[0, 18], [1, 16]], 0)
-    lin(v("ONE", 0, 288), v("XQ", 0, 288), 0.0, 1.0)
+    io(xq, [[0, 12], [1, 16]], 0)
+    lin(one, x192, 0.0, 1.0)
     ts(i1, v("XF", 0, 128), col(cP), eq)
     lin(col(cNN), col(cN), -1.0)
     lin(col(cG), col(cP), 1.0, col(cNN))
@@ -426,17 +487,27 @@ def rank_program(g, core, T, topo):
     ts(v("LB", 0, 144), x144, -15.0, add, col(cG), eq)
     for name, c in (("L0", col(cW0)), ("L1", col(cW1)), ("LD", 256.0), ("LR", 512.0), ("LX", -256.0), ("LE", col(cWE)), ("LP", col(cW01))):
         lin(v(name, 0, 144), v("LB", 0, 144), c)
-    for name, c in (("ID", 2 * B), ("IB", B), ("ND", -2 * B), ("IF", 1.0), ("NF", -1.0)):
+    for name, c in (("ID", 2 * B), ("IB", B), ("ND", -2 * B), ("IF", 1.0)):
         lin(full(name), i1, c)
-    for name, c in (("IG", GROW / 2), ("IW", 0.75 * B), ("NW", -0.75 * B), ("I2", 2.0), ("IO", DROP / 2)):
+    for name, c in (("IG", GROW / 2), ("IW", 0.75 * B), ("NW", -0.75 * B), ("I2", 2.0), ("IO", DROP + LIFT if OPT["ne"] else DROP / 2)):
         ts(full(name), i1, c, mul)
+    if OPT["ne"]:
+        ts(v("LN", 0, 144), v("LE", 0, 144), -4096.0, mul)
+        lin(ch(CI), x12, 16.0, col(cN))
+    else:
+        lin(full("NF"), i1, -1.0)
     lin(v("NV", 0, 192), xg, -1.0, scaled(cN, -1.0, 192.0))
     lin(v("NV", 192, 384), xg, -1.0, col(cNN))
     io(v("X", 3264, BS), [[0, 192]], 0)
     sel(v("RN", 0, 192), v("X", 3264, BS), [[0, 12], [1, 16]], ne, -BIG)
     lin(v("RS", 0, 192), v("RN", 0, 192), -1.0)
     lin(v("CM", 0, 192), v("RN", 0, 192), 1.0, 2.0)
-    io(cl(CT), [[1, 12]], 2 ** 22 - 64)
+    io(cl(CT), [[1, 12]], -64 if OPT["iscan"] else 2 ** 22 - 64)
+    if OPT["iscan"]:
+        lin(v("XA", 0, 192), xg, 1.0, 1.0)
+        lin(v("DF", 0, 192), xg, 0.0)
+        lin(full("IC"), i1, RISE)
+        lin(full("NC"), i1, -RISE)
     thf = raw(T.THF[0:8, :], "THF", n=384)
     cp(thf, raw(T.TH[0:8, :], "TH", n=384))
     ts(v("LF", 0, 144), x144, scaled(cP, 16.0, 15.0), eq, 256.0, mul)
@@ -464,7 +535,9 @@ def rank_program(g, core, T, topo):
     io(v("LW", 384, 592), [[0, 208]], 4000)
     io(v("CH", 0, 24), [[-384, 2], [-16, 12]], 576)
     io(cl(C2), [[32, 12]], 15 * 2 ** 20 + 30)
-    io(ch(HA), [[-16, 12]], 0)
+    io(ch(HA), [[-256, 12]], 3072)
+    lin(ch(HN), x12, 0.0, scaled(cN, -1.0, 192.0))
+    io(ch(HC), [[0, 12]], -4)
     io(ch(CN), [[1, 12]], 204)
     io(ch(CC, 24), [[2, 2], [0, 12]], 1)
     io(cl(4, 18), [[2, 6], [0, 3]], 1)
@@ -477,14 +550,14 @@ def rank_program(g, core, T, topo):
     else:
         cp(v("CU", 24, 42), cl(4, 18))
     ts(v("NM", 0, 192), xq, col(cN), ne, -FAR, mul)
-    ts(v("MK", 0, 288), v("XQ", 0, 288), col(cN), ge, 4096.0, mul)
-    sel(v("MK", 0, 288), v("MK", 0, 288), [[0, 6], [1, 3], [0, 16]], ne, 0.0, base=-1)
-    io(v("DD", 0, 288), [[0, 288]], 1)
-    c16 = scaled(cN, 16.0)
+    io(v("MK", 0, 288), [[0, 6], [1, 48]], 0)
+    ts(v("SB", 0, 288), v("MK", 0, 288), col(cN), eq, scaled(cN, 16.0, 2304.0 + LIFT), mul)
+    ts(v("B0", 0, 288), v("MK", 0, 288), scaled(cN, 1.0, 32.0), eq, scaled(cN, 16.0, 2560.0 + LIFT), mul)
+    mm([(v("P6", 0, 288), i1, v("SB", 0, 288)), (v("P6", 0, 288), i1, v("B0", 0, 288))])
+    ts(v("DD", 0, 288), v("P6", 0, 288), 1.0, mx)
     for j in range(2):
         lin(v("DD", 16 * j, 288, 48), v("ONE", 0, 6), 0.0)
-        lin(v("DD", 15 + 32 * j, 288, 48), v("ONE", 0, 6), 2304.0 + 256 * j + LIFT, c16)
-    ts(v("LH", 0, 144), v("LB", 0, 144), scaled(cW5, 384.0, scaled(cW4, 15.0, scaled(cW0, 1.0, col(cW6)))), mul, 1.0 / 16, mul)
+    ts(v("LH", 0, 144), v("LB", 0, 144), scaled(cW5, 384.0, scaled(cW4, 15.0, scaled(cW0, 1.0, col(cW6)))), mul)
     lin(col(cK1), col(cW1), -1.0, 1.0)
     lin(col(cK0), col(cWH), -1.0, scaled(cW0, -1.0, 1.0))
     lin(v("VR", 192, 384), x192, col(cW1))
@@ -507,9 +580,11 @@ def rank_program(g, core, T, topo):
 
     def take(t, j, table, src):
         arrive(t, j, src)
-        to = ind(v(table, 0, WIDE), v("OI", 16 * t, 16 * t + 12))
+        to = ind(v(table, -PAD, WIDE), v("OI", 16 * t, 16 * t + 12))
         if table == "K":
             act(to, src, AF.Silu, first=1300.0 * (t == 0))
+            if OPT["ne"]:
+                act(v("K", 2048, 2240), v("AX", 3072, 3264))
         else:
             cp(to, src)
 
@@ -521,12 +596,12 @@ def rank_program(g, core, T, topo):
 
     def relist(t):
         b = t % 2
-        at(t, 4.55)
+        at(t, "value")
         act(v("VAL", 0, 192), ind(v("AX", 0, EXT + 192), v("WU", 144 * t + 112, 144 * t + 124)))
-        at(t, 5.3)
+        at(t, "list")
         cp(ind(v("AX", BS * b, BS * b + BS), v("WU", 144 * t + 128, 144 * t + 140)), v("VAL", 0, 192))
         items = diag(v("P7", 0, 192), "LE", "AX", BS * b, BS * b + 3072)
-        at(t, 12.6)
+        at(t, "relist")
         for c in range(4):
             mm(items[4 * c:4 * c + 4], c == 0, c == 3)
         if t < STEPS - 2:
@@ -553,7 +628,7 @@ def rank_program(g, core, T, topo):
         def wb(j):
             return v("WB", 64 * t + 16 * j, 64 * t + 16 * j + 12)
         kF, cF, kM, kS, kJ, cM, cS, cJ, cU = range(9)
-        JF, JM, JS, WX, EFU, CU_, CO_, VU, PU = 0, 16, 28, 48, 64, 80, 96, 112, 128
+        JF, JM, JS, JJ, WX, EFU, CU_, CO_, VU, PU = 0, 12, 24, 36, 48, 64, 80, 96, 112, 128
         sN, cFb, GE, TD = range(4)
         blk = v("AX", BS * b, BS * b + BS)
         z, zn = zs(t), zs(t + 2)
@@ -562,38 +637,41 @@ def rank_program(g, core, T, topo):
         for n, (lo, hi, e) in enumerate(pieces):
             if t and n == late:
                 relist(t - 1)
-            at(t, -7.1 + 0.35 * lo)
+            at(t, "owners", 0.35 * lo)
             (cp if e == "v" else act)(v("AX", BS * b + 256 * lo, BS * b + 256 * hi), ind(v("A", 0, 2240), v("G", 192 * b + 16 * lo, 192 * b + 16 * hi)))
             for P, L in (("P1", "L0"), ("P2", "L1")):
                 first = [(v(P, 0, 192), i1, v("NV", 192 * b, 192 * b + 192))] if lo == 0 else []
                 mm(first + diag(v(P, 16 * lo, 16 * hi), L, "AX", BS * b + 256 * lo, BS * b + 256 * hi), lo == 0, hi == 12)
         if t and late == len(pieces):
             relist(t - 1)
-        at(t, -2.1)
+        at(t, "sign")
         act(v("SG", 0, 192), v("P1", 0, 192), AF.Sign)
-        at(t, -0.7)
+        at(t, "stale")
         tt(v("Q", 0, 192), v("SG", 0, 192), v("P2", 0, 192), mul)
         s1 = v("SIG", 0, 192)
         ts(s1, v("Q", 0, 192), 0.0, ne)
-        at(t, -0.1)
+        at(t, "thresholds")
         thr = v("P4", 0, 12)
-        mm([(thr, full("IF"), v("TT", 12 * b, 12 * b + 12))] + [(thr, ig, x) for s in idle[b::2] for x in (s, v("ONE", 0, 12))])
-        at(t, -8.0)
+        mm([(thr, full("IF"), v("TT", 12 * b, 12 * b + 12))] + [(thr, ig, x) for s in idle[b::2] for x in (s, v("ONE", 0, 12))]
+           + [(thr, full("IC"), v("XA", 0, 192, 16))] * OPT["iscan"])
+        if OPT["iscan"]:
+            act(v("DF", 0, 192, 16), thr)
+        at(t, "idle states")
         pool_copy(v("X", 3072, 3264), z)
         if t:
-            at(t, -6.2)
+            at(t, "take states")
             arrive(t - 1, 1, v("OI", 16 * t - 16, 16 * t - 4))
             take(t - 1, 0, "M", v("ZI", 192 * t - 192, 192 * t))
-            at(t, -0.9)
+            at(t, "take names")
             take(t - 1, 2, "K", v("EM", 192 * t - 192, 192 * t))
         key = v("P0", 0, 192)
-        mm([(key, i1, x192), (key, i2b, one)], True, False)
+        mm([(key, i1, x192), (key, full("IC"), v("XA", 0, 192)) if OPT["iscan"] else (key, i2b, one)], True, False)
         for lo, hi, e in OPT["mch" if t else "mch0"]:
             x, ab, o = v("X", 256 * lo, 256 * hi), v("ABX", 256 * lo, 256 * hi), v("P0", 16 * lo, 16 * hi)
-            at(t, -5.5 + 0.35 * lo)
+            at(t, "distances", 0.35 * lo)
             for c in range(lo // 2, hi // 2):
                 tt(v("X", 512 * c, 512 * c + 512), ind(v("M", 0, 2048), v("G", 192 * b + 32 * c, 192 * b + 32 * c + 32)), raw(T["ZR%d" % b][:, c], "ZR%d" % b, 0, 512, n=512), sub)
-            at(t, -2.9 + 0.22 * lo)
+            at(t, "sizes", 0.22 * lo)
             if e == "a":
                 act(ab, x, AF.Abs)
                 mm(diag(o, "LD", "ABX", 256 * lo, 256 * hi), False, False)
@@ -601,33 +679,39 @@ def rank_program(g, core, T, topo):
                 mm(diag(o, "LX", "X", 256 * lo, 256 * hi), False, False)
                 ts(ab, x, 0.0, mx)
                 mm(diag(o, "LR", "ABX", 256 * lo, 256 * hi), False, False)
-        at(t, -0.2)
+        at(t, "key")
         mm([(key, ib, s1)], False, True)
-        at(t, 0.0)
-        scan(v("SC", 0, 192), v("RS", 0, 192), key, mn)
-        at(t, 0.7)
+        at(t, "nearest")
+        if OPT["iscan"]:
+            scan(v("SI", 0, 192), v("DF", 0, 192), key, mn, mx)
+            ts(wi(cF), v("SI", 15, 192, 16), 255, band)
+        else:
+            scan(v("SC", 0, 192), v("RS", 0, 192), key, mn)
+            tt(wi(kF), v("SC", 15, 192, 16), thr, mn)
+            ts(wi(cF), wi(kF), 255, band)
+        ts(wu(JF), wi(cF), 16.0, mul, col(cN), add)
+        act(v("LW", 192, 384), ind(blk, wu(JF)))
+        at(t, "stale key")
         act(v("DT", 0, 192), key)
-        key = v("P7", 192, 384)
-        mm([(key, n2b, s1), (key, full("IF"), v("DT", 0, 192))])
+        key = v("P0", 192, 384)
+        if OPT["iscan"]:
+            mm([(key, full("IF"), v("DT", 0, 192)), (key, full("NC"), v("XA", 0, 192)), (key, i2b, one), (key, n2b, s1)])
+        else:
+            mm([(key, n2b, s1), (key, full("IF"), v("DT", 0, 192))])
         row = v("P3", 192, 384)
         mm([(row, i1, x192), (row, i2b, one), (row, i2b, one)], True, False)
         mm([(row, n2b, s1)], False, True)
+        at(t, "first stale")
         scan(v("SC", 576, 768), v("RS", 0, 192), row, mn)
-        at(t, 0.1)
-        tt(wi(kF), v("SC", 15, 192, 16), thr, mn)
-        ts(wi(cF), wi(kF), 255, band)
-        ts(wu(JF), wi(cF), 16.0, mul, col(cN), add)
-        act(v("LW", 192, 384), ind(blk, wu(JF)))
-        at(t, 1.7)
+        at(t, "fired")
         cp(wb(cFb), wi(cF))
         act(wb(sN), wb(cFb), AF.Sign, -191.5)
         idle.append(wb(sN))
         zf = v("ZE", 192 * t, 192 * t + 192)
-        at(t, 2.35)
         act(zf, ind(v("X", 0, BS), wu(JF)), AF.Abs)
         send(t, 0, v("ZI", 192 * t, 192 * t + 192), zf)
-        at(t, 1.0)
-        par, test, oo = v("P5", 0, 12), v("P2", 0, 12), v("P5", 16, 28)
+        at(t, "name")
+        par, test = v("P5", 0, 12), v("P2", 0, 12)
         if OPT["pick_e"]:
             el = pick(v("P1", 0, 192), v("LW", 192, 384), 768)
             ts(wu(EFU), el, -LIFT, add)
@@ -638,46 +722,54 @@ def rank_program(g, core, T, topo):
             act(el, v("P1", 0, 12))
         ext = v("AX", EXT, EXT + 192)
         act(ext, ind(v("K", 0, 2240), wu(EFU)))
-        at(t, 1.2)
-        mm([(par, i1, ch(WA + b))] + diag(par, "LP", "LW", 192, 384))
-        at(t, 1.8)
+        at(t, "partner")
+        mm([(par, i1, ch(WA + b))], True, False)
+        mm(diag(par, "LP", "LW", 192, 384), False, True)
+        at(t, "same name")
         ts(wu(WX), par, col(cNN), add)
         tt(wb(GE), par, cl(VID), ge)
-        act(v("LQ", 0, 192), ind(v("LW", 0, 592), wu(WX)))
-        at(t, 2.5)
-        mm([(test, full("NF"), el), (test, ib, wb(GE))], True, False)
-        mm(diag(test, "LE", "LQ", 0, 192), False, True)
-        mm([(oo, full("IF"), el), (oo, full("IO"), wb(sN))], True, False)
-        at(t, 3.2)
-        ts(wb(TD), test, 0.0, eq, DROP, mul)
-        mm([(oo, i1, wb(TD))], False, True)
-        ts(v("OO", 16 * t, 16 * t + 12), oo, DROP / 2 - LIFT, add)
+        if OPT["ne"]:
+            (act if OPT["ne"] == 1 else pool_copy)(v("LW", 592, 784), v("LW", 192, 384))
+            tt(v("LQ", 0, 192), ind(v("LW", 0, 592), wu(WX)), v("LW", 592, 784), ne)
+            mm([(test, i1, ch(CI)), (test, full("IO"), v("ONE", 0, 12))], True, False)
+            mm([(test, nw, wb(GE))], False, False)
+            mm(diag(test, "LN", "LQ", 0, 192), False, True)
+            tt(v("OO", 16 * t, 16 * t + 12), test, el, mx)
+        else:
+            oo = v("P5", 16, 28)
+            act(v("LQ", 0, 192), ind(v("LW", 0, 592), wu(WX)))
+            mm([(test, full("NF"), el), (test, ib, wb(GE))], True, False)
+            mm(diag(test, "LE", "LQ", 0, 192), False, True)
+            mm([(oo, full("IF"), el), (oo, full("IO"), wb(sN))], True, False)
+            ts(wb(TD), test, 0.0, eq, DROP, mul)
+            mm([(oo, i1, wb(TD))], False, True)
+            ts(v("OO", 16 * t, 16 * t + 12), oo, DROP / 2, add)
         send(t, 1, v("OI", 16 * t, 16 * t + 12), v("OO", 16 * t, 16 * t + 12))
-        at(t, 2.0)
+        late = 5.0 * (t == STEPS - 1)
+        at(t, "claimed", late)
         if OPT["pick_c"]:
             cl_ = pick(v("P3", 0, 192), ext, 960)
             win = v("SC", 960, 1152)
-        mm([(v("P6", 0, 288), i1, v("MK", 0, 288))], True, False)
-        mm([(v("P6", 48 * c + lo, 48 * c + lo + n), full("BC"), v("AX", EXT + 32 * c, EXT + 32 * c + n)) for c in range(6) for lo, n in ((0, 16), (16, 32))], False, True)
+        mm([(v("P6", 48 * c + lo, 48 * c + lo + n), full("BC"), v("AX", EXT + 32 * c, EXT + 32 * c + n)) for c in range(6) for lo, n in ((0, 16), (16, 32))], each=True)
         act(v("CB", 0, 288), v("P6", 0, 288))
         if not OPT["pick_c"]:
             mm(diag(v("P3", 0, 12), "LE", "AX", EXT, EXT + 192))
             cl_ = win = w(1)
             act(cl_, v("P3", 0, 12))
-        at(t, 2.8)
+        at(t, "compare", late)
         tt(v("B0", 0, 288), ind(win, v("CU", 24, 42)), v("CB", 0, 288), eq)
         ts(wu(CU_), cl_, -LIFT, add)
         lin(v("GM", 0, 192), ind(v("A", 0, 2240), wu(CU_)), col(cK0 + b))
-        at(t, 3.3)
+        at(t, "winners", late)
         scan(v("SB", 0, 288), v("DD", 0, 288), v("B0", 0, 288), mx, mul)
         for j in range(2):
             mine = v("SC", 975 + 16 * j, 1152, 32) if OPT["pick_c"] else v("W", 96 * t + 16 + j, 96 * t + 28, 2)
-            tt(raw(T.W[:, 96 * t + 32 + j:96 * t + 44:2], "W", 96 * t + 32, 96 * t + 44, j, 6), v("SB", 15 + 32 * j, 288, 48), mine, mx)
-        ts(wu(CO_), w(2), -LIFT, add)
+            o = 144 * t + CO_
+            tt(raw(T.WU[:, o + j:o + 12:2], "WU", o, o + 12, j, 6), v("SB", 15 + 32 * j, 288, 48), mine, mx)
         for c in range(5, -1, -1):
-            at(t, 5.1 - 0.22 * c)
-            tt(ind(v("A", 0, AW), wu(CO_ + 2 * c, 2)), v("GM", 32 * c, 32 * c + 32), v("VR", 192 * b + 32 * c, 192 * b + 32 * c + 32), add)
-        at(t, 3.4)
+            at(t, "claim", late - 0.33 * c)
+            tt(ind(v("A", -PAD, AW), wu(CO_ + 2 * c, 2)), v("GM", 32 * c, 32 * c + 32), v("VR", 192 * b + 32 * c, 192 * b + 32 * c + 32), add)
+        at(t, "other rows", -late)
         scan(v("SC", 384, 576), v("RS", 0, 192), key, mn)
         scan(v("SC", 192, 384), v("CM", 0, 192), key, mx)
         tt(wi(kM), cl(C2), v("SC", 207, 384, 16), sub)
@@ -685,28 +777,27 @@ def rank_program(g, core, T, topo):
         mm([(v("P4", 16, 40), iw, ch(CC, 24)), (ths, i1, ch(CN)), (thj, i1, wb(cFb)), (ths, iw, wb(sN)), (thj, nw, wb(sN))])
         tt(wi(kS, 2), v("SC", 399, 768, 16), v("P4", 16, 40), mn)
         ts(wi(cM, 3), wi(kM, 3), 255, band)
-        ts(wu(JM, 24), wi(cM, 2), 16.0, mul, col(cN), add)
+        ts(wu(JM, 36), wi(cM, 3), 16.0, mul, col(cN), add)
         act(v("LS", 0, 192), ind(blk, wu(JS)))
         h = v("P4", 48, 60)
-        mm([(h, i1, ch(HA))] + diag(h, "LH", "LS", 0, 192))
-        at(t, 4.15)
-        tt(w(3), h, wi(cS), add)
-        ts(wu(VU), w(3), 16.0, mul, -45888.0, add)
-        at(t, 5.2)
-        tt(wi(cU), wi(cS), wi(cJ), mn)
-        ts(wu(PU), wi(cU), 16.0, mul, col(cN), add)
-        at(t, 4.7)
+        mm([(h, i1, ch(HA)), (h, i1, ch(HN)), (h, ig, ch(HC))], True, False)
+        mm(diag(h, "LH", "LS", 0, 192), False, True)
+        at(t, "hint")
+        tt(wu(VU), h, wu(JS), add)
+        at(t, "row")
+        tt(wu(PU), wu(JS), wu(JJ), mn)
+        at(t, "farthest", -late)
         eo, em = (v("EO", 192 * t, 192 * t + 192), v("EM", 192 * t, 192 * t + 192)) if t < STEPS - 1 else (v("ZE", 1152, 1344), v("ZI", 1152, 1344))
         act(eo, ind(blk, wu(JM)))
         send(t, 2, em, eo)
-        at(t, 4.6)
+        at(t, "halve")
         act(v("XS", 0, 192), ind(v("X", 0, BS), wu(JS)))
         u = v("P6", 320, 512)
         mm([(u, full("I2"), zf), (u, i1, v("XS", 0, 192))])
-        at(t, 4.8)
+        at(t, "state")
         lin(v("U", 0, 192), u, 0.5 - 2.0 ** -11, ROUND)
         lin(zn, v("U", 0, 192), 1.0, -ROUND)
-        at(t, 6.0)
+        at(t, "spread")
         if t < STEPS - 2:
             spread(t + 2, pool_copy)
         else:

from concourse.mybir import dt, AluOpType as Op, ActivationFunctionType as AF

N, STEPS = 4, 6
BS = 3456
EXT = 2 * BS
B = float(2 ** 21)
BIG = float(2 ** 24)
FAR = float(2 ** 21)
ROUND = 12582912.0
GROW = 96.0 * 256
DROP = 2304.0
LIFT = 256.0
RISE = 73728.0
PAD = 256
WIDE = 4608
AW = 2816
bf, f32, i32, u16 = "bfloat16", "float32", "int32", "uint16"

SCRATCH = {}
for _n, _w, _d in (
        ("M", PAD + WIDE, bf), ("K", PAD + WIDE, f32), ("KB", PAD + WIDE, bf), ("A", PAD + AW, bf), ("AX", EXT + 192, bf), ("X", BS, bf), ("ABX", 3072, bf),
        ("ZE", 1344, bf), ("ZI", 1344, bf), ("EO", 960, f32), ("EM", 960, f32), ("OO", 96, u16), ("OI", 96, u16), ("G", 384, u16),
        ("EI", 384, i32), ("OW", 256, i32), ("OB", 256, bf), ("OH", 512, bf), ("EN", 128, i32), ("SR", 256, bf), ("SK", 256, f32),
        ("TH", 384, i32), ("THF", 384, f32), ("TT", 32, f32), ("XF", 192, bf), ("XG", 192, bf), ("XQ", 288, bf),
        ("PI", 8, i32), ("CO", 48, f32), ("W", 96 * STEPS, f32), ("WI", 112 * STEPS, i32), ("WU", 144 * STEPS, u16), ("WB", 64 * STEPS, bf),
        ("CU", 80, u16), ("CL", 128, f32), ("CH", 112, bf),
        ("LB", 144, bf), ("LD", 144, bf), ("LR", 144, bf), ("LX", 144, bf), ("L0", 144, bf), ("L1", 144, bf), ("LE", 144, bf), ("LP", 144, bf),
        ("LH", 144, bf), ("LT", 144, bf), ("LF", 144, f32), ("BO", 144, bf), ("I1", 128, bf), ("I2", 128, bf), ("IB", 128, bf), ("ID", 128, bf), ("ND", 128, bf),
        ("IG", 128, bf), ("IO", 128, bf), ("IW", 128, bf), ("NW", 128, bf), ("IF", 128, f32), ("NF", 128, f32), ("ON", 128, bf), ("BC", 128, bf),
        ("SI", 192, i32), ("DF", 192, f32), ("XA", 192, bf), ("IC", 128, bf), ("NC", 128, bf), ("LN", 144, bf), ("ONE", 288, bf), ("RS", 192, bf), ("RN", 192, bf), ("CM", 192, bf), ("NV", 384, bf), ("NM", 192, bf),
        ("MK", 288, bf), ("DD", 288, bf), ("VR", 384, bf), ("LW", 784, bf), ("LQ", 192, bf), ("LS", 192, bf), ("SG", 192, bf), ("Q", 192, bf), ("SIG", 208, bf),
        ("DT", 384, f32), ("SC", 1152, f32), ("XS", 192, bf), ("U", 192, f32), ("CB", 288, f32), ("B0", 288, bf), ("SB", 288, bf), ("GM", 192, bf), ("VAL", 192, bf),
        ("EF", 192, f32), ("YE", 384, f32), ("YT", 384, f32), ("YO", 256, f32), ("YK", 128, f32), ("T1", 384, bf), ("T2", 384, bf), ("T3", 384, bf)):
    SCRATCH[_n] = ("sbuf", [128, _w], _d)
SCRATCH["ZR0"] = ("sbuf", [128, 6, 512], bf)
SCRATCH["ZR1"] = ("sbuf", [128, 6, 512], bf)
SCRATCH["Z"] = ("sbuf", [128, 48, 32], bf)
for _k in range(8):
    SCRATCH["P%d" % _k] = ("psum", [128, 512], f32)
SEMAPHORES = ["v", "a", "pe", "p", "sent"] + ["d%d" % _k for _k in range(40)] + ["r%d" % _k for _k in range(18)]
CY, WAKE, FLIGHT = 0.83, 170.0, 2600.0
GATH, SCAT = 1.56, 3.8
OPT = {"pick_e": True, "pick_c": True, "mch": ((0, 4, "a"), (4, 8, "a"), (8, 12, "v")), "ach": ((0, 4, "a"), (4, 8, "a"), (8, 12, "a")),
       "mch0": ((0, 4, "v"), (4, 8, "a"), (8, 12, "v")),
       "ach0": ((0, 4, "a"), (4, 8, "a"), (8, 12, "a")), "val": 0, "iscan": True, "ne": 2, "tries": 18000, "more": 7000, "heat": 400, "seed": 13, "tied": 0.0, "mix": 0.7, "wary": 0.0}
DUE = {"owners": -6.5, "sign": -2.0, "stale": -0.9, "thresholds": -3.0, "idle states": -8.0, "take states": -6.8, "take names": -0.9,
       "distances": -5.9, "sizes": -2.6, "key": -0.2, "nearest": 0.0, "stale key": 2.6, "first stale": 2.5, "fired": 2.6, "name": 1.3,
       "partner": 1.45, "same name": 2.2, "claimed": 2.1, "compare": 3.7, "winners": 4.3, "claim": 7.0, "other rows": 7.05, "hint": 7.08,
       "row": 7.1, "farthest": 7.3, "halve": 7.2, "state": 7.25, "spread": 7.5, "value": 7.1, "list": 13.3, "relist": 17.0}
SLOW = (1.4, 2.0 / GATH, 5.5 / SCAT)
PLAN = {}


def needs(ops):
    seen, deps, after = {}, [], []
    for n, o in enumerate(ops):
        e, d, f = o["e"], set(), set(o["after"])
        for w, accs in ((0, o["r"]), (1, o["w"])):
            for (name, lo, hi, pk) in accs:
                for (l2, h2, p2, w2, m) in seen.get(name, []):
                    e2 = ops[m]["e"]
                    if name[0] == "P" and name[1:].isdigit():
                        if e2 == e == "pe":
                            if not (o["mid"] and ops[m]["mid"]):
                                f.add(m)
                        elif e2 != e or ((w or w2) and lo < h2 and l2 < hi):
                            d.add(m)
                    elif (w or w2) and lo < h2 and l2 < hi and (pk is None or p2 is None or pk == p2):
                        d.add(m)
        for w, accs in ((0, o["r"]), (1, o["w"])):
            for (name, lo, hi, pk) in accs:
                old = seen.get(name, [])
                if w and pk is None and not o["mid"]:
                    old = [x for x in old if not (lo <= x[0] and x[1] <= hi)]
                seen[name] = old + [(lo, hi, pk, w, n)]
        deps.append(d)
        after.append(f)
    return deps, after


def place(ops, pred, prio):
    start, end = [0.0] * len(ops), 0.0
    busy = {q: ([], []) for q in ("v", "a", "pe", "p", "sp", "x")}
    for i in prio:
        q, c, l = ops[i]
        s = 0.0
        for m, d in pred[i]:
            d += start[m]
            if d > s:
                s = d
        if c:
            on, off = busy[q]
            lo = hi = len(on)
            if hi and off[-1] > s:
                lo = 0
                while lo < hi:
                    mid = (lo + hi) >> 1
                    if off[mid] <= s:
                        lo = mid + 1
                    else:
                        hi = mid
                hi = len(on)
                while lo < hi and on[lo] < s + c:
                    s = off[lo]
                    lo += 1
            on.insert(lo, s)
            off.insert(lo, s + c)
        start[i] = s
        if s + c + l > end:
            end = s + c + l
    return start, end


def replay(ops, pred, start):
    begin, free, end = [0.0] * len(ops), {}, 0.0
    for i in sorted(range(len(ops)), key=lambda i: start[i]):
        q, c, l = ops[i]
        s = free.get(q, 0.0) if c else 0.0
        for m, d in pred[i]:
            d += begin[m]
            if d > s:
                s = d
        begin[i] = s
        if c:
            free[q] = s + c
        if s + c + l > end:
            end = s + c + l
    return begin, end


def ranked(succ, due, kind, shift):
    key = [due[i] + shift[kind[i]] for i in range(len(due))]
    for i in range(len(due) - 1, -1, -1):
        k = key[i]
        for j in succ[i]:
            if key[j] <= k:
                k = key[j] - 0.01
        key[i] = k
    return sorted(range(len(due)), key=lambda i: key[i]), key


def blocked(ops, pred, start):
    ends = {(ops[i][0], round(start[i] + ops[i][1])): i for i in range(len(ops)) if ops[i][1]}
    i, pairs = max(range(len(ops)), key=lambda i: start[i] + ops[i][1] + ops[i][2]), []
    while start[i] > 1.0:
        m, ready = max([(m, start[m] + d) for m, d in pred[i]] + [(None, 0.0)], key=lambda x: x[1])
        if ready < start[i] - 0.5:
            m = ends.get((ops[i][0], round(start[i])))
            if m is None or m == i:
                break
            pairs.append((m, i))
        i = m
    return pairs


def order(ops, deps, after):
    n = len(ops)
    pred, succ, behind = [[] for _ in ops], [[] for _ in ops], []
    for i in range(n):
        near = deps[i] | after[i]
        far = 0
        for m in near:
            far |= behind[m]
        behind.append(far | sum(1 << m for m in near))
        for m in near:
            if not far >> m & 1 or ops[m]["l"]:
                pred[i].append((m, ops[m]["c"] + ops[m]["l"] + (WAKE if m in deps[i] else 0.0) + 0.001))
                succ[m].append(i)
    short = [(o["q"], o["c"], o["l"]) for o in ops]
    kinds = sorted(set(o["kind"] for o in ops))
    kind = [kinds.index(o["kind"]) for o in ops]
    alike = [[m for m, y in enumerate(kinds) if y[1:] == x[1:] and (x[0] < 0) == (y[0] < 0)] for x in kinds]
    steady = [m for m, x in enumerate(kinds) if x[0] == 1]
    due = [o["due"] for o in ops]
    shift, seed = [0.0] * len(kinds), OPT["seed"]
    prio, key = ranked(succ, due, kind, shift)
    slow = [(o["q"], o["slow"], o["l"]) for o in ops]
    pred2 = [[(m, d + ops[m]["slow"] - ops[m]["c"]) for m, d in pred[i]] for i in range(n)]
    start, end = place(short, pred, prio)
    best, pairs, mix = (end, start, shift, key), blocked(short, pred, start), 0.0
    for r in range(OPT["tries"] + OPT["more"]):
        heat = OPT["heat"] * (1 - r / OPT["tries"])
        if r >= OPT["tries"]:
            heat = 150.0 * (1 - (r - OPT["tries"]) / OPT["more"])
        if r == OPT["tries"]:
            mix = OPT["mix"]
            fast, start, shift, key = best
            end = fast * (1 - mix) + mix * replay(slow, pred2, start)[1] / 1.5
            best = (end, start, shift, key)
        trial = list(shift)
        seed = (seed * 1103515245 + 12345) % 2 ** 31
        moves = {}
        if r % 3 and pairs:
            x, y = pairs[(seed >> 8) % len(pairs)]
            more = 20.0 + (seed >> 4) % 200
            if seed >> 20 & 1:
                todo = [x]
                while todo:
                    m = todo.pop()
                    if kind[m] not in moves and due[m] + shift[kind[m]] < key[y] + more:
                        moves[kind[m]] = key[y] + more - due[m] - shift[kind[m]]
                        todo += succ[m]
            else:
                moves[kind[y]] = min(key[x] - more - due[y] - shift[kind[y]], 0.0)
        else:
            x = steady[(seed >> 8) % len(steady)] if seed >> 24 & 1 else (seed >> 8) % len(kinds)
            moves[x] = ((seed >> 3) % 31 - 15) * (20.0, 60.0, 200.0)[(seed >> 20) % 3]
        for x, by in moves.items():
            for m in alike[x] if r < OPT["tries"] * OPT["tied"] else [x]:
                trial[m] += by
        prio, k2 = ranked(succ, due, kind, trial)
        s2, e2 = place(short, pred, prio)
        e1 = e2
        if mix:
            if e1 > fast + 1200.0:
                continue
            s3, e3 = replay(slow, pred2, s2)
            e2 = e1 * (1 - mix) + mix * e3 / 1.5
        if e2 <= end + heat:
            shift, start, end, key, fast = trial, s2, e2, k2, e1
            pairs = blocked(short, pred, start) + (blocked(slow, pred2, s3) if mix else [])
            if end < best[0]:
                best = (end, start, shift, key)
    PLAN["end"] = best[0]
    PLAN["dbg"] = (ops, pred, best[1], short)
    return sorted(range(n), key=lambda i: best[1][i])


def schedule(g, T, ops):
    queue = {"v": g.vector, "a": g.scalar, "pe": g.tensor, "p": g, "sp": g.sync}
    if "seq" not in PLAN:
        PLAN["deps"], after = needs(ops)
        PLAN["seq"] = order(ops, PLAN["deps"], after)
    seq, deps = PLAN["seq"], PLAN["deps"]
    at = {m: n for n, m in enumerate(seq)}
    known, clock, waits, marked = {e: {} for e in queue}, {}, {}, set()
    for i in seq:
        o = ops[i]
        mine, ws = known[o["e"]], []
        for m in sorted(deps[i], key=lambda m: -at[m]):
            key = ops[m]["e"] if ops[m]["k"] == "c" else ("x", m)
            if ops[m]["k"] == "s" or mine.get(key, -1) >= at[m]:
                continue
            ws.append(m)
            marked.add(m)
            for k2, v2 in clock[m].items():
                if mine.get(k2, -1) < v2:
                    mine[k2] = v2
        waits[i] = ws
        clock[i] = {} if o["k"] == "x" else dict(mine)
        clock[i][o["e"] if o["k"] == "c" else ("x", i)] = at[i]
    count, val, nd, sent = {e: 0 for e in queue}, {}, 0, 0
    for i in seq:
        o = ops[i]
        e = o["e"]
        for m in waits[i]:
            queue[e].wait_ge(val[m][0], val[m][1])
        if o["k"] == "c":
            ins = o["f"]()
            if i in marked:
                count[e] += 1
                val[i] = (T.sem[e], count[e])
                ins.then_inc(T.sem[e], 1)
        elif o["k"] == "d":
            val[i] = (T.sem["d%d" % nd], 16)
            nd += 1
            o["f"]().then_inc(val[i][0], 16)
        elif o["k"] == "x":
            val[i] = o["f"]
        else:
            sent += o["f"]()
    for i in seq:
        if ops[i]["k"] in "dx" and i not in marked:
            g.sync.wait_ge(val[i][0], val[i][1])
    g.wait_ge(T.sem["sent"], sent)


def rank_program(g, core, T, topo):
    rank = T.rank_of(core)
    if rank is None:
        return
    ops, sends, step, now = [], {}, [-1, {}], [0.0]
    V, S, PE = g.vector, g.scalar, g.tensor

    def at(t, x, by=0.0):
        now[0] = 13000.0 + 14000.0 * t + 1000.0 * (DUE[x] + by if x in DUE else x)

    def v(name, lo, hi, st=1):
        if name in ("A", "M", "K", "KB"):
            lo, hi = lo + PAD, hi + PAD
        return (T[name][:, lo:hi:st] if st > 1 else T[name][:, lo:hi], [(name, lo, hi, None)], [], (hi - lo + st - 1) // st, False)

    def raw(ap, name, lo=0, hi=10 ** 6, pk=None, n=0):
        return (ap, [(name, lo, hi, pk)], [], n, False)

    def ind(win, off):
        return (win[0].indirect(off[0]), win[1], off[1], 16 * off[3], True)

    def op(e, f, outs, ins, c, k="c", lat=0.0, after=(), mid=False):
        r, w = [], []
        for x in ins:
            if isinstance(x, tuple):
                r += x[1] + x[2]
        for x in outs:
            w += x[1]
            r += x[2]
        key = (step[0] if step[0] in (-1, 0, STEPS - 1) else 1, e, k, w[0][0] if w else r[0][0])
        step[1][key] = step[1].get(key, 0) + 1
        now[0] += 10.0
        rate = SLOW[2] if outs and outs[0][4] else SLOW[1] if any(isinstance(x, tuple) and x[4] for x in ins) else 1.0
        slow = SLOW[0] * (55 + (c - 55) * rate) if k == "c" else c
        if step[0] < 0:
            c = c + OPT["wary"] * (slow - c)
        ops.append({"slow": slow, "mid": mid, "due": now[0], "kind": key + (step[1][key],), "e": e, "q": "x" if k == "x" else e, "f": f, "r": r, "w": w, "k": k, "c": c, "l": lat, "after": after})

    def cost(o, x, f=1.0):
        n = max(o[3], x[3])
        if o[4]:
            return 50 + SCAT * CY * n
        if x[4]:
            return 55 + GATH * CY * n
        if f == 1.0 and all(SCRATCH[y[1][0][0]][2] in (bf, u16) for y in (o, x)):
            f = 0.5
        return 30 + CY * max(64, f * n)

    def a_(x):
        return x[0] if isinstance(x, tuple) else x

    def tt(o, x, y, f):
        two = 1.01 if "psum" in (SCRATCH[x[1][0][0]][0], SCRATCH[y[1][0][0]][0]) else 2.0
        op("v", lambda: V.tensor_tensor(o[0], x[0], y[0], f), [o], [x, y], cost(o, x, two))

    def ts(o, x, s1, f1, s2=None, f2=None):
        if f2 is None:
            op("v", lambda: V.tensor_scalar(o[0], x[0], a_(s1), None, f1), [o], [x, s1], cost(o, x))
        else:
            op("v", lambda: V.tensor_scalar(o[0], x[0], a_(s1), a_(s2), f1, f2), [o], [x, s1, s2], cost(o, x))

    def cp(o, x):
        op("v", lambda: V.tensor_copy(o[0], x[0]), [o], [x], cost(o, x))

    def ms(o, c):
        op("v", lambda: V.memset(o[0], c), [o], [], cost(o, o))

    def scan(o, d0, d1, f, f0=Op.add):
        fast = all(SCRATCH[y[1][0][0]][2] == bf for y in (o, d0, d1))
        op("v", lambda: V.tensor_tensor_scan(o[0], d0[0], d1[0], 0.0, f0, f), [o], [d0, d1], cost(o, d0, 1.0 if fast else 1.01))

    def act(o, x, f=AF.Copy, bias=0.0, scale=1.0, first=0.0):
        if f in (AF.Copy, AF.Silu):
            op("a", lambda: S.activation(o[0], x[0], f), [o], [x], cost(o, x, 1.01) + first)
        else:
            op("a", lambda: S.activation(o[0], x[0], f, bias=a_(bias), scale=a_(scale)), [o], [x, bias, scale], cost(o, x, 1.01))

    def lin(o, x, scale, bias=0.0):
        act(o, x, AF.Identity, bias, scale)

    def io(o, pattern, base, cm=0):
        if SCRATCH[o[1][0][0]][2] == i32:
            op("p", lambda: g.iota(o[0], pattern, base, cm), [o], [], 130 + 2 * CY * o[3])
        else:
            op("p", lambda: g.iota(o[0], pattern, base, cm, allow_small_or_imprecise_dtypes=True), [o], [], 130 + 2 * CY * o[3])

    def sel(o, x, pattern, f, fill, cm=0, base=0):
        op("p", lambda: g.affine_select(o[0], x[0], pattern, f, fill, base, cm), [o], [x], 170 + 2 * CY * o[3])

    def mm(items, start=True, stop=True, each=False):
        def f():
            for n, (o, l, r) in enumerate(items):
                ins = PE.matmul(o[0], l[0], r[0], each or (start and n == 0), each or (stop and n == len(items) - 1))
            return ins
        c = sum(0.42 * max(min(64, l[3]), r[3]) * (4 if SCRATCH[l[1][0][0]][2] == f32 else 1) for o, l, r in items)
        op("pe", f, [x[0] for x in items], [x[1] for x in items] + [x[2] for x in items], c, mid=not (start or stop))

    def diag(o, L, name, lo, hi):
        return [(o, v(L, 15 - q, 143 - q), v(name, lo + q, hi, 16)) for q in range(16)]

    def dma(e, o, x, kb=32):
        q = {"sp": g.sync, "a": g.scalar}[e]
        op(e, lambda: q.dma_start(o[0], x[0]), [o], [x], 50.0, "d", 2000.0 + 5 * kb)

    def send(t, j, dst, src):
        to = T.cores[(rank + 1 + t % (N - 1)) % N]
        rid, pid = topo.addr(to, core)

        def f():
            g.remote_dma(dst[0], src[0], T.sem["r%d" % (3 * t + j)], T.sem["sent"], pid, rid, topo.mask(core, to))
            return len(topo.engines(core, to))
        first = not sends
        sends[t, j] = len(ops)
        op("p", f, [], [src], 2500.0 if first else 500.0, "s")

    def arrive(t, j, dst):
        frm = T.cores[(rank - 1 - t % (N - 1)) % N]
        op("sp", (T.sem["r%d" % (3 * t + j)], len(topo.engines(frm, core))), [dst], [], 0.0, "x", FLIGHT + (0, -100, 600)[j] + 500 * (j != 1), (sends[t, j],))

    def col(j):
        return v("CO", j, j + 1)

    def cl(j, n=12):
        return v("CL", 16 * j, 16 * j + n)

    def ch(j, n=12):
        return v("CH", 12 * j, 12 * j + n)

    def zr(b, lo, hi):
        return raw(T["ZR%d" % b][:, :, lo:hi], "ZR%d" % b, lo, hi, n=6 * (hi - lo))

    def zs(n, lo=0, hi=32):
        return raw(T.Z[:, 6 * n:6 * n + 6, lo:hi], "Z", n, n + 1, n=6 * (hi - lo))

    def spread(n, copy):
        for o in (0, 256):
            copy(zr(n % 2, o, o + 16), zs(n, o // 16, o // 16 + 16))
            for s in (16, 32, 64, 128):
                if n == 1 and s == 128:
                    dma("sp", zr(n % 2, o + s, o + 2 * s), zr(n % 2, o, o + s), 480)
                else:
                    copy(zr(n % 2, o + s, o + 2 * s), zr(n % 2, o, o + s))

    def pool_copy(o, x):
        sel(o, x, [[0, o[3]]], ge, 0.0)

    def rows(name, r):
        return raw(T[name][r::16, PAD:PAD + 2048], name, PAD, PAD + 2048, r)

    def hbm(name):
        return raw(T[name][:], name)

    def full(name, n=128):
        return v(name, 0, n)

    add, sub, mul, mx, mn = Op.add, Op.subtract, Op.mult, Op.max, Op.min
    eq, ne, ge, band = Op.is_equal, Op.not_equal, Op.is_ge, Op.bitwise_and
    x12, x144, x192 = v("XF", 0, 12), v("XF", 0, 144), v("XF", 0, 192)
    xg, xq, one = v("XG", 0, 192), v("XQ", 0, 192), v("ONE", 0, 192)
    i1, ib, i2b, n2b, ig, iw, nw = full("I1"), full("IB"), full("ID"), full("ND"), full("IG"), full("IW"), full("NW")
    (cN, cG, cN14, cNN, c12, cK0, cK1, cW01, _x, cWE, _y, cWH, _z, cW0, cW1, cW2, cW3, cW4, cW5, cW6, cP, cX) = range(22)
    spare = [cX]

    def scaled(j, scale, bias=0.0):
        spare[0] += 1
        lin(col(spare[0]), col(j), scale, bias)
        return col(spare[0])
    IL, VID, C2, CT = range(4)
    WA, HA, CC, CN, CI, HN, HC = 0, 2, 3, 5, 6, 7, 8

    at(0, -13.0)
    dma("sp", v("OW", 0, 256), hbm("own"), 128)
    dma("a", raw(T.Z[:, 0:12], "Z", 0, 2), hbm("st"), 96)
    dma("sp", v("EI", 0, 384), hbm("ends"), 192)
    dma("a", v("M", 0, 2048), hbm("msg"), 512)
    dma("sp", v("EN", 0, 128), hbm("enc"), 64)
    dma("a", raw(T.TH[0:8, :], "TH"), hbm("th"))
    ms(v("A", 0, 2240), 0.0)
    io(v("PI", 0, 1), [[0, 1]], 0, 1)
    io(col(cP), [[0, 1]], 0, 1)
    io(x192, [[1, 192]], 0)
    ts(v("PI", 1, 2), v("PI", 0, 1), 15, band)
    cp(col(cN), v("PI", 1, 2))
    lin(v("SR", 128, 256), v("XF", 0, 128), 1.0, 128.0)
    lin(v("SR", 0, 128), v("XF", 0, 128), 0.0, scaled(cN, 128.0, 128.0))
    dma("sp", rows("A", 2), v("SR", 0, 128))
    dma("sp", rows("A", 3), v("SR", 128, 256))
    ts(v("OB", 0, 256), v("OW", 0, 256), -192.0, add)
    dma("sp", rows("A", 0), raw(T.OB[0:64, :], "OB"))
    dma("sp", rows("A", 1), raw(T.OB[64:128, :], "OB"))
    lin(v("OH", 0, 256), v("OB", 0, 256), 1.0, 3256.5)
    dma("a", rows("A", 4), raw(T.OH[0:64, 0:256], "OH", 0, 256))
    ts(v("OH", 256, 512), v("OB", 0, 256), 0.0, ge)
    dma("sp", rows("A", 5), raw(T.OH[0:64, 256:512], "OH", 256, 512))
    lin(col(c12), col(cN), 12.0)
    ts(v("CU", 0, 12), x12, col(c12), add)
    cp(v("G", 0, 192), ind(v("EI", 0, 384), v("CU", 0, 12)))
    spread(0, cp)
    at(STEPS, 0.0)
    io(xg, [[16, 12], [0, 16]], 0)
    io(xq, [[0, 12], [1, 16]], 0)
    lin(one, x192, 0.0, 1.0)
    ts(i1, v("XF", 0, 128), col(cP), eq)
    lin(col(cNN), col(cN), -1.0)
    lin(col(cG), col(cP), 1.0, col(cNN))
    ts(v("PI", 3, 4), v("PI", 0, 1), 14, band)
    cp(col(cN14), v("PI", 3, 4))
    ts(v("CO", cW01, cW01 + 6), v("XF", 0, 6), col(cN14), eq)
    ts(v("CO", cW0, cW0 + 7), v("XF", 0, 7), col(cN), eq)
    ts(v("LB", 0, 144), x144, -15.0, add, col(cG), eq)
    for name, c in (("L0", col(cW0)), ("L1", col(cW1)), ("LD", 256.0), ("LR", 512.0), ("LX", -256.0), ("LE", col(cWE)), ("LP", col(cW01))):
        lin(v(name, 0, 144), v("LB", 0, 144), c)
    for name, c in (("ID", 2 * B), ("IB", B), ("ND", -2 * B), ("IF", 1.0)):
        lin(full(name), i1, c)
    for name, c in (("IG", GROW / 2), ("IW", 0.75 * B), ("NW", -0.75 * B), ("I2", 2.0), ("IO", DROP + LIFT if OPT["ne"] else DROP / 2)):
        ts(full(name), i1, c, mul)
    if OPT["ne"]:
        ts(v("LN", 0, 144), v("LE", 0, 144), -4096.0, mul)
        lin(ch(CI), x12, 16.0, col(cN))
    else:
        lin(full("NF"), i1, -1.0)
    lin(v("NV", 0, 192), xg, -1.0, scaled(cN, -1.0, 192.0))
    lin(v("NV", 192, 384), xg, -1.0, col(cNN))
    io(v("X", 3264, BS), [[0, 192]], 0)
    sel(v("RN", 0, 192), v("X", 3264, BS), [[0, 12], [1, 16]], ne, -BIG)
    lin(v("RS", 0, 192), v("RN", 0, 192), -1.0)
    lin(v("CM", 0, 192), v("RN", 0, 192), 1.0, 2.0)
    io(cl(CT), [[1, 12]], -64 if OPT["iscan"] else 2 ** 22 - 64)
    if OPT["iscan"]:
        lin(v("XA", 0, 192), xg, 1.0, 1.0)
        lin(v("DF", 0, 192), xg, 0.0)
        lin(full("IC"), i1, RISE)
        lin(full("NC"), i1, -RISE)
    thf = raw(T.THF[0:8, :], "THF", n=384)
    cp(thf, raw(T.TH[0:8, :], "TH", n=384))
    ts(v("LF", 0, 144), x144, scaled(cP, 16.0, 15.0), eq, 256.0, mul)
    mm([(v("P7", 0, 24), raw(T.LF[0:8, 15 - q:143 - q], "LF", n=128), raw(T.THF[0:8, q::16], "THF", n=24)) for q in range(16)])
    tt(v("TT", 0, 12), v("P7", 0, 12), cl(CT), add)
    tt(v("TT", 12, 24), v("P7", 12, 24), cl(CT), add)
    ts(v("T1", 0, 192), xg, 2176.0, add, col(cW2), mul)
    ts(v("T1", 192, 384), xq, 128.0, add, col(cW3), mul)
    mm([(v("P5", 0, 192), i1, v("T1", 192 * j, 192 * j + 192)) for j in range(2)])
    lin(v("T2", 0, 192), xg, scaled(cW6, 16.0), scaled(cW5, 129.0))
    lin(v("T2", 192, 384), xq, col(cW0))
    mm([(v("P5", 192, 384), i1, v("T2", 192 * j, 192 * j + 192)) for j in range(2)])
    act(v("AX", 3072, BS), v("P5", 0, 384))
    dma("sp", v("AX", BS + 3072, 2 * BS), v("AX", 3072, BS), 96)
    act(v("K", 2048, 2240), v("P5", 0, 192))
    at(0, -3.0)
    io(v("K", 0, 2048), [[0, 2048]], 0)
    ts(v("SK", 0, 128), v("EN", 0, 128), 16 * ROUND + 128, add, -16 * ROUND, add)
    tt(v("SK", 128, 256), v("EN", 0, 128), v("SK", 0, 128), sub)
    lin(v("SK", 128, 256), v("SK", 128, 256), 1.0, LIFT)
    dma("sp", rows("K", 2), v("SK", 0, 128))
    dma("sp", rows("K", 3), v("SK", 128, 256))
    at(STEPS, 0.0)
    io(v("LW", 0, 192), [[0, 192]], 4000)
    io(v("LW", 384, 592), [[0, 208]], 4000)
    io(v("CH", 0, 24), [[-384, 2], [-16, 12]], 576)
    io(cl(C2), [[32, 12]], 15 * 2 ** 20 + 30)
    io(ch(HA), [[-256, 12]], 3072)
    lin(ch(HN), x12, 0.0, scaled(cN, -1.0, 192.0))
    io(ch(HC), [[0, 12]], -4)
    io(ch(CN), [[1, 12]], 204)
    io(ch(CC, 24), [[2, 2], [0, 12]], 1)
    io(cl(4, 18), [[2, 6], [0, 3]], 1)
    io(v("CL", 64, 82, 3), [[2, 6]], 0)
    ts(full("ON"), v("XG", 0, 128), col(cG), eq)
    lin(full("BC"), full("ON"), col(cWE))
    lin(cl(VID), x12, 16.0, scaled(cN, 2.0, 192.0))
    if OPT["pick_c"]:
        ts(v("CU", 24, 42), cl(4, 18), 16.0, mul, 15.0, add)
    else:
        cp(v("CU", 24, 42), cl(4, 18))
    ts(v("NM", 0, 192), xq, col(cN), ne, -FAR, mul)
    io(v("MK", 0, 288), [[0, 6], [1, 48]], 0)
    ts(v("SB", 0, 288), v("MK", 0, 288), col(cN), eq, scaled(cN, 16.0, 2304.0 + LIFT), mul)
    ts(v("B0", 0, 288), v("MK", 0, 288), scaled(cN, 1.0, 32.0), eq, scaled(cN, 16.0, 2560.0 + LIFT), mul)
    mm([(v("P6", 0, 288), i1, v("SB", 0, 288)), (v("P6", 0, 288), i1, v("B0", 0, 288))])
    ts(v("DD", 0, 288), v("P6", 0, 288), 1.0, mx)
    for j in range(2):
        lin(v("DD", 16 * j, 288, 48), v("ONE", 0, 6), 0.0)
    ts(v("LH", 0, 144), v("LB", 0, 144), scaled(cW5, 384.0, scaled(cW4, 15.0, scaled(cW0, 1.0, col(cW6)))), mul)
    lin(col(cK1), col(cW1), -1.0, 1.0)
    lin(col(cK0), col(cWH), -1.0, scaled(cW0, -1.0, 1.0))
    lin(v("VR", 192, 384), x192, col(cW1))
    ts(v("T3", 0, 192), x192, -192.0, add, col(cW0), mul)
    ts(v("T3", 192, 384), xg, 3072.0, add, col(cW4), mul)
    mm([(v("P4", 0, 192), i1, v("T3", 192 * j, 192 * j + 192)) for j in range(2)])
    act(v("VR", 0, 192), v("P4", 0, 192))
    ts(v("CU", 12, 24), x12, col(c12), add, 192.0, add)
    cp(v("G", 192, 384), ind(v("EI", 0, 384), v("CU", 12, 24)))
    at(0, 0.5)
    spread(1, pool_copy)
    at(STEPS, 0.0)
    lin(cl(IL), x12, 16.0, col(cN))
    ts(cl(6), cl(IL), -5.5, add, 1.0 / 12, mul)
    cp(v("EI", 0, 12), cl(6))
    lin(cl(7), cl(IL), 16.0)
    ts(cl(6), v("EI", 0, 12), -191.0, mul)
    tt(cl(6), cl(6), cl(7), add)
    cp(v("CU", 48, 60), cl(6))

    def take(t, j, table, src):
        arrive(t, j, src)
        to = ind(v(table, -PAD, WIDE), v("OI", 16 * t, 16 * t + 12))
        if table == "K":
            act(to, src, AF.Silu, first=1300.0 * (t == 0))
            if OPT["ne"]:
                act(v("K", 2048, 2240), v("AX", 3072, 3264))
        else:
            cp(to, src)

    def pick(P, src, out):
        mm([(P, i1, v("NM", 0, 192))], True, False)
        mm([(P, full("BC"), src)], False, True)
        scan(v("SC", out, out + 192), v("RN", 0, 192), P, mx)
        return v("SC", out + 15, out + 192, 16)

    def relist(t):
        b = t % 2
        at(t, "value")
        act(v("VAL", 0, 192), ind(v("AX", 0, EXT + 192), v("WU", 144 * t + 112, 144 * t + 124)))
        at(t, "list")
        cp(ind(v("AX", BS * b, BS * b + BS), v("WU", 144 * t + 128, 144 * t + 140)), v("VAL", 0, 192))
        items = diag(v("P7", 0, 192), "LE", "AX", BS * b, BS * b + 3072)
        at(t, "relist")
        for c in range(4):
            mm(items[4 * c:4 * c + 4], c == 0, c == 3)
        if t < STEPS - 2:
            ts(v("G", 192 * b, 192 * b + 192), v("P7", 0, 192), -LIFT, add)
        else:
            lin(v("EF", 0, 192), v("P7", 0, 192), 1.0, -LIFT)
            act(v("YE", 192 * b, 192 * b + 192), ind(v("EF", 0, 192), v("CU", 48, 60)))
            dma("sp", raw(T.ye[:, 192 * b:192 * b + 192], "ye", b, b + 1), v("YE", 192 * b, 192 * b + 192), 96)

    idle = []
    for t in range(STEPS):
        b = t % 2
        step[0], step[1] = t, {}

        def w(j, n=12):
            return v("W", 96 * t + 16 * j, 96 * t + 16 * j + n)

        def wi(j, n=1):
            return v("WI", 112 * t + 12 * j, 112 * t + 12 * (j + n))

        def wu(j, n=12):
            return v("WU", 144 * t + j, 144 * t + j + n)

        def wb(j):
            return v("WB", 64 * t + 16 * j, 64 * t + 16 * j + 12)
        kF, cF, kM, kS, kJ, cM, cS, cJ, cU = range(9)
        JF, JM, JS, JJ, WX, EFU, CU_, CO_, VU, PU = 0, 12, 24, 36, 48, 64, 80, 96, 112, 128
        sN, cFb, GE, TD = range(4)
        blk = v("AX", BS * b, BS * b + BS)
        z, zn = zs(t), zs(t + 2)
        pieces = OPT["ach"] if t else OPT["ach0"]
        late = len(pieces) if t == 1 else OPT["val"]
        for n, (lo, hi, e) in enumerate(pieces):
            if t and n == late:
                relist(t - 1)
            at(t, "owners", 0.35 * lo)
            (cp if e == "v" else act)(v("AX", BS * b + 256 * lo, BS * b + 256 * hi), ind(v("A", 0, 2240), v("G", 192 * b + 16 * lo, 192 * b + 16 * hi)))
            for P, L in (("P1", "L0"), ("P2", "L1")):
                first = [(v(P, 0, 192), i1, v("NV", 192 * b, 192 * b + 192))] if lo == 0 else []
                mm(first + diag(v(P, 16 * lo, 16 * hi), L, "AX", BS * b + 256 * lo, BS * b + 256 * hi), lo == 0, hi == 12)
        if t and late == len(pieces):
            relist(t - 1)
        at(t, "sign")
        act(v("SG", 0, 192), v("P1", 0, 192), AF.Sign)
        at(t, "stale")
        tt(v("Q", 0, 192), v("SG", 0, 192), v("P2", 0, 192), mul)
        s1 = v("SIG", 0, 192)
        ts(s1, v("Q", 0, 192), 0.0, ne)
        at(t, "thresholds")
        thr = v("P4", 0, 12)
        mm([(thr, full("IF"), v("TT", 12 * b, 12 * b + 12))] + [(thr, ig, x) for s in idle[b::2] for x in (s, v("ONE", 0, 12))]
           + [(thr, full("IC"), v("XA", 0, 192, 16))] * OPT["iscan"])
        if OPT["iscan"]:
            act(v("DF", 0, 192, 16), thr)
        at(t, "idle states")
        pool_copy(v("X", 3072, 3264), z)
        if t:
            at(t, "take states")
            arrive(t - 1, 1, v("OI", 16 * t - 16, 16 * t - 4))
            take(t - 1, 0, "M", v("ZI", 192 * t - 192, 192 * t))
            at(t, "take names")
            take(t - 1, 2, "K", v("EM", 192 * t - 192, 192 * t))
        key = v("P0", 0, 192)
        mm([(key, i1, x192), (key, full("IC"), v("XA", 0, 192)) if OPT["iscan"] else (key, i2b, one)], True, False)
        for lo, hi, e in OPT["mch" if t else "mch0"]:
            x, ab, o = v("X", 256 * lo, 256 * hi), v("ABX", 256 * lo, 256 * hi), v("P0", 16 * lo, 16 * hi)
            at(t, "distances", 0.35 * lo)
            for c in range(lo // 2, hi // 2):
                tt(v("X", 512 * c, 512 * c + 512), ind(v("M", 0, 2048), v("G", 192 * b + 32 * c, 192 * b + 32 * c + 32)), raw(T["ZR%d" % b][:, c], "ZR%d" % b, 0, 512, n=512), sub)
            at(t, "sizes", 0.22 * lo)
            if e == "a":
                act(ab, x, AF.Abs)
                mm(diag(o, "LD", "ABX", 256 * lo, 256 * hi), False, False)
            else:
                mm(diag(o, "LX", "X", 256 * lo, 256 * hi), False, False)
                ts(ab, x, 0.0, mx)
                mm(diag(o, "LR", "ABX", 256 * lo, 256 * hi), False, False)
        at(t, "key")
        mm([(key, ib, s1)], False, True)
        at(t, "nearest")
        if OPT["iscan"]:
            scan(v("SI", 0, 192), v("DF", 0, 192), key, mn, mx)
            ts(wi(cF), v("SI", 15, 192, 16), 255, band)
        else:
            scan(v("SC", 0, 192), v("RS", 0, 192), key, mn)
            tt(wi(kF), v("SC", 15, 192, 16), thr, mn)
            ts(wi(cF), wi(kF), 255, band)
        ts(wu(JF), wi(cF), 16.0, mul, col(cN), add)
        act(v("LW", 192, 384), ind(blk, wu(JF)))
        at(t, "stale key")
        act(v("DT", 0, 192), key)
        key = v("P0", 192, 384)
        if OPT["iscan"]:
            mm([(key, full("IF"), v("DT", 0, 192)), (key, full("NC"), v("XA", 0, 192)), (key, i2b, one), (key, n2b, s1)])
        else:
            mm([(key, n2b, s1), (key, full("IF"), v("DT", 0, 192))])
        row = v("P3", 192, 384)
        mm([(row, i1, x192), (row, i2b, one), (row, i2b, one)], True, False)
        mm([(row, n2b, s1)], False, True)
        at(t, "first stale")
        scan(v("SC", 576, 768), v("RS", 0, 192), row, mn)
        at(t, "fired")
        cp(wb(cFb), wi(cF))
        act(wb(sN), wb(cFb), AF.Sign, -191.5)
        idle.append(wb(sN))
        zf = v("ZE", 192 * t, 192 * t + 192)
        act(zf, ind(v("X", 0, BS), wu(JF)), AF.Abs)
        send(t, 0, v("ZI", 192 * t, 192 * t + 192), zf)
        at(t, "name")
        par, test = v("P5", 0, 12), v("P2", 0, 12)
        if OPT["pick_e"]:
            el = pick(v("P1", 0, 192), v("LW", 192, 384), 768)
            ts(wu(EFU), el, -LIFT, add)
        else:
            mm(diag(v("P1", 0, 12), "LE", "LW", 192, 384))
            ts(wu(EFU), v("P1", 0, 12), -LIFT, add)
            el = w(0)
            act(el, v("P1", 0, 12))
        ext = v("AX", EXT, EXT + 192)
        act(ext, ind(v("K", 0, 2240), wu(EFU)))
        at(t, "partner")
        mm([(par, i1, ch(WA + b))], True, False)
        mm(diag(par, "LP", "LW", 192, 384), False, True)
        at(t, "same name")
        ts(wu(WX), par, col(cNN), add)
        tt(wb(GE), par, cl(VID), ge)
        if OPT["ne"]:
            (act if OPT["ne"] == 1 else pool_copy)(v("LW", 592, 784), v("LW", 192, 384))
            tt(v("LQ", 0, 192), ind(v("LW", 0, 592), wu(WX)), v("LW", 592, 784), ne)
            mm([(test, i1, ch(CI)), (test, full("IO"), v("ONE", 0, 12))], True, False)
            mm([(test, nw, wb(GE))], False, False)
            mm(diag(test, "LN", "LQ", 0, 192), False, True)
            tt(v("OO", 16 * t, 16 * t + 12), test, el, mx)
        else:
            oo = v("P5", 16, 28)
            act(v("LQ", 0, 192), ind(v("LW", 0, 592), wu(WX)))
            mm([(test, full("NF"), el), (test, ib, wb(GE))], True, False)
            mm(diag(test, "LE", "LQ", 0, 192), False, True)
            mm([(oo, full("IF"), el), (oo, full("IO"), wb(sN))], True, False)
            ts(wb(TD), test, 0.0, eq, DROP, mul)
            mm([(oo, i1, wb(TD))], False, True)
            ts(v("OO", 16 * t, 16 * t + 12), oo, DROP / 2, add)
        send(t, 1, v("OI", 16 * t, 16 * t + 12), v("OO", 16 * t, 16 * t + 12))
        late = 5.0 * (t == STEPS - 1)
        at(t, "claimed", late)
        if OPT["pick_c"]:
            cl_ = pick(v("P3", 0, 192), ext, 960)
            win = v("SC", 960, 1152)
        mm([(v("P6", 48 * c + lo, 48 * c + lo + n), full("BC"), v("AX", EXT + 32 * c, EXT + 32 * c + n)) for c in range(6) for lo, n in ((0, 16), (16, 32))], each=True)
        act(v("CB", 0, 288), v("P6", 0, 288))
        if not OPT["pick_c"]:
            mm(diag(v("P3", 0, 12), "LE", "AX", EXT, EXT + 192))
            cl_ = win = w(1)
            act(cl_, v("P3", 0, 12))
        at(t, "compare", late)
        tt(v("B0", 0, 288), ind(win, v("CU", 24, 42)), v("CB", 0, 288), eq)
        ts(wu(CU_), cl_, -LIFT, add)
        lin(v("GM", 0, 192), ind(v("A", 0, 2240), wu(CU_)), col(cK0 + b))
        at(t, "winners", late)
        scan(v("SB", 0, 288), v("DD", 0, 288), v("B0", 0, 288), mx, mul)
        for j in range(2):
            mine = v("SC", 975 + 16 * j, 1152, 32) if OPT["pick_c"] else v("W", 96 * t + 16 + j, 96 * t + 28, 2)
            o = 144 * t + CO_
            tt(raw(T.WU[:, o + j:o + 12:2], "WU", o, o + 12, j, 6), v("SB", 15 + 32 * j, 288, 48), mine, mx)
        for c in range(5, -1, -1):
            at(t, "claim", late - 0.33 * c)
            tt(ind(v("A", -PAD, AW), wu(CO_ + 2 * c, 2)), v("GM", 32 * c, 32 * c + 32), v("VR", 192 * b + 32 * c, 192 * b + 32 * c + 32), add)
        at(t, "other rows", -late)
        scan(v("SC", 384, 576), v("RS", 0, 192), key, mn)
        scan(v("SC", 192, 384), v("CM", 0, 192), key, mx)
        tt(wi(kM), cl(C2), v("SC", 207, 384, 16), sub)
        ths, thj = v("P4", 16, 28), v("P4", 28, 40)
        mm([(v("P4", 16, 40), iw, ch(CC, 24)), (ths, i1, ch(CN)), (thj, i1, wb(cFb)), (ths, iw, wb(sN)), (thj, nw, wb(sN))])
        tt(wi(kS, 2), v("SC", 399, 768, 16), v("P4", 16, 40), mn)
        ts(wi(cM, 3), wi(kM, 3), 255, band)
        ts(wu(JM, 36), wi(cM, 3), 16.0, mul, col(cN), add)
        act(v("LS", 0, 192), ind(blk, wu(JS)))
        h = v("P4", 48, 60)
        mm([(h, i1, ch(HA)), (h, i1, ch(HN)), (h, ig, ch(HC))], True, False)
        mm(diag(h, "LH", "LS", 0, 192), False, True)
        at(t, "hint")
        tt(wu(VU), h, wu(JS), add)
        at(t, "row")
        tt(wu(PU), wu(JS), wu(JJ), mn)
        at(t, "farthest", -late)
        eo, em = (v("EO", 192 * t, 192 * t + 192), v("EM", 192 * t, 192 * t + 192)) if t < STEPS - 1 else (v("ZE", 1152, 1344), v("ZI", 1152, 1344))
        act(eo, ind(blk, wu(JM)))
        send(t, 2, em, eo)
        at(t, "halve")
        act(v("XS", 0, 192), ind(v("X", 0, BS), wu(JS)))
        u = v("P6", 320, 512)
        mm([(u, full("I2"), zf), (u, i1, v("XS", 0, 192))])
        at(t, "state")
        lin(v("U", 0, 192), u, 0.5 - 2.0 ** -11, ROUND)
        lin(zn, v("U", 0, 192), 1.0, -ROUND)
        at(t, "spread")
        if t < STEPS - 2:
            spread(t + 2, pool_copy)
        else:
            dma("sp", raw(T.yz[:, 192 * b:192 * b + 192], "yz", b, b + 1), zn, 48)
    relist(STEPS - 1)
    t = STEPS - 1
    at(t, 4.0)
    arrive(t, 1, v("OI", 16 * t, 16 * t + 12))
    take(t, 0, "M", v("ZI", 192 * t, 192 * t + 192))
    dma("sp", hbm("ym"), v("M", 0, 2048), 512)
    at(t, 6.0)
    for c in range(2):
        act(v("KB", 1024 * c, 1024 * c + 1024), v("K", 1024 * c, 1024 * c + 1024))
    take(t, 2, "KB", v("ZI", 1152, 1344))
    mm([(v("P2", 0, 128), v("LE", 15 - c, 143 - c), v("KB", 128 * c, 128 * c + 128)) for c in range(16)])
    lin(v("YK", 0, 128), v("P2", 0, 128), 1.0, -LIFT)
    dma("a", hbm("yk"), v("YK", 0, 128), 64)
    ts(v("BO", 0, 144), x144, scaled(cN, 64.0, scaled(cG, 0.5, 7.0)), eq, col(cW01), mul)
    mm([(v("P1", 0, 256), v("BO", 7 - c, 135 - c), v("A", 256 * c, 256 * c + 256)) for c in range(8)])
    lin(v("YO", 0, 256), v("P1", 0, 256), 1.0, 192.0)
    dma("a", hbm("yo"), v("YO", 0, 256), 128)
    ts(v("LT", 0, 144), x144, col(cP), eq, 48.0, mul)
    yt = raw(T.P3[0:8, 0:384], "P3", 0, 384, n=384)
    mm([(yt, raw(T.IF[0:8, 0:8], "IF", n=8), thf)] +
       [(raw(T.P3[0:8, 192 * (t % 2) + q:192 * (t % 2) + 192:16], "P3", 0, 384, n=12), v("LT", q, 128, 16), idle[t]) for t in range(STEPS) for q in range(16)])
    lin(raw(T.YT[0:8, :], "YT", n=384), yt, 1.0, 144.0)
    dma("sp", hbm("yt"), raw(T.YT[0:8, :], "YT"))
    schedule(g, T, ops)
